import numpy as np
import ml_dtypes


def mxq(x, axis, fmt="e4m3"):
    dtype, down = {"e4m3": (ml_dtypes.float8_e4m3fn, 7), "e5m2": (ml_dtypes.float8_e5m2, 14)}[fmt]
    v = np.moveaxis(np.asarray(x, np.float32).astype(ml_dtypes.bfloat16).astype(np.float64), axis, -1)
    blocks = v.reshape(v.shape[:-1] + (-1, 32))
    amax = np.abs(blocks).max(-1, keepdims=True)
    byte = np.maximum(np.where(amax > 0, np.frexp(amax)[1] - 1 + 127, 0) - down, 1)
    scale = np.exp2(byte - 127.0)
    codes = (blocks / scale).astype(np.float32).astype(dtype).astype(np.float64)
    return np.moveaxis((codes * scale).reshape(v.shape), -1, axis)


WIDE = False


def mx_kscale(k):
    if not WIDE:
        return np.ones(k)
    levels = np.array([10, -10, 5, -5, 0])
    if k % 512:
        return np.exp2(np.random.permutation(np.resize(levels, k // 32))).repeat(32)
    a = np.empty((k // 512, 16))
    for p in range(k // 512):
        a[p, :8] = np.random.permutation(np.resize(levels, 8))
        for g in range(8):
            far = levels[np.abs(levels - a[p, g]) >= 10]
            a[p, g + 8] = far[np.random.randint(len(far))]
    return np.exp2(a.ravel()).repeat(32)


def f64(x):
    return np.asarray(x).astype(np.float64)


def striped(idx):
    return np.tile(np.asarray(idx).reshape(-1, 16).T, (8, 1)).astype(np.uint16)


def unstriped(offs):
    return offs[:16].T.reshape(-1).astype(np.int64)


E2M1 = np.array([0.0, 0.5, 1.0, 1.5, 2.0, 3.0, 4.0, 6.0, -0.0, -0.5, -1.0, -1.5, -2.0, -3.0, -4.0, -6.0])


def pack_weight(w, fmt):
    k, n = w.shape
    w = f64(np.asarray(w, np.float32).astype(ml_dtypes.bfloat16)).reshape(k // 32, 32, n)
    amax = np.abs(w).max(1)
    if fmt == "e4m3":
        byte = np.frexp(amax)[1] - 1 + 127 - 7
    else:
        mant, ex = np.frexp(amax / 6.0)
        byte = np.where(mant > 0.5, ex, ex - 1) + 127
    byte = np.clip(np.where(amax > 0, byte, 1), 1, 254)
    scaled = (w * np.exp2(127.0 - byte)[:, None, :]).reshape(k, n).astype(np.float32)
    by_word = np.ascontiguousarray(scaled.reshape(k // 512, 128, 4, n).transpose(0, 1, 3, 2))
    if fmt == "e4m3":
        words = by_word.astype(ml_dtypes.float8_e4m3fn).view(np.uint8)
    else:
        c = by_word.astype(ml_dtypes.float4_e2m1fn).view(np.uint8) & 0xF
        words = (c[..., 0::2] | (c[..., 1::2] << 4)).reshape(k // 512, 128, 2 * n)
    return np.ascontiguousarray(words), np.ascontiguousarray(byte.astype(np.uint8).reshape(k // 512, 16, n))


def unpack_weight(words, scales, fmt):
    g, _, n = scales.shape
    words = np.ascontiguousarray(words).reshape(g, 128, n, -1)
    if fmt == "e4m3":
        vals = words.view(ml_dtypes.float8_e4m3fn).astype(np.float64)
    else:
        nib = np.empty((g, 128, n, 4), np.uint8)
        nib[..., 0::2] = words & 0xF
        nib[..., 1::2] = words >> 4
        vals = E2M1[nib]
    vals = vals * np.repeat(np.exp2(scales.astype(np.float64) - 127.0), 8, axis=1)[..., None]
    return vals.transpose(0, 1, 3, 2).reshape(g * 512, n)


B, N, T, D, DV, NQ = 2, 512, 2048, 1024, 256, 128


def setup_inputs():
    n = np.random.standard_normal
    seg = T // B
    idx = np.concatenate([b * seg + np.random.permutation(seg)[:N] for b in range(B)])
    s = mx_kscale(D)[:, None]
    u = np.ones(T)
    u[idx] = mx_kscale(B * N)
    r = np.random.uniform(0.5, 2.0, T)
    k = n((D, T)) / s
    v = n((DV, T)) / (u * r)
    kp = pack_weight(k, "e2m1")
    return {
        "qT": (n((B, D, NQ)) * s * (1.00 / np.sqrt(D))).astype(np.float32),
        "k_words": np.ascontiguousarray(kp[0].reshape(D // 1024, 2, 128, T, 2).transpose(0, 2, 3, 1, 4)).reshape(D // 1024, 128, T, 4),
        "k_scales": kp[1],
        "vT": v.astype(np.float32),
        "vs": np.tile(u * r, (128, 1)).astype(np.float32),
        "sink": (2.0 + 3.0 * n((B, NQ, 1))).astype(np.float32),
        "offs": striped(idx),
    }


def reference(qT, k_words, k_scales, vT, vs, sink, offs):
    idx = unstriped(offs)
    k = unpack_weight(k_words.reshape(D // 1024, 128, T, 2, 2).transpose(0, 3, 1, 2, 4).reshape(D // 512, 128, 2 * T), k_scales, "e2m1")
    v = f64(vT)
    pick = lambda x: x[:, idx].reshape(x.shape[0], B, N).transpose(1, 0, 2)
    q = f64(qT)
    score = mxq(q, 1, "e4m3").transpose(0, 2, 1) @ pick(k)
    m = np.maximum(score.max(-1, keepdims=True), f64(sink))
    p = np.exp(score - m)
    total = p.sum(-1, keepdims=True) + np.exp(f64(sink) - m)
    w = p * pick(f64(vs))[:, :1, :]
    y = mxq(w, 2, "e4m3") @ mxq(pick(v).transpose(0, 2, 1), 1, "e4m3")
    y = y / total
    return y

@@ -1,0 +1,273 @@
+from contextlib import ExitStack
+
+import concourse.mybir as mybir
+from concourse.masks import make_identity
+
+B, N, T, D, DV, NQ = 2, 512, 2048, 1024, 256, 128
+FLOPS = 2 * B * NQ * N * (D + DV)
+
+F32 = mybir.dt.float32
+BF16 = mybir.dt.bfloat16
+I32 = mybir.dt.int32
+U32 = mybir.dt.uint32
+U16 = mybir.dt.uint16
+U8 = mybir.dt.uint8
+FP8X4 = mybir.dt.float8_e4m3fn_x4
+FP4X4 = mybir.dt.float4_e2m1fn_x4
+ALU = mybir.AluOpType
+ACT = mybir.ActivationFunctionType
+
+P = 128
+SEG = T // B
+PASSES = D // 512
+HALVES = DV // P
+COLS = N // 16
+
+
+def tile_attend_sink_seg_kernel(tc, qT, k_words, k_scales, vT, vs, sink, offs, out):
+    nc = tc.nc
+    with ExitStack() as ctx:
+        keep = ctx.enter_context(tc.tile_pool(name="keep", bufs=1))
+        psum = ctx.enter_context(tc.psum_pool(name="psum", bufs=1))
+
+        def sb(name, shape, dtype):
+            return keep.tile(shape, dtype, name=name, align_bytes=64)
+
+        offsets = keep.tile([P, B * COLS], U16, name="offsets")
+        nc.sync.dma_start(offsets[:], offs)
+
+        def seg(b):
+            return slice(b * SEG, (b + 1) * SEG)
+
+        def listed(window, b):
+            return window[:, 0 : (b + 1) * SEG].indirect(offsets[:, b * COLS : (b + 1) * COLS])
+
+        ks_pool = sb("ks_pool", [P, T // 4], I32)
+        vs_pool = sb("vs_pool", [P, T], F32)
+        kw_pool = sb("kw_pool", [P, T], I32)
+        v_raw = [sb("v_raw%d" % h, [P, T], F32) for h in range(HALVES)]
+        v_bf = [sb("v_bf%d" % h, [P, T], BF16) for h in range(HALVES)]
+        q_raw = [sb("q_raw%d" % b, [P, PASSES, 4 * NQ], F32) for b in range(B)]
+        sinks = sb("sinks", [P, B], F32)
+        ident = sb("ident", [P, P], F32)
+        warm = sb("warm", [P, 2], F32)
+        ks_high = [sb("ks_high%d" % b, [P, N // 4], I32) for b in range(B)]
+
+        nc.vector.memset(ks_pool[:], 0)
+        nc.vector.memset(warm[:, 0:1], 0.0)
+        nc.scalar.activation(warm[:, 1:2], warm[:, 0:1], ACT.Exp)
+        nc.vector.memset(vs_pool[:], 0.0)
+        make_identity(nc, ident[:])
+        for b in range(B):
+            nc.gpsimd.memset(ks_high[b][:], 0)
+
+        kw_hbm = k_words[0].rearrange("p t c -> p (t c)").bitcast(I32)
+        ks_hbm = k_scales.bitcast(I32)
+
+        def load_kw(b):
+            nc.sync.dma_start(kw_pool[:, seg(b)], kw_hbm[:, seg(b)])
+
+        def load_q(b):
+            nc.sync.dma_start(q_raw[b][:], qT[b].rearrange("(o p j) q -> p o (j q)", o=PASSES, j=4))
+
+        def load_v(b, h):
+            nc.sync.dma_start(v_raw[h][:, seg(b)], vT[h * P : (h + 1) * P, seg(b)])
+
+        def load_sinks(rows):
+            with nc.allow_non_contiguous_dma(reason="one sink a partition"):
+                nc.sync.dma_start(sinks[rows, :], sink[:, rows, 0].rearrange("b q -> q b"))
+
+        load_v(0, 0)
+        load_sinks(slice(0, 96))
+        for quad in range(4):
+            nc.sync.dma_start(ks_pool[32 * quad : 32 * quad + 8, :], ks_hbm[:, 4 * quad : 4 * quad + 4, :])
+        nc.gpsimd.dma_start(vs_pool[0:1, :], vs[0:1, :])
+        load_kw(0)
+        load_q(0)
+        load_sinks(slice(96, P))
+        load_v(0, 1)
+        load_kw(1)
+        load_q(1)
+        load_v(1, 0)
+        load_v(1, 1)
+
+        ks_got = [sb("ks_got%d" % b, [P, N], U8) for b in range(B)]
+        kw_got = [sb("kw_got%d" % b, [P, N], U32) for b in range(B)]
+        k_codes = [sb("k_codes%d" % b, [P, PASSES, 2 * N], U8) for b in range(B)]
+        vs_got = [sb("vs_got%d" % b, [P, N], F32) for b in range(B)]
+        vs_col = [sb("vs_col%d" % b, [P, 4], F32) for b in range(B)]
+        q_bf = [sb("q_bf%d" % b, [P, PASSES * NQ * 4], BF16) for b in range(B)]
+        q_codes = [sb("q_codes%d" % b, [P, PASSES * NQ], U32) for b in range(B)]
+        q_scales = [sb("q_scales%d" % b, [P, PASSES * NQ], U8) for b in range(B)]
+        v_got = [[sb("v_got%d%d" % (b, h), [P, N], BF16) for h in range(HALVES)] for b in range(B)]
+        v_in = [[sb("v_in%d%d" % (b, h), [P, 4 * P], BF16) for h in range(HALVES)] for b in range(B)]
+        v_codes = [sb("v_codes%d" % b, [P, DV], U32) for b in range(B)]
+        v_scales = [sb("v_scales%d" % b, [P, DV], U8) for b in range(B)]
+        neg_a = [sb("neg_a%d" % b, [P, N + 1], F32) for b in range(B)]
+        neg_m = [sb("neg_m%d" % b, [P, 1], F32) for b in range(B)]
+        probs = [sb("probs%d" % b, [P, N + 1], F32) for b in range(B)]
+        total = [sb("total%d" % b, [P, 1], F32) for b in range(B)]
+        r_total = [sb("r_total%d" % b, [P, 1], F32) for b in range(B)]
+        w_bf = [sb("w_bf%d" % b, [P, 4 * NQ], BF16) for b in range(B)]
+        w_codes = [sb("w_codes%d" % b, [P, NQ], U32) for b in range(B)]
+        w_scales = [sb("w_scales%d" % b, [P, NQ], U8) for b in range(B)]
+        result = [sb("result%d" % b, [P, DV], F32) for b in range(B)]
+
+        scores = [psum.tile([P, N], F32, name="scores%d" % b) for b in range(B)]
+        turned_v = [psum.tile([P, HALVES, 2, P], F32, name="turned_v%d" % b) for b in range(B)]
+        turned_p = [psum.tile([P, 4, NQ], F32, name="turned_p%d" % b) for b in range(B)]
+
+        def gather_ks(b):
+            nc.vector.tensor_copy(ks_got[b][:], listed(ks_pool[:].bitcast(U8), b))
+            nc.gpsimd.dma_start(ks_high[b][0:100, :], ks_got[b][:].bitcast(I32)[4:104, :])
+
+        def gather_kw(b):
+            nc.vector.tensor_copy(kw_got[b][:], listed(kw_pool[:].bitcast(U32), b))
+
+        def part_kw(b):
+            nc.vector.tensor_copy(
+                k_codes[b][:].bitcast(U16), kw_got[b][:].bitcast(U16).rearrange("p (s o) -> p o s", o=PASSES)
+            )
+
+        def gather_vs(b):
+            nc.vector.tensor_copy(vs_got[b][:], listed(vs_pool[:], b))
+            turned = psum.tile([P, 4, P], F32, name="spare%d" % b, tag="spare%d" % b)
+            for t in range(4):
+                nc.tensor.transpose(turned[:, t, :], vs_got[b][:, t:N:4], ident[:])
+            nc.vector.tensor_copy(vs_col[b][:], turned[:, :, 0])
+
+        def group_q(b):
+            nc.scalar.activation(
+                q_bf[b][:].rearrange("p (o q j) -> p o q j", o=PASSES, j=4),
+                q_raw[b][:].rearrange("p o (j q) -> p o q j", j=4),
+                ACT.Copy,
+            )
+
+        def quant_q(b):
+            nc.vector.quantize_mx(q_codes[b][:].bitcast(FP8X4), q_scales[b][:], q_bf[b][:])
+
+        def paired(b, h):
+            return v_got[b][h][:].rearrange("p (u s j) -> p s u j", u=2, j=2)
+
+        def turn_v(b, h):
+            words = v_got[b][h][:].bitcast(F32)
+            for u in range(2):
+                nc.tensor.transpose(turned_v[b][:, h, u, :], words[:, u * P : (u + 1) * P], ident[:])
+            nc.scalar.copy(
+                v_in[b][h][:].bitcast(F32).rearrange("p (e u) -> p e u", u=2),
+                turned_v[b][:, h].rearrange("p u e -> p e u"),
+            )
+
+        def gather_v_scalar(b, h):
+            nc.scalar.activation(v_bf[h][:, seg(b)], v_raw[h][:, seg(b)], ACT.Copy)
+            nc.scalar.activation(paired(b, h), listed(v_bf[h][:], b), ACT.Copy)
+            turn_v(b, h)
+
+        def gather_v_vector(b, h):
+            nc.vector.tensor_copy(paired(b, h), listed(v_raw[h][:], b))
+            turn_v(b, h)
+
+        def quant_v(b, h):
+            cols = slice(h * P, (h + 1) * P)
+            nc.vector.quantize_mx(v_codes[b][:, cols].bitcast(FP8X4), v_scales[b][:, cols], v_in[b][h][:])
+
+        def score(b):
+            k_planes = [ks_got[b][:], ks_high[b][:].bitcast(U8)]
+            for o in range(PASSES):
+                cols = slice(o * NQ, (o + 1) * NQ)
+                nc.tensor.matmul_mx(
+                    scores[b][:],
+                    lhsT=q_codes[b][:, cols].bitcast(FP8X4),
+                    lhsT_scale=q_scales[b][:, cols],
+                    rhs=k_codes[b][:, o, :].bitcast(FP4X4),
+                    rhs_scale=k_planes[o],
+                    start=(o == 0),
+                    stop=(o == PASSES - 1),
+                )
+
+        def negate_sink(b):
+            nc.gpsimd.tensor_scalar(neg_a[b][:, N : N + 1], sinks[:, b : b + 1], -1.0, 0.0, ALU.mult, ALU.add)
+
+        def row_max(b):
+            nc.vector.tensor_scalar(
+                neg_a[b][:, 0:N].rearrange("p (t s) -> p t s", t=4),
+                scores[b][:].rearrange("p (s t) -> p t s", t=4),
+                -1.0,
+                neg_a[b][:, N : N + 1],
+                ALU.mult,
+                ALU.min,
+                accum_out=neg_m[b][:],
+            )
+
+        def exponentials(b):
+            nc.scalar.activation(
+                probs[b][:], neg_a[b][:], ACT.Exp, bias=neg_m[b][:], scale=-1.0, accum_out=total[b][:]
+            )
+            for t in range(4):
+                nc.tensor.transpose(turned_p[b][:, t, :], probs[b][:, t * P : (t + 1) * P], ident[:])
+
+        def weigh(b):
+            nc.vector.tensor_tensor(
+                w_bf[b][:].rearrange("p (q t) -> p q t", t=4),
+                turned_p[b][:].rearrange("p t q -> p q t"),
+                vs_col[b][:].unsqueeze(1).to_broadcast([P, NQ, 4]),
+                ALU.mult,
+            )
+
+        def quant_w(b):
+            nc.vector.quantize_mx(w_codes[b][:].bitcast(FP8X4), w_scales[b][:], w_bf[b][:])
+
+        def finish(b):
+            sums = psum.tile([P, 4, P], F32, name="sums%d" % b, tag="spare%d" % b)
+            y = sums[:].rearrange("p a c -> p (a c)")[:, 0:DV]
+            nc.tensor.matmul_mx(
+                y,
+                lhsT=w_codes[b][:].bitcast(FP8X4),
+                lhsT_scale=w_scales[b][:],
+                rhs=v_codes[b][:].bitcast(FP8X4),
+                rhs_scale=v_scales[b][:],
+                start=True,
+                stop=True,
+            )
+            nc.scalar.activation(result[b][:], y, ACT.Copy, scale=r_total[b][:])
+            nc.sync.dma_start(out[b], result[b][:])
+
+        def invert(b):
+            nc.vector.reciprocal(r_total[b][:], total[b][:])
+
+        gather_ks(0)
+        gather_kw(0)
+        gather_ks(1)
+        gather_v_scalar(0, 0)
+        group_q(0)
+        part_kw(0)
+        negate_sink(0)
+        negate_sink(1)
+        quant_q(0)
+        score(0)
+        row_max(0)
+        exponentials(0)
+        gather_kw(1)
+        group_q(1)
+        part_kw(1)
+        quant_q(1)
+        score(1)
+        row_max(1)
+        exponentials(1)
+        gather_v_scalar(0, 1)
+        gather_vs(0)
+        weigh(0)
+        invert(0)
+        gather_vs(1)
+        gather_v_scalar(1, 0)
+        gather_v_vector(1, 1)
+        weigh(1)
+        invert(1)
+        quant_v(0, 0)
+        quant_v(0, 1)
+        quant_w(0)
+        finish(0)
+        quant_w(1)
+        quant_v(1, 0)
+        quant_v(1, 1)
+        finish(1)

@@ -22,6 +22,8 @@ SEG = T // B
 PASSES = D // 512
 HALVES = DV // P
 COLS = N // 16
+HALF = N // 2
+FAR = float(2**100)
 
 
 def tile_attend_sink_seg_kernel(tc, qT, k_words, k_scales, vT, vs, sink, offs, out):
@@ -51,6 +53,7 @@ def tile_attend_sink_seg_kernel(tc, qT, k_words, k_scales, vT, vs, sink, offs, o
         sinks = sb("sinks", [P, B], F32)
         ident = sb("ident", [P, P], F32)
         warm = sb("warm", [P, 2], F32)
+        neg_all = sb("neg_all", [P, B, 2, HALF + 8], F32)
         ks_high = [sb("ks_high%d" % b, [P, N // 4], I32) for b in range(B)]
 
         nc.vector.memset(ks_pool[:], 0)
@@ -60,6 +63,7 @@ def tile_attend_sink_seg_kernel(tc, qT, k_words, k_scales, vT, vs, sink, offs, o
         make_identity(nc, ident[:])
         for b in range(B):
             nc.gpsimd.memset(ks_high[b][:], 0)
+        nc.gpsimd.memset(neg_all[:, :, :, HALF : HALF + 2], FAR)
 
         kw_hbm = k_words[0].rearrange("p t c -> p (t c)").bitcast(I32)
         ks_hbm = k_scales.bitcast(I32)
@@ -77,19 +81,9 @@ def tile_attend_sink_seg_kernel(tc, qT, k_words, k_scales, vT, vs, sink, offs, o
             with nc.allow_non_contiguous_dma(reason="one sink a partition"):
                 nc.sync.dma_start(sinks[rows, :], sink[:, rows, 0].rearrange("b q -> q b"))
 
-        load_v(0, 0)
-        load_sinks(slice(0, 96))
-        for quad in range(4):
-            nc.sync.dma_start(ks_pool[32 * quad : 32 * quad + 8, :], ks_hbm[:, 4 * quad : 4 * quad + 4, :])
-        nc.gpsimd.dma_start(vs_pool[0:1, :], vs[0:1, :])
-        load_kw(0)
-        load_q(0)
-        load_sinks(slice(96, P))
-        load_v(0, 1)
-        load_kw(1)
-        load_q(1)
-        load_v(1, 0)
-        load_v(1, 1)
+        def load_key_scales():
+            for quad in range(4):
+                nc.sync.dma_start(ks_pool[32 * quad : 32 * quad + 8, :], ks_hbm[:, 4 * quad : 4 * quad + 4, :])
 
         ks_got = [sb("ks_got%d" % b, [P, N], U8) for b in range(B)]
         kw_got = [sb("kw_got%d" % b, [P, N], U32) for b in range(B)]
@@ -100,14 +94,13 @@ def tile_attend_sink_seg_kernel(tc, qT, k_words, k_scales, vT, vs, sink, offs, o
         q_codes = [sb("q_codes%d" % b, [P, PASSES * NQ], U32) for b in range(B)]
         q_scales = [sb("q_scales%d" % b, [P, PASSES * NQ], U8) for b in range(B)]
         v_got = [[sb("v_got%d%d" % (b, h), [P, N], BF16) for h in range(HALVES)] for b in range(B)]
-        v_in = [[sb("v_in%d%d" % (b, h), [P, 4 * P], BF16) for h in range(HALVES)] for b in range(B)]
+        v_in = [sb("v_in%d" % b, [P, HALVES, 4 * P], BF16) for b in range(B)]
         v_codes = [sb("v_codes%d" % b, [P, DV], U32) for b in range(B)]
         v_scales = [sb("v_scales%d" % b, [P, DV], U8) for b in range(B)]
-        neg_a = [sb("neg_a%d" % b, [P, N + 1], F32) for b in range(B)]
         neg_m = [sb("neg_m%d" % b, [P, 1], F32) for b in range(B)]
-        probs = [sb("probs%d" % b, [P, N + 1], F32) for b in range(B)]
-        total = [sb("total%d" % b, [P, 1], F32) for b in range(B)]
-        r_total = [sb("r_total%d" % b, [P, 1], F32) for b in range(B)]
+        probs = [sb("probs%d" % b, [P, 2, 2, P + 8], F32) for b in range(B)]
+        total = sb("total", [P, B], F32)
+        r_total = sb("r_total", [P, B], F32)
         w_bf = [sb("w_bf%d" % b, [P, 4 * NQ], BF16) for b in range(B)]
         w_codes = [sb("w_codes%d" % b, [P, NQ], U32) for b in range(B)]
         w_scales = [sb("w_scales%d" % b, [P, NQ], U8) for b in range(B)]
@@ -116,6 +109,9 @@ def tile_attend_sink_seg_kernel(tc, qT, k_words, k_scales, vT, vs, sink, offs, o
         scores = [psum.tile([P, N], F32, name="scores%d" % b) for b in range(B)]
         turned_v = [psum.tile([P, HALVES, 2, P], F32, name="turned_v%d" % b) for b in range(B)]
         turned_p = [psum.tile([P, 4, NQ], F32, name="turned_p%d" % b) for b in range(B)]
+
+        def in_runs(got):
+            return got.rearrange("p (u g r) -> p g u r", u=2, r=16)
 
         def gather_ks(b):
             nc.vector.tensor_copy(ks_got[b][:], listed(ks_pool[:].bitcast(U8), b))
@@ -130,46 +126,48 @@ def tile_attend_sink_seg_kernel(tc, qT, k_words, k_scales, vT, vs, sink, offs, o
             )
 
         def gather_vs(b):
-            nc.vector.tensor_copy(vs_got[b][:], listed(vs_pool[:], b))
+            nc.vector.tensor_copy(in_runs(vs_got[b][:].bitcast(U32)), listed(vs_pool[:].bitcast(U32), b))
             turned = psum.tile([P, 4, P], F32, name="spare%d" % b, tag="spare%d" % b)
             for t in range(4):
-                nc.tensor.transpose(turned[:, t, :], vs_got[b][:, t:N:4], ident[:])
-            nc.vector.tensor_copy(vs_col[b][:], turned[:, :, 0])
+                nc.tensor.transpose(turned[:, t, :], vs_got[b][:, (t // 2) * HALF + t % 2 : (t // 2 + 1) * HALF : 2], ident[:])
+            nc.scalar.copy(vs_col[b][:], turned[:, :, 0])
 
-        def group_q(b):
-            nc.scalar.activation(
+        def group_q(b, copy):
+            copy(
                 q_bf[b][:].rearrange("p (o q j) -> p o q j", o=PASSES, j=4),
                 q_raw[b][:].rearrange("p o (j q) -> p o q j", j=4),
-                ACT.Copy,
             )
 
         def quant_q(b):
             nc.vector.quantize_mx(q_codes[b][:].bitcast(FP8X4), q_scales[b][:], q_bf[b][:])
 
-        def paired(b, h):
-            return v_got[b][h][:].rearrange("p (u s j) -> p s u j", u=2, j=2)
 
         def turn_v(b, h):
             words = v_got[b][h][:].bitcast(F32)
             for u in range(2):
                 nc.tensor.transpose(turned_v[b][:, h, u, :], words[:, u * P : (u + 1) * P], ident[:])
             nc.scalar.copy(
-                v_in[b][h][:].bitcast(F32).rearrange("p (e u) -> p e u", u=2),
+                v_in[b][:, h, :].bitcast(F32).rearrange("p (e u) -> p e u", u=2),
                 turned_v[b][:, h].rearrange("p u e -> p e u"),
             )
 
         def gather_v_scalar(b, h):
             nc.scalar.activation(v_bf[h][:, seg(b)], v_raw[h][:, seg(b)], ACT.Copy)
-            nc.scalar.activation(paired(b, h), listed(v_bf[h][:], b), ACT.Copy)
+            nc.scalar.activation(in_runs(v_got[b][h][:]), listed(v_bf[h][:], b), ACT.Copy)
             turn_v(b, h)
 
         def gather_v_vector(b, h):
-            nc.vector.tensor_copy(paired(b, h), listed(v_raw[h][:], b))
+            nc.vector.tensor_copy(in_runs(v_got[b][h][:]), listed(v_raw[h][:], b))
             turn_v(b, h)
 
         def quant_v(b, h):
             cols = slice(h * P, (h + 1) * P)
-            nc.vector.quantize_mx(v_codes[b][:, cols].bitcast(FP8X4), v_scales[b][:, cols], v_in[b][h][:])
+            nc.vector.quantize_mx(v_codes[b][:, cols].bitcast(FP8X4), v_scales[b][:, cols], v_in[b][:, h, :])
+
+        def quant_v_whole(b):
+            nc.vector.quantize_mx(
+                v_codes[b][:].bitcast(FP8X4), v_scales[b][:], v_in[b][:].rearrange("p h c -> p (h c)")
+            )
 
         def score(b):
             k_planes = [ks_got[b][:], ks_high[b][:].bitcast(U8)]
@@ -185,15 +183,15 @@ def tile_attend_sink_seg_kernel(tc, qT, k_words, k_scales, vT, vs, sink, offs, o
                     stop=(o == PASSES - 1),
                 )
 
-        def negate_sink(b):
-            nc.gpsimd.tensor_scalar(neg_a[b][:, N : N + 1], sinks[:, b : b + 1], -1.0, 0.0, ALU.mult, ALU.add)
+        def negate_sinks():
+            nc.gpsimd.tensor_scalar(neg_all[:, :, 0, HALF], sinks[:], -1.0, 0.0, ALU.mult, ALU.add)
 
         def row_max(b):
             nc.vector.tensor_scalar(
-                neg_a[b][:, 0:N].rearrange("p (t s) -> p t s", t=4),
-                scores[b][:].rearrange("p (s t) -> p t s", t=4),
+                neg_all[:, b, :, 0:HALF].rearrange("p u (g r) -> p u g r", r=16),
+                scores[b][:].rearrange("p (g u r) -> p u g r", u=2, r=16),
                 -1.0,
-                neg_a[b][:, N : N + 1],
+                neg_all[:, b, 0, HALF : HALF + 1],
                 ALU.mult,
                 ALU.min,
                 accum_out=neg_m[b][:],
@@ -201,10 +199,15 @@ def tile_attend_sink_seg_kernel(tc, qT, k_words, k_scales, vT, vs, sink, offs, o
 
         def exponentials(b):
             nc.scalar.activation(
-                probs[b][:], neg_a[b][:], ACT.Exp, bias=neg_m[b][:], scale=-1.0, accum_out=total[b][:]
+                probs[b][:, :, :, 0 : P + 1],
+                neg_all[:, b, :, 0 : HALF + 2].rearrange("p u (s j) -> p u j s", j=2),
+                ACT.Exp,
+                bias=neg_m[b][:],
+                scale=-1.0,
+                accum_out=total[:, b : b + 1],
             )
             for t in range(4):
-                nc.tensor.transpose(turned_p[b][:, t, :], probs[b][:, t * P : (t + 1) * P], ident[:])
+                nc.tensor.transpose(turned_p[b][:, t, :], probs[b][:, t // 2, t % 2, 0:P], ident[:])
 
         def weigh(b):
             nc.vector.tensor_tensor(
@@ -229,26 +232,37 @@ def tile_attend_sink_seg_kernel(tc, qT, k_words, k_scales, vT, vs, sink, offs, o
                 start=True,
                 stop=True,
             )
-            nc.scalar.activation(result[b][:], y, ACT.Copy, scale=r_total[b][:])
+            nc.scalar.activation(result[b][:], y, ACT.Copy, scale=r_total[:, b : b + 1])
             nc.sync.dma_start(out[b], result[b][:])
 
-        def invert(b):
-            nc.vector.reciprocal(r_total[b][:], total[b][:])
+        def invert():
+            nc.vector.reciprocal(r_total[:], total[:])
 
+        load_v(0, 0)
+        load_sinks(slice(0, 96))
+        load_key_scales()
+        nc.gpsimd.dma_start(vs_pool[0:1, :], vs[0:1, :])
+        load_kw(0)
+        load_q(0)
+        load_sinks(slice(96, P))
+        load_v(0, 1)
+        load_kw(1)
+        load_q(1)
+        load_v(1, 0)
+        load_v(1, 1)
         gather_ks(0)
         gather_kw(0)
         gather_ks(1)
         gather_v_scalar(0, 0)
-        group_q(0)
+        group_q(0, nc.scalar.copy)
         part_kw(0)
-        negate_sink(0)
-        negate_sink(1)
+        negate_sinks()
         quant_q(0)
         score(0)
         row_max(0)
         exponentials(0)
         gather_kw(1)
-        group_q(1)
+        group_q(1, nc.scalar.copy)
         part_kw(1)
         quant_q(1)
         score(1)
@@ -257,14 +271,12 @@ def tile_attend_sink_seg_kernel(tc, qT, k_words, k_scales, vT, vs, sink, offs, o
         gather_v_scalar(0, 1)
         gather_vs(0)
         weigh(0)
-        invert(0)
         gather_vs(1)
         gather_v_scalar(1, 0)
         gather_v_vector(1, 1)
         weigh(1)
-        invert(1)
-        quant_v(0, 0)
-        quant_v(0, 1)
+        invert()
+        quant_v_whole(0)
         quant_w(0)
         finish(0)
         quant_w(1)

@@ -32,8 +32,8 @@ def tile_attend_sink_seg_kernel(tc, qT, k_words, k_scales, vT, vs, sink, offs, o
         keep = ctx.enter_context(tc.tile_pool(name="keep", bufs=1))
         psum = ctx.enter_context(tc.psum_pool(name="psum", bufs=1))
 
-        def sb(name, shape, dtype):
-            return keep.tile(shape, dtype, name=name, align_bytes=64)
+        def sb(name, shape, dtype, tag=None):
+            return keep.tile(shape, dtype, name=name, tag=tag or name, align_bytes=64)
 
         offsets = keep.tile([P, B * COLS], U16, name="offsets")
         nc.sync.dma_start(offsets[:], offs)
@@ -44,25 +44,25 @@ def tile_attend_sink_seg_kernel(tc, qT, k_words, k_scales, vT, vs, sink, offs, o
         def listed(window, b):
             return window[:, 0 : (b + 1) * SEG].indirect(offsets[:, b * COLS : (b + 1) * COLS])
 
-        ks_pool = sb("ks_pool", [P, T // 4], I32)
+        ks_pool = sb("ks_pool", [P, T // 4], I32, tag="early")
         vs_pool = sb("vs_pool", [P, T], F32)
         kw_pool = sb("kw_pool", [P, T], I32)
-        v_raw = [sb("v_raw%d" % h, [P, T], F32) for h in range(HALVES)]
-        v_bf = [sb("v_bf%d" % h, [P, T], BF16) for h in range(HALVES)]
+        v_raw = {(0, 0): sb("v_raw00", [P, SEG], F32), (1, 0): sb("v_raw10", [P, SEG], F32)}
+        v_raw.setdefault((0, 1), v_raw[0, 0])
+        v_bf = sb("v_bf", [P, 3 * SEG], BF16)
         q_raw = [sb("q_raw%d" % b, [P, PASSES, 4 * NQ], F32) for b in range(B)]
         sinks = sb("sinks", [P, B], F32)
         ident = sb("ident", [P, P], F32)
         warm = sb("warm", [P, 2], F32)
         neg_all = sb("neg_all", [P, B, 2, HALF + 8], F32)
-        ks_high = [sb("ks_high%d" % b, [P, N // 4], I32) for b in range(B)]
+        ks_high = sb("ks_high", [P, B * N // 4], I32)
 
-        nc.vector.memset(ks_pool[:], 0)
+        nc.gpsimd.memset(ks_pool[:], 0)
         nc.vector.memset(warm[:, 0:1], 0.0)
         nc.scalar.activation(warm[:, 1:2], warm[:, 0:1], ACT.Exp)
         nc.vector.memset(vs_pool[:], 0.0)
         make_identity(nc, ident[:])
-        for b in range(B):
-            nc.gpsimd.memset(ks_high[b][:], 0)
+        nc.gpsimd.memset(ks_high[96:P, :], 0)
         nc.gpsimd.memset(neg_all[:, :, :, HALF : HALF + 2], FAR)
 
         kw_hbm = k_words[0].rearrange("p t c -> p (t c)").bitcast(I32)
@@ -75,25 +75,25 @@ def tile_attend_sink_seg_kernel(tc, qT, k_words, k_scales, vT, vs, sink, offs, o
             nc.sync.dma_start(q_raw[b][:], qT[b].rearrange("(o p j) q -> p o (j q)", o=PASSES, j=4))
 
         def load_v(b, h):
-            nc.sync.dma_start(v_raw[h][:, seg(b)], vT[h * P : (h + 1) * P, seg(b)])
+            nc.sync.dma_start(v_raw[b, h][:], vT[h * P : (h + 1) * P, seg(b)])
 
-        def load_sinks(rows):
+        def load_sinks(rows, queue):
             with nc.allow_non_contiguous_dma(reason="one sink a partition"):
-                nc.sync.dma_start(sinks[rows, :], sink[:, rows, 0].rearrange("b q -> q b"))
+                queue.dma_start(sinks[rows, :], sink[:, rows, 0].rearrange("b q -> q b"))
 
         def load_key_scales():
-            for quad in range(4):
-                nc.sync.dma_start(ks_pool[32 * quad : 32 * quad + 8, :], ks_hbm[:, 4 * quad : 4 * quad + 4, :])
+            for r in range(4):
+                nc.sync.dma_start(ks_pool[r:P:16, :], ks_hbm[:, r:16:4, :].rearrange("o f t -> f o t"))
 
-        ks_got = [sb("ks_got%d" % b, [P, N], U8) for b in range(B)]
+        ks_got = sb("ks_got", [P, B * N], U8)
         kw_got = [sb("kw_got%d" % b, [P, N], U32) for b in range(B)]
-        k_codes = [sb("k_codes%d" % b, [P, PASSES, 2 * N], U8) for b in range(B)]
-        vs_got = [sb("vs_got%d" % b, [P, N], F32) for b in range(B)]
+        k_codes = [sb("k_codes%d" % b, [P, PASSES, 2 * N], U8, tag="mid%d" % b) for b in range(B)]
+        vs_got = {}
         vs_col = [sb("vs_col%d" % b, [P, 4], F32) for b in range(B)]
         q_bf = [sb("q_bf%d" % b, [P, PASSES * NQ * 4], BF16) for b in range(B)]
-        q_codes = [sb("q_codes%d" % b, [P, PASSES * NQ], U32) for b in range(B)]
+        q_codes = [sb("q_codes%d" % b, [P, PASSES * NQ], U32, tag="late%d" % b) for b in range(B)]
         q_scales = [sb("q_scales%d" % b, [P, PASSES * NQ], U8) for b in range(B)]
-        v_got = [[sb("v_got%d%d" % (b, h), [P, N], BF16) for h in range(HALVES)] for b in range(B)]
+        v_got = [{}, {}]
         v_in = [sb("v_in%d" % b, [P, HALVES, 4 * P], BF16) for b in range(B)]
         v_codes = [sb("v_codes%d" % b, [P, DV], U32) for b in range(B)]
         v_scales = [sb("v_scales%d" % b, [P, DV], U8) for b in range(B)]
@@ -106,16 +106,16 @@ def tile_attend_sink_seg_kernel(tc, qT, k_words, k_scales, vT, vs, sink, offs, o
         w_scales = [sb("w_scales%d" % b, [P, NQ], U8) for b in range(B)]
         result = [sb("result%d" % b, [P, DV], F32) for b in range(B)]
 
-        scores = [psum.tile([P, N], F32, name="scores%d" % b) for b in range(B)]
+        scores = [psum.tile([P, N], F32, name="scores%d" % b, tag="scores%d" % b) for b in range(B)]
         turned_v = [psum.tile([P, HALVES, 2, P], F32, name="turned_v%d" % b) for b in range(B)]
         turned_p = [psum.tile([P, 4, NQ], F32, name="turned_p%d" % b) for b in range(B)]
 
         def in_runs(got):
             return got.rearrange("p (u g r) -> p g u r", u=2, r=16)
 
-        def gather_ks(b):
-            nc.vector.tensor_copy(ks_got[b][:], listed(ks_pool[:].bitcast(U8), b))
-            nc.gpsimd.dma_start(ks_high[b][0:100, :], ks_got[b][:].bitcast(I32)[4:104, :])
+        def gather_ks():
+            nc.vector.tensor_copy(ks_got[:], ks_pool[:].bitcast(U8).indirect(offsets[:]))
+            nc.sync.dma_start(ks_high[0:112, :], ks_got[:].bitcast(I32)[16:P, :])
 
         def gather_kw(b):
             nc.vector.tensor_copy(kw_got[b][:], listed(kw_pool[:].bitcast(U32), b))
@@ -125,9 +125,12 @@ def tile_attend_sink_seg_kernel(tc, qT, k_words, k_scales, vT, vs, sink, offs, o
                 k_codes[b][:].bitcast(U16), kw_got[b][:].bitcast(U16).rearrange("p (s o) -> p o s", o=PASSES)
             )
 
-        def gather_vs(b):
+        def gather_vs(b, tag=None):
+            vs_got[b] = sb("vs_got%d" % b, [P, N], F32, tag=tag)
             nc.vector.tensor_copy(in_runs(vs_got[b][:].bitcast(U32)), listed(vs_pool[:].bitcast(U32), b))
-            turned = psum.tile([P, 4, P], F32, name="spare%d" % b, tag="spare%d" % b)
+
+        def turn_vs(b):
+            turned = psum.tile([P, 4, P], F32, name="turned_vs%d" % b, tag="scores%d" % b)
             for t in range(4):
                 nc.tensor.transpose(turned[:, t, :], vs_got[b][:, (t // 2) * HALF + t % 2 : (t // 2 + 1) * HALF : 2], ident[:])
             nc.scalar.copy(vs_col[b][:], turned[:, :, 0])
@@ -151,13 +154,17 @@ def tile_attend_sink_seg_kernel(tc, qT, k_words, k_scales, vT, vs, sink, offs, o
                 turned_v[b][:, h].rearrange("p u e -> p e u"),
             )
 
+        def cast_v(b, h):
+            nc.scalar.activation(v_bf[:, seg(b + h)], v_raw[b, h][:], ACT.Copy)
+
         def gather_v_scalar(b, h):
-            nc.scalar.activation(v_bf[h][:, seg(b)], v_raw[h][:, seg(b)], ACT.Copy)
-            nc.scalar.activation(in_runs(v_got[b][h][:]), listed(v_bf[h][:], b), ACT.Copy)
+            v_got[b][h] = sb("v_got%d%d" % (b, h), [P, N], BF16)
+            nc.scalar.activation(in_runs(v_got[b][h][:]), listed(v_bf[:, h * SEG :], b), ACT.Copy)
             turn_v(b, h)
 
-        def gather_v_vector(b, h):
-            nc.vector.tensor_copy(in_runs(v_got[b][h][:]), listed(v_raw[h][:], b))
+        def gather_v_vector(b, h, tag):
+            v_got[b][h] = sb("v_got%d%d" % (b, h), [P, N], BF16, tag=tag)
+            nc.vector.tensor_copy(in_runs(v_got[b][h][:]), listed(v_raw[b, h][:], b))
             turn_v(b, h)
 
         def quant_v(b, h):
@@ -170,7 +177,7 @@ def tile_attend_sink_seg_kernel(tc, qT, k_words, k_scales, vT, vs, sink, offs, o
             )
 
         def score(b):
-            k_planes = [ks_got[b][:], ks_high[b][:].bitcast(U8)]
+            k_planes = [plane[:, b * N : (b + 1) * N] for plane in (ks_got[:], ks_high[:].bitcast(U8))]
             for o in range(PASSES):
                 cols = slice(o * NQ, (o + 1) * NQ)
                 nc.tensor.matmul_mx(
@@ -184,7 +191,7 @@ def tile_attend_sink_seg_kernel(tc, qT, k_words, k_scales, vT, vs, sink, offs, o
                 )
 
         def negate_sinks():
-            nc.gpsimd.tensor_scalar(neg_all[:, :, 0, HALF], sinks[:], -1.0, 0.0, ALU.mult, ALU.add)
+            nc.scalar.activation(neg_all[:, :, 0, HALF], sinks[:], ACT.Copy, scale=-1.0)
 
         def row_max(b):
             nc.vector.tensor_scalar(
@@ -239,47 +246,51 @@ def tile_attend_sink_seg_kernel(tc, qT, k_words, k_scales, vT, vs, sink, offs, o
             nc.vector.reciprocal(r_total[:], total[:])
 
         load_v(0, 0)
-        load_sinks(slice(0, 96))
+        load_sinks(slice(0, 96), nc.sync)
         load_key_scales()
+        load_sinks(slice(96, P), nc.gpsimd)
         nc.gpsimd.dma_start(vs_pool[0:1, :], vs[0:1, :])
-        load_kw(0)
         load_q(0)
-        load_sinks(slice(96, P))
-        load_v(0, 1)
-        load_kw(1)
+        load_kw(0)
         load_q(1)
+        load_kw(1)
         load_v(1, 0)
+        gather_ks()
+        v_raw.setdefault((1, 1), sb("v_raw11", [P, SEG], F32, tag="early"))
         load_v(1, 1)
-        gather_ks(0)
-        gather_kw(0)
-        gather_ks(1)
+        cast_v(0, 0)
+        load_v(0, 1)
         gather_v_scalar(0, 0)
         group_q(0, nc.scalar.copy)
-        part_kw(0)
         negate_sinks()
+        gather_kw(0)
         quant_q(0)
+        part_kw(0)
         score(0)
+        group_q(1, nc.scalar.copy)
+        gather_kw(1)
+        quant_q(1)
+        part_kw(1)
+        score(1)
         row_max(0)
         exponentials(0)
-        gather_kw(1)
-        group_q(1, nc.scalar.copy)
-        part_kw(1)
-        quant_q(1)
-        score(1)
+        gather_vs(0, "mid0")
+        turn_vs(0)
         row_max(1)
         exponentials(1)
-        gather_v_scalar(0, 1)
-        gather_vs(0)
-        weigh(0)
-        gather_vs(1)
+        gather_vs(1, "mid1")
+        turn_vs(1)
+        cast_v(1, 0)
         gather_v_scalar(1, 0)
-        gather_v_vector(1, 1)
-        weigh(1)
+        cast_v(1, 1)
+        gather_v_scalar(1, 1)
+        gather_v_vector(0, 1, "late1")
+        weigh(0)
         invert()
-        quant_v_whole(0)
         quant_w(0)
-        finish(0)
+        quant_v_whole(1)
+        weigh(1)
         quant_w(1)
-        quant_v(1, 0)
-        quant_v(1, 1)
         finish(1)
+        quant_v_whole(0)
+        finish(0)

@@ -22,8 +22,6 @@ SEG = T // B
 PASSES = D // 512
 HALVES = DV // P
 COLS = N // 16
-HALF = N // 2
-FAR = float(2**100)
 
 
 def tile_attend_sink_seg_kernel(tc, qT, k_words, k_scales, vT, vs, sink, offs, out):
@@ -49,21 +47,22 @@ def tile_attend_sink_seg_kernel(tc, qT, k_words, k_scales, vT, vs, sink, offs, o
         kw_pool = sb("kw_pool", [P, T], I32)
         v_raw = {(0, 0): sb("v_raw00", [P, SEG], F32), (1, 0): sb("v_raw10", [P, SEG], F32)}
         v_raw.setdefault((0, 1), v_raw[0, 0])
-        v_bf = sb("v_bf", [P, 3 * SEG], BF16)
+        v_bf = {(b, h): sb("v_bf%d%d" % (b, h), [P, (b + 1) * SEG], BF16) for b, h in ((0, 0), (1, 0), (1, 1))}
         q_raw = [sb("q_raw%d" % b, [P, PASSES, 4 * NQ], F32) for b in range(B)]
         sinks = sb("sinks", [P, B], F32)
         ident = sb("ident", [P, P], F32)
         warm = sb("warm", [P, 2], F32)
-        neg_all = sb("neg_all", [P, B, 2, HALF + 8], F32)
+        neg_all = sb("neg_all", [P, B, N + 8], F32)
         ks_high = sb("ks_high", [P, B * N // 4], I32)
 
         nc.gpsimd.memset(ks_pool[:], 0)
         nc.vector.memset(warm[:, 0:1], 0.0)
         nc.scalar.activation(warm[:, 1:2], warm[:, 0:1], ACT.Exp)
         nc.vector.memset(vs_pool[:], 0.0)
+        for h in range(HALVES):
+            nc.vector.memset(v_bf[1, h][:, seg(0)].bitcast(I32), 0)
         make_identity(nc, ident[:])
         nc.gpsimd.memset(ks_high[96:P, :], 0)
-        nc.gpsimd.memset(neg_all[:, :, :, HALF : HALF + 2], FAR)
 
         kw_hbm = k_words[0].rearrange("p t c -> p (t c)").bitcast(I32)
         ks_hbm = k_scales.bitcast(I32)
@@ -98,7 +97,7 @@ def tile_attend_sink_seg_kernel(tc, qT, k_words, k_scales, vT, vs, sink, offs, o
         v_codes = [sb("v_codes%d" % b, [P, DV], U32) for b in range(B)]
         v_scales = [sb("v_scales%d" % b, [P, DV], U8) for b in range(B)]
         neg_m = [sb("neg_m%d" % b, [P, 1], F32) for b in range(B)]
-        probs = [sb("probs%d" % b, [P, 2, 2, P + 8], F32) for b in range(B)]
+        probs = [sb("probs%d" % b, [P, N + 8], F32) for b in range(B)]
         total = sb("total", [P, B], F32)
         r_total = sb("r_total", [P, B], F32)
         w_bf = [sb("w_bf%d" % b, [P, 4 * NQ], BF16) for b in range(B)]
@@ -109,9 +108,6 @@ def tile_attend_sink_seg_kernel(tc, qT, k_words, k_scales, vT, vs, sink, offs, o
         scores = [psum.tile([P, N], F32, name="scores%d" % b, tag="scores%d" % b) for b in range(B)]
         turned_v = [psum.tile([P, HALVES, 2, P], F32, name="turned_v%d" % b) for b in range(B)]
         turned_p = [psum.tile([P, 4, NQ], F32, name="turned_p%d" % b) for b in range(B)]
-
-        def in_runs(got):
-            return got.rearrange("p (u g r) -> p g u r", u=2, r=16)
 
         def gather_ks():
             nc.vector.tensor_copy(ks_got[:], ks_pool[:].bitcast(U8).indirect(offsets[:]))
@@ -127,12 +123,12 @@ def tile_attend_sink_seg_kernel(tc, qT, k_words, k_scales, vT, vs, sink, offs, o
 
         def gather_vs(b, tag=None):
             vs_got[b] = sb("vs_got%d" % b, [P, N], F32, tag=tag)
-            nc.vector.tensor_copy(in_runs(vs_got[b][:].bitcast(U32)), listed(vs_pool[:].bitcast(U32), b))
+            nc.vector.tensor_copy(vs_got[b][:], listed(vs_pool[:], b))
 
         def turn_vs(b):
             turned = psum.tile([P, 4, P], F32, name="turned_vs%d" % b, tag="scores%d" % b)
             for t in range(4):
-                nc.tensor.transpose(turned[:, t, :], vs_got[b][:, (t // 2) * HALF + t % 2 : (t // 2 + 1) * HALF : 2], ident[:])
+                nc.tensor.transpose(turned[:, t, :], vs_got[b][:, t:N:4], ident[:])
             nc.scalar.copy(vs_col[b][:], turned[:, :, 0])
 
         def group_q(b, copy):
@@ -148,23 +144,23 @@ def tile_attend_sink_seg_kernel(tc, qT, k_words, k_scales, vT, vs, sink, offs, o
         def turn_v(b, h):
             words = v_got[b][h][:].bitcast(F32)
             for u in range(2):
-                nc.tensor.transpose(turned_v[b][:, h, u, :], words[:, u * P : (u + 1) * P], ident[:])
+                nc.tensor.transpose(turned_v[b][:, h, u, :], words[:, u : 2 * P : 2], ident[:])
             nc.scalar.copy(
                 v_in[b][:, h, :].bitcast(F32).rearrange("p (e u) -> p e u", u=2),
                 turned_v[b][:, h].rearrange("p u e -> p e u"),
             )
 
         def cast_v(b, h):
-            nc.scalar.activation(v_bf[:, seg(b + h)], v_raw[b, h][:], ACT.Copy)
+            nc.scalar.activation(v_bf[b, h][:, seg(b)], v_raw[b, h][:], ACT.Copy)
 
         def gather_v_scalar(b, h):
             v_got[b][h] = sb("v_got%d%d" % (b, h), [P, N], BF16)
-            nc.scalar.activation(in_runs(v_got[b][h][:]), listed(v_bf[:, h * SEG :], b), ACT.Copy)
+            nc.scalar.activation(v_got[b][h][:], listed(v_bf[b, h][:], b), ACT.Copy)
             turn_v(b, h)
 
         def gather_v_vector(b, h, tag):
             v_got[b][h] = sb("v_got%d%d" % (b, h), [P, N], BF16, tag=tag)
-            nc.vector.tensor_copy(in_runs(v_got[b][h][:]), listed(v_raw[b, h][:], b))
+            nc.vector.tensor_copy(v_got[b][h][:], listed(v_raw[b, h][:], b))
             turn_v(b, h)
 
         def quant_v(b, h):
@@ -191,14 +187,14 @@ def tile_attend_sink_seg_kernel(tc, qT, k_words, k_scales, vT, vs, sink, offs, o
                 )
 
         def negate_sinks():
-            nc.scalar.activation(neg_all[:, :, 0, HALF], sinks[:], ACT.Copy, scale=-1.0)
+            nc.scalar.activation(neg_all[:, :, N], sinks[:], ACT.Copy, scale=-1.0)
 
         def row_max(b):
             nc.vector.tensor_scalar(
-                neg_all[:, b, :, 0:HALF].rearrange("p u (g r) -> p u g r", r=16),
-                scores[b][:].rearrange("p (g u r) -> p u g r", u=2, r=16),
+                neg_all[:, b, 0:N].rearrange("p (t s) -> p t s", t=4),
+                scores[b][:].rearrange("p (s t) -> p t s", t=4),
                 -1.0,
-                neg_all[:, b, 0, HALF : HALF + 1],
+                neg_all[:, b, N : N + 1],
                 ALU.mult,
                 ALU.min,
                 accum_out=neg_m[b][:],
@@ -206,15 +202,15 @@ def tile_attend_sink_seg_kernel(tc, qT, k_words, k_scales, vT, vs, sink, offs, o
 
         def exponentials(b):
             nc.scalar.activation(
-                probs[b][:, :, :, 0 : P + 1],
-                neg_all[:, b, :, 0 : HALF + 2].rearrange("p u (s j) -> p u j s", j=2),
+                probs[b][:, 0 : N + 1],
+                neg_all[:, b, 0 : N + 1],
                 ACT.Exp,
                 bias=neg_m[b][:],
                 scale=-1.0,
                 accum_out=total[:, b : b + 1],
             )
             for t in range(4):
-                nc.tensor.transpose(turned_p[b][:, t, :], probs[b][:, t // 2, t % 2, 0:P], ident[:])
+                nc.tensor.transpose(turned_p[b][:, t, :], probs[b][:, t * P : (t + 1) * P], ident[:])
 
         def weigh(b):
             nc.vector.tensor_tensor(

@@ -47,22 +47,20 @@ def tile_attend_sink_seg_kernel(tc, qT, k_words, k_scales, vT, vs, sink, offs, o
         kw_pool = sb("kw_pool", [P, T], I32)
         v_raw = {(0, 0): sb("v_raw00", [P, SEG], F32), (1, 0): sb("v_raw10", [P, SEG], F32)}
         v_raw.setdefault((0, 1), v_raw[0, 0])
-        v_bf = {(b, h): sb("v_bf%d%d" % (b, h), [P, (b + 1) * SEG], BF16) for b, h in ((0, 0), (1, 0), (1, 1))}
+        v_bf = sb("v_bf", [P, 3 * SEG], BF16)
         q_raw = [sb("q_raw%d" % b, [P, PASSES, 4 * NQ], F32) for b in range(B)]
         sinks = sb("sinks", [P, B], F32)
         ident = sb("ident", [P, P], F32)
         warm = sb("warm", [P, 2], F32)
         neg_all = sb("neg_all", [P, B, N + 8], F32)
-        ks_high = sb("ks_high", [P, B * N // 4], I32)
+        k_planes = sb("k_planes", [P, PASSES * B * N // 4], I32)
 
-        nc.gpsimd.memset(ks_pool[:], 0)
+        nc.gpsimd.memset(ks_pool[0:96, :], 0)
         nc.vector.memset(warm[:, 0:1], 0.0)
         nc.scalar.activation(warm[:, 1:2], warm[:, 0:1], ACT.Exp)
         nc.vector.memset(vs_pool[:], 0.0)
-        for h in range(HALVES):
-            nc.vector.memset(v_bf[1, h][:, seg(0)].bitcast(I32), 0)
         make_identity(nc, ident[:])
-        nc.gpsimd.memset(ks_high[96:P, :], 0)
+        nc.gpsimd.memset(k_planes[:], 0)
 
         kw_hbm = k_words[0].rearrange("p t c -> p (t c)").bitcast(I32)
         ks_hbm = k_scales.bitcast(I32)
@@ -81,8 +79,7 @@ def tile_attend_sink_seg_kernel(tc, qT, k_words, k_scales, vT, vs, sink, offs, o
                 queue.dma_start(sinks[rows, :], sink[:, rows, 0].rearrange("b q -> q b"))
 
         def load_key_scales():
-            for r in range(4):
-                nc.sync.dma_start(ks_pool[r:P:16, :], ks_hbm[:, r:16:4, :].rearrange("o f t -> f o t"))
+            nc.sync.dma_start(ks_pool[96:P, :], ks_hbm.rearrange("o f t -> f o t"))
 
         ks_got = sb("ks_got", [P, B * N], U8)
         kw_got = [sb("kw_got%d" % b, [P, N], U32) for b in range(B)]
@@ -111,7 +108,9 @@ def tile_attend_sink_seg_kernel(tc, qT, k_words, k_scales, vT, vs, sink, offs, o
 
         def gather_ks():
             nc.vector.tensor_copy(ks_got[:], ks_pool[:].bitcast(U8).indirect(offsets[:]))
-            nc.sync.dma_start(ks_high[0:112, :], ks_got[:].bitcast(I32)[16:P, :])
+            for quad in range(4):
+                rows = ks_got[:].bitcast(I32)[96 + 8 * quad : 104 + 8 * quad, :]
+                nc.sync.dma_start(k_planes[32 * quad : 32 * quad + 4, :], rows)
 
         def gather_kw(b):
             nc.vector.tensor_copy(kw_got[b][:], listed(kw_pool[:].bitcast(U32), b))
@@ -141,27 +140,29 @@ def tile_attend_sink_seg_kernel(tc, qT, k_words, k_scales, vT, vs, sink, offs, o
             nc.vector.quantize_mx(q_codes[b][:].bitcast(FP8X4), q_scales[b][:], q_bf[b][:])
 
 
-        def turn_v(b, h):
-            words = v_got[b][h][:].bitcast(F32)
+        def turn_v(b, h, pairs):
             for u in range(2):
-                nc.tensor.transpose(turned_v[b][:, h, u, :], words[:, u : 2 * P : 2], ident[:])
+                nc.tensor.transpose(turned_v[b][:, h, u, :], pairs[u], ident[:])
             nc.scalar.copy(
                 v_in[b][:, h, :].bitcast(F32).rearrange("p (e u) -> p e u", u=2),
                 turned_v[b][:, h].rearrange("p u e -> p e u"),
             )
 
         def cast_v(b, h):
-            nc.scalar.activation(v_bf[b, h][:, seg(b)], v_raw[b, h][:], ACT.Copy)
+            nc.scalar.activation(v_bf[:, seg(b + h)], v_raw[b, h][:], ACT.Copy)
 
-        def gather_v_scalar(b, h):
-            v_got[b][h] = sb("v_got%d%d" % (b, h), [P, N], BF16)
-            nc.scalar.activation(v_got[b][h][:], listed(v_bf[b, h][:], b), ACT.Copy)
-            turn_v(b, h)
+        def gather_v_scalar(b, h, tag=None):
+            v_got[b][h] = sb("v_got%d%d" % (b, h), [P, N], BF16, tag=tag)
+            dealt = v_got[b][h][:].rearrange("p (u s j) -> p s u j", u=2, j=2)
+            nc.scalar.activation(dealt, listed(v_bf[:, h * SEG :], b), ACT.Copy)
+            words = v_got[b][h][:].bitcast(F32)
+            turn_v(b, h, [words[:, u * P : (u + 1) * P] for u in range(2)])
 
         def gather_v_vector(b, h, tag):
             v_got[b][h] = sb("v_got%d%d" % (b, h), [P, N], BF16, tag=tag)
             nc.vector.tensor_copy(v_got[b][h][:], listed(v_raw[b, h][:], b))
-            turn_v(b, h)
+            words = v_got[b][h][:].bitcast(F32)
+            turn_v(b, h, [words[:, u : 2 * P : 2] for u in range(2)])
 
         def quant_v(b, h):
             cols = slice(h * P, (h + 1) * P)
@@ -173,7 +174,6 @@ def tile_attend_sink_seg_kernel(tc, qT, k_words, k_scales, vT, vs, sink, offs, o
             )
 
         def score(b):
-            k_planes = [plane[:, b * N : (b + 1) * N] for plane in (ks_got[:], ks_high[:].bitcast(U8))]
             for o in range(PASSES):
                 cols = slice(o * NQ, (o + 1) * NQ)
                 nc.tensor.matmul_mx(
@@ -181,13 +181,13 @@ def tile_attend_sink_seg_kernel(tc, qT, k_words, k_scales, vT, vs, sink, offs, o
                     lhsT=q_codes[b][:, cols].bitcast(FP8X4),
                     lhsT_scale=q_scales[b][:, cols],
                     rhs=k_codes[b][:, o, :].bitcast(FP4X4),
-                    rhs_scale=k_planes[o],
+                    rhs_scale=k_planes[:].bitcast(U8)[:, (o * B + b) * N : (o * B + b + 1) * N],
                     start=(o == 0),
                     stop=(o == PASSES - 1),
                 )
 
         def negate_sinks():
-            nc.scalar.activation(neg_all[:, :, N], sinks[:], ACT.Copy, scale=-1.0)
+            nc.gpsimd.tensor_scalar(neg_all[:, :, N], sinks[:], -1.0, 0.0, ALU.mult, ALU.add)
 
         def row_max(b):
             nc.vector.tensor_scalar(
@@ -241,16 +241,15 @@ def tile_attend_sink_seg_kernel(tc, qT, k_words, k_scales, vT, vs, sink, offs, o
         def invert():
             nc.vector.reciprocal(r_total[:], total[:])
 
-        load_v(0, 0)
-        load_sinks(slice(0, 96), nc.sync)
         load_key_scales()
-        load_sinks(slice(96, P), nc.gpsimd)
-        nc.gpsimd.dma_start(vs_pool[0:1, :], vs[0:1, :])
-        load_q(0)
+        load_sinks(slice(0, P), nc.gpsimd)
+        load_v(0, 0)
         load_kw(0)
-        load_q(1)
+        load_q(0)
         load_kw(1)
+        load_q(1)
         load_v(1, 0)
+        nc.sync.dma_start(vs_pool[0:1, :], vs[0:1, :])
         gather_ks()
         v_raw.setdefault((1, 1), sb("v_raw11", [P, SEG], F32, tag="early"))
         load_v(1, 1)
@@ -270,23 +269,23 @@ def tile_attend_sink_seg_kernel(tc, qT, k_words, k_scales, vT, vs, sink, offs, o
         score(1)
         row_max(0)
         exponentials(0)
-        gather_vs(0, "mid0")
-        turn_vs(0)
         row_max(1)
         exponentials(1)
-        gather_vs(1, "mid1")
-        turn_vs(1)
+        gather_vs(0)
+        turn_vs(0)
         cast_v(1, 0)
-        gather_v_scalar(1, 0)
+        gather_v_scalar(1, 0, "mid0")
         cast_v(1, 1)
         gather_v_scalar(1, 1)
         gather_v_vector(0, 1, "late1")
+        gather_vs(1, "mid1")
+        turn_vs(1)
         weigh(0)
         invert()
         quant_w(0)
-        quant_v_whole(1)
-        weigh(1)
-        quant_w(1)
-        finish(1)
         quant_v_whole(0)
         finish(0)
+        weigh(1)
+        quant_v_whole(1)
+        quant_w(1)
+        finish(1)

@@ -47,7 +47,7 @@ def tile_attend_sink_seg_kernel(tc, qT, k_words, k_scales, vT, vs, sink, offs, o
         kw_pool = sb("kw_pool", [P, T], I32)
         v_raw = {(0, 0): sb("v_raw00", [P, SEG], F32), (1, 0): sb("v_raw10", [P, SEG], F32)}
         v_raw.setdefault((0, 1), v_raw[0, 0])
-        v_bf = sb("v_bf", [P, 3 * SEG], BF16)
+        v_bf = sb("v_bf", [P, 3 * SEG], BF16, tag="cast")
         q_raw = [sb("q_raw%d" % b, [P, PASSES, 4 * NQ], F32) for b in range(B)]
         sinks = sb("sinks", [P, B], F32)
         ident = sb("ident", [P, P], F32)
@@ -90,7 +90,7 @@ def tile_attend_sink_seg_kernel(tc, qT, k_words, k_scales, vT, vs, sink, offs, o
         q_codes = [sb("q_codes%d" % b, [P, PASSES * NQ], U32, tag="late%d" % b) for b in range(B)]
         q_scales = [sb("q_scales%d" % b, [P, PASSES * NQ], U8) for b in range(B)]
         v_got = [{}, {}]
-        v_in = [sb("v_in%d" % b, [P, HALVES, 4 * P], BF16) for b in range(B)]
+        v_in = {}
         v_codes = [sb("v_codes%d" % b, [P, DV], U32) for b in range(B)]
         v_scales = [sb("v_scales%d" % b, [P, DV], U8) for b in range(B)]
         neg_m = [sb("neg_m%d" % b, [P, 1], F32) for b in range(B)]
@@ -103,7 +103,8 @@ def tile_attend_sink_seg_kernel(tc, qT, k_words, k_scales, vT, vs, sink, offs, o
         result = [sb("result%d" % b, [P, DV], F32) for b in range(B)]
 
         scores = [psum.tile([P, N], F32, name="scores%d" % b, tag="scores%d" % b) for b in range(B)]
-        turned_v = [psum.tile([P, HALVES, 2, P], F32, name="turned_v%d" % b) for b in range(B)]
+        turned_v = {0: psum.tile([P, HALVES, 2, P], F32, name="turned_v0")}
+        pairs = {}
         turned_p = [psum.tile([P, 4, NQ], F32, name="turned_p%d" % b) for b in range(B)]
 
         def gather_ks():
@@ -122,30 +123,34 @@ def tile_attend_sink_seg_kernel(tc, qT, k_words, k_scales, vT, vs, sink, offs, o
 
         def gather_vs(b, tag=None):
             vs_got[b] = sb("vs_got%d" % b, [P, N], F32, tag=tag)
-            nc.vector.tensor_copy(vs_got[b][:], listed(vs_pool[:], b))
+            dealt = vs_got[b][:].bitcast(U32).rearrange("p (u s j) -> p s u j", u=2, j=2)
+            nc.vector.tensor_copy(dealt, listed(vs_pool[:].bitcast(U32), b))
 
         def turn_vs(b):
-            turned = psum.tile([P, 4, P], F32, name="turned_vs%d" % b, tag="scores%d" % b)
+            turned = psum.tile([P, 4, P], F32, name="turned_vs%d" % b, tag=("scores0", "spare1")[b])
             for t in range(4):
-                nc.tensor.transpose(turned[:, t, :], vs_got[b][:, t:N:4], ident[:])
+                nc.tensor.transpose(turned[:, t, :], vs_got[b][:, (t // 2) * 2 * P + t % 2 : (t // 2 + 1) * 2 * P : 2], ident[:])
             nc.scalar.copy(vs_col[b][:], turned[:, :, 0])
 
         def group_q(b, copy):
             copy(
-                q_bf[b][:].rearrange("p (o q j) -> p o q j", o=PASSES, j=4),
-                q_raw[b][:].rearrange("p o (j q) -> p o q j", j=4),
+                q_bf[b][:].rearrange("p (o c i j) -> p o c j i", o=PASSES, i=4, j=4),
+                q_raw[b][:].rearrange("p o (j c i) -> p o c j i", j=4, i=4),
             )
 
         def quant_q(b):
             nc.vector.quantize_mx(q_codes[b][:].bitcast(FP8X4), q_scales[b][:], q_bf[b][:])
 
 
-        def turn_v(b, h, pairs):
+        def turn_v(b, h):
             for u in range(2):
-                nc.tensor.transpose(turned_v[b][:, h, u, :], pairs[u], ident[:])
+                nc.tensor.transpose(turned_v[b][:, h, u, :], pairs[b, h][u], ident[:])
+
+        def weave_v(b, tag=None):
+            v_in.setdefault(b, sb("v_in%d" % b, [P, HALVES, 4 * P], BF16, tag=tag))
             nc.scalar.copy(
-                v_in[b][:, h, :].bitcast(F32).rearrange("p (e u) -> p e u", u=2),
-                turned_v[b][:, h].rearrange("p u e -> p e u"),
+                v_in[b][:].bitcast(F32).rearrange("p h (e u) -> p h e u", u=2),
+                turned_v[b][:].rearrange("p h u e -> p h e u"),
             )
 
         def cast_v(b, h):
@@ -156,13 +161,13 @@ def tile_attend_sink_seg_kernel(tc, qT, k_words, k_scales, vT, vs, sink, offs, o
             dealt = v_got[b][h][:].rearrange("p (u s j) -> p s u j", u=2, j=2)
             nc.scalar.activation(dealt, listed(v_bf[:, h * SEG :], b), ACT.Copy)
             words = v_got[b][h][:].bitcast(F32)
-            turn_v(b, h, [words[:, u * P : (u + 1) * P] for u in range(2)])
+            pairs.setdefault((b, h), [words[:, u * P : (u + 1) * P] for u in range(2)])
 
         def gather_v_vector(b, h, tag):
             v_got[b][h] = sb("v_got%d%d" % (b, h), [P, N], BF16, tag=tag)
             nc.vector.tensor_copy(v_got[b][h][:], listed(v_raw[b, h][:], b))
             words = v_got[b][h][:].bitcast(F32)
-            turn_v(b, h, [words[:, u : 2 * P : 2] for u in range(2)])
+            pairs.setdefault((b, h), [words[:, u : 2 * P : 2] for u in range(2)])
 
         def quant_v(b, h):
             cols = slice(h * P, (h + 1) * P)
@@ -247,8 +252,8 @@ def tile_attend_sink_seg_kernel(tc, qT, k_words, k_scales, vT, vs, sink, offs, o
         load_kw(0)
         load_q(0)
         load_kw(1)
-        load_q(1)
         load_v(1, 0)
+        load_q(1)
         nc.sync.dma_start(vs_pool[0:1, :], vs[0:1, :])
         gather_ks()
         v_raw.setdefault((1, 1), sb("v_raw11", [P, SEG], F32, tag="early"))
@@ -256,36 +261,43 @@ def tile_attend_sink_seg_kernel(tc, qT, k_words, k_scales, vT, vs, sink, offs, o
         cast_v(0, 0)
         load_v(0, 1)
         gather_v_scalar(0, 0)
-        group_q(0, nc.scalar.copy)
+        turn_v(0, 0)
         negate_sinks()
         gather_kw(0)
-        quant_q(0)
+        group_q(0, nc.scalar.copy)
         part_kw(0)
+        quant_q(0)
         score(0)
-        group_q(1, nc.scalar.copy)
+        cast_v(1, 0)
+        gather_v_scalar(1, 0)
         gather_kw(1)
-        quant_q(1)
+        group_q(1, nc.vector.tensor_copy)
         part_kw(1)
+        quant_q(1)
         score(1)
         row_max(0)
         exponentials(0)
-        row_max(1)
-        exponentials(1)
         gather_vs(0)
         turn_vs(0)
-        cast_v(1, 0)
-        gather_v_scalar(1, 0, "mid0")
+        row_max(1)
+        exponentials(1)
+        turned_v.setdefault(1, psum.tile([P, HALVES, 2, P], F32, name="turned_v1", tag="scores1"))
+        turn_v(1, 0)
         cast_v(1, 1)
         gather_v_scalar(1, 1)
-        gather_v_vector(0, 1, "late1")
+        turn_v(1, 1)
         gather_vs(1, "mid1")
         turn_vs(1)
+        gather_v_vector(0, 1, "late1")
+        turn_v(0, 1)
+        weave_v(0, "cast")
+        weave_v(1)
         weigh(0)
         invert()
+        weigh(1)
         quant_w(0)
         quant_v_whole(0)
         finish(0)
-        weigh(1)
-        quant_v_whole(1)
         quant_w(1)
+        quant_v_whole(1)
         finish(1)

@@ -43,10 +43,10 @@ def tile_attend_sink_seg_kernel(tc, qT, k_words, k_scales, vT, vs, sink, offs, o
             return window[:, 0 : (b + 1) * SEG].indirect(offsets[:, b * COLS : (b + 1) * COLS])
 
         ks_pool = sb("ks_pool", [P, T // 4], I32, tag="early")
-        vs_pool = sb("vs_pool", [P, T], F32)
+        vs_pool = sb("vs_pool", [P, T], F32, tag="scales")
         kw_pool = sb("kw_pool", [P, T], I32)
-        v_raw = {(0, 0): sb("v_raw00", [P, SEG], F32), (1, 0): sb("v_raw10", [P, SEG], F32)}
-        v_raw.setdefault((0, 1), v_raw[0, 0])
+        v_raw = {(0, 0): sb("v_raw00", [P, SEG], F32, tag="stage"), (1, 0): sb("v_raw10", [P, SEG], F32)}
+        v_raw.setdefault((1, 1), v_raw[0, 0])
         v_bf = sb("v_bf", [P, 3 * SEG], BF16, tag="cast")
         q_raw = [sb("q_raw%d" % b, [P, PASSES, 4 * NQ], F32) for b in range(B)]
         sinks = sb("sinks", [P, B], F32)
@@ -85,19 +85,18 @@ def tile_attend_sink_seg_kernel(tc, qT, k_words, k_scales, vT, vs, sink, offs, o
         kw_got = [sb("kw_got%d" % b, [P, N], U32) for b in range(B)]
         k_codes = [sb("k_codes%d" % b, [P, PASSES, 2 * N], U8, tag="mid%d" % b) for b in range(B)]
         vs_got = {}
-        vs_col = [sb("vs_col%d" % b, [P, 4], F32) for b in range(B)]
+        vs_col = [sb("vs_col%d" % b, [P, 8], F32, tag="dealt%d" % b) for b in range(B)]
         q_bf = [sb("q_bf%d" % b, [P, PASSES * NQ * 4], BF16) for b in range(B)]
         q_codes = [sb("q_codes%d" % b, [P, PASSES * NQ], U32, tag="late%d" % b) for b in range(B)]
         q_scales = [sb("q_scales%d" % b, [P, PASSES * NQ], U8) for b in range(B)]
         v_got = [{}, {}]
         v_in = {}
-        v_codes = [sb("v_codes%d" % b, [P, DV], U32) for b in range(B)]
+        v_codes = {}
         v_scales = [sb("v_scales%d" % b, [P, DV], U8) for b in range(B)]
-        neg_m = [sb("neg_m%d" % b, [P, 1], F32) for b in range(B)]
-        probs = [sb("probs%d" % b, [P, N + 8], F32) for b in range(B)]
+        neg_m = {}
+        probs = {}
         total = sb("total", [P, B], F32)
-        r_total = sb("r_total", [P, B], F32)
-        w_bf = [sb("w_bf%d" % b, [P, 4 * NQ], BF16) for b in range(B)]
+        w_bf = [sb("w_bf%d" % b, [P, 4 * NQ], BF16, tag="weights%d" % b) for b in range(B)]
         w_codes = [sb("w_codes%d" % b, [P, NQ], U32) for b in range(B)]
         w_scales = [sb("w_scales%d" % b, [P, NQ], U8) for b in range(B)]
         result = [sb("result%d" % b, [P, DV], F32) for b in range(B)]
@@ -123,14 +122,8 @@ def tile_attend_sink_seg_kernel(tc, qT, k_words, k_scales, vT, vs, sink, offs, o
 
         def gather_vs(b, tag=None):
             vs_got[b] = sb("vs_got%d" % b, [P, N], F32, tag=tag)
-            dealt = vs_got[b][:].bitcast(U32).rearrange("p (u s j) -> p s u j", u=2, j=2)
-            nc.vector.tensor_copy(dealt, listed(vs_pool[:].bitcast(U32), b))
-
-        def turn_vs(b):
-            turned = psum.tile([P, 4, P], F32, name="turned_vs%d" % b, tag=("scores0", "spare1")[b])
-            for t in range(4):
-                nc.tensor.transpose(turned[:, t, :], vs_got[b][:, (t // 2) * 2 * P + t % 2 : (t // 2 + 1) * 2 * P : 2], ident[:])
-            nc.scalar.copy(vs_col[b][:], turned[:, :, 0])
+            nc.vector.tensor_copy(vs_got[b][:], listed(vs_pool[:], b))
+            nc.sync.dma_start(vs_col[b][:, 0:4], vs_got[b][0:1, :])
 
         def group_q(b, copy):
             copy(
@@ -146,11 +139,11 @@ def tile_attend_sink_seg_kernel(tc, qT, k_words, k_scales, vT, vs, sink, offs, o
             for u in range(2):
                 nc.tensor.transpose(turned_v[b][:, h, u, :], pairs[b, h][u], ident[:])
 
-        def weave_v(b, tag=None):
-            v_in.setdefault(b, sb("v_in%d" % b, [P, HALVES, 4 * P], BF16, tag=tag))
-            nc.scalar.copy(
-                v_in[b][:].bitcast(F32).rearrange("p h (e u) -> p h e u", u=2),
-                turned_v[b][:].rearrange("p h u e -> p h e u"),
+        def weave_v(b, first, count, copy, tag=None):
+            v_in.setdefault((b, first), sb("v_in%d%d" % (b, first), [P, count * 4 * P], BF16, tag=tag))
+            copy(
+                v_in[b, first][:].bitcast(F32).rearrange("p (h e u) -> p h e u", h=count, u=2),
+                turned_v[b][:, first : first + count].rearrange("p h u e -> p h e u"),
             )
 
         def cast_v(b, h):
@@ -169,14 +162,10 @@ def tile_attend_sink_seg_kernel(tc, qT, k_words, k_scales, vT, vs, sink, offs, o
             words = v_got[b][h][:].bitcast(F32)
             pairs.setdefault((b, h), [words[:, u : 2 * P : 2] for u in range(2)])
 
-        def quant_v(b, h):
-            cols = slice(h * P, (h + 1) * P)
-            nc.vector.quantize_mx(v_codes[b][:, cols].bitcast(FP8X4), v_scales[b][:, cols], v_in[b][:, h, :])
-
-        def quant_v_whole(b):
-            nc.vector.quantize_mx(
-                v_codes[b][:].bitcast(FP8X4), v_scales[b][:], v_in[b][:].rearrange("p h c -> p (h c)")
-            )
+        def quant_v(b, first, count, tag=None):
+            v_codes.setdefault(b, sb("v_codes%d" % b, [P, DV], U32, tag=tag))
+            cols = slice(first * P, (first + count) * P)
+            nc.vector.quantize_mx(v_codes[b][:, cols].bitcast(FP8X4), v_scales[b][:, cols], v_in[b, first][:])
 
         def score(b):
             for o in range(PASSES):
@@ -194,7 +183,8 @@ def tile_attend_sink_seg_kernel(tc, qT, k_words, k_scales, vT, vs, sink, offs, o
         def negate_sinks():
             nc.gpsimd.tensor_scalar(neg_all[:, :, N], sinks[:], -1.0, 0.0, ALU.mult, ALU.add)
 
-        def row_max(b):
+        def row_max(b, tag=None):
+            neg_m.setdefault(b, sb("neg_m%d" % b, [P, 1], F32, tag=tag))
             nc.vector.tensor_scalar(
                 neg_all[:, b, 0:N].rearrange("p (t s) -> p t s", t=4),
                 scores[b][:].rearrange("p (s t) -> p t s", t=4),
@@ -205,7 +195,8 @@ def tile_attend_sink_seg_kernel(tc, qT, k_words, k_scales, vT, vs, sink, offs, o
                 accum_out=neg_m[b][:],
             )
 
-        def exponentials(b):
+        def exponentials(b, tag=None):
+            probs.setdefault(b, sb("probs%d" % b, [P, N + 8], F32, tag=tag))
             nc.scalar.activation(
                 probs[b][:, 0 : N + 1],
                 neg_all[:, b, 0 : N + 1],
@@ -221,14 +212,14 @@ def tile_attend_sink_seg_kernel(tc, qT, k_words, k_scales, vT, vs, sink, offs, o
             nc.vector.tensor_tensor(
                 w_bf[b][:].rearrange("p (q t) -> p q t", t=4),
                 turned_p[b][:].rearrange("p t q -> p q t"),
-                vs_col[b][:].unsqueeze(1).to_broadcast([P, NQ, 4]),
+                vs_col[b][:, 0:4].unsqueeze(1).to_broadcast([P, NQ, 4]),
                 ALU.mult,
             )
 
         def quant_w(b):
             nc.vector.quantize_mx(w_codes[b][:].bitcast(FP8X4), w_scales[b][:], w_bf[b][:])
 
-        def finish(b):
+        def finish(b, r_total):
             sums = psum.tile([P, 4, P], F32, name="sums%d" % b, tag="spare%d" % b)
             y = sums[:].rearrange("p a c -> p (a c)")[:, 0:DV]
             nc.tensor.matmul_mx(
@@ -244,7 +235,9 @@ def tile_attend_sink_seg_kernel(tc, qT, k_words, k_scales, vT, vs, sink, offs, o
             nc.sync.dma_start(out[b], result[b][:])
 
         def invert():
+            r_total = sb("r_total", [P, B], F32, tag="weights0")
             nc.vector.reciprocal(r_total[:], total[:])
+            return r_total
 
         load_key_scales()
         load_sinks(slice(0, P), nc.gpsimd)
@@ -256,12 +249,13 @@ def tile_attend_sink_seg_kernel(tc, qT, k_words, k_scales, vT, vs, sink, offs, o
         load_q(1)
         nc.sync.dma_start(vs_pool[0:1, :], vs[0:1, :])
         gather_ks()
-        v_raw.setdefault((1, 1), sb("v_raw11", [P, SEG], F32, tag="early"))
-        load_v(1, 1)
         cast_v(0, 0)
+        load_v(1, 1)
+        v_raw.setdefault((0, 1), sb("v_raw01", [P, SEG], F32, tag="early"))
         load_v(0, 1)
         gather_v_scalar(0, 0)
         turn_v(0, 0)
+        weave_v(0, 0, 1, nc.scalar.copy)
         negate_sinks()
         gather_kw(0)
         group_q(0, nc.scalar.copy)
@@ -275,29 +269,28 @@ def tile_attend_sink_seg_kernel(tc, qT, k_words, k_scales, vT, vs, sink, offs, o
         part_kw(1)
         quant_q(1)
         score(1)
-        row_max(0)
-        exponentials(0)
         gather_vs(0)
-        turn_vs(0)
-        row_max(1)
-        exponentials(1)
-        turned_v.setdefault(1, psum.tile([P, HALVES, 2, P], F32, name="turned_v1", tag="scores1"))
-        turn_v(1, 0)
+        row_max(0, "column0")
         cast_v(1, 1)
-        gather_v_scalar(1, 1)
+        exponentials(0, "stage")
+        gather_vs(1, "late0")
+        row_max(1, "scales")
+        gather_v_scalar(1, 1, "column0")
+        exponentials(1, "cast")
+        turned_v.setdefault(1, psum.tile([P, HALVES, 2, P], F32, name="turned_v1", tag="scores0"))
+        turn_v(1, 0)
         turn_v(1, 1)
-        gather_vs(1, "mid1")
-        turn_vs(1)
-        gather_v_vector(0, 1, "late1")
+        gather_v_vector(0, 1, "stage")
         turn_v(0, 1)
-        weave_v(0, "cast")
-        weave_v(1)
+        quant_v(0, 0, 1)
+        weave_v(1, 0, 2, nc.scalar.copy)
         weigh(0)
-        invert()
-        weigh(1)
         quant_w(0)
-        quant_v_whole(0)
-        finish(0)
+        weigh(1)
+        r_total = invert()
+        quant_v(1, 0, 2, "dealt0")
         quant_w(1)
-        quant_v_whole(1)
-        finish(1)
+        finish(1, r_total)
+        weave_v(0, 1, 1, nc.scalar.copy, "dealt1")
+        quant_v(0, 1, 1)
+        finish(0, r_total)

@@ -51,13 +51,10 @@ def tile_attend_sink_seg_kernel(tc, qT, k_words, k_scales, vT, vs, sink, offs, o
         q_raw = [sb("q_raw%d" % b, [P, PASSES, 4 * NQ], F32) for b in range(B)]
         sinks = sb("sinks", [P, B], F32)
         ident = sb("ident", [P, P], F32)
-        warm = sb("warm", [P, 2], F32)
         neg_all = sb("neg_all", [P, B, N + 8], F32)
         k_planes = sb("k_planes", [P, PASSES * B * N // 4], I32)
 
         nc.gpsimd.memset(ks_pool[0:96, :], 0)
-        nc.vector.memset(warm[:, 0:1], 0.0)
-        nc.scalar.activation(warm[:, 1:2], warm[:, 0:1], ACT.Exp)
         nc.vector.memset(vs_pool[:], 0.0)
         make_identity(nc, ident[:])
         nc.gpsimd.memset(k_planes[:], 0)

@@ -28,10 +28,14 @@ def tile_attend_sink_seg_kernel(tc, qT, k_words, k_scales, vT, vs, sink, offs, o
     nc = tc.nc
     with ExitStack() as ctx:
         keep = ctx.enter_context(tc.tile_pool(name="keep", bufs=1))
+        lent = ctx.enter_context(tc.tile_pool(name="lent", bufs=1))
         psum = ctx.enter_context(tc.psum_pool(name="psum", bufs=1))
 
         def sb(name, shape, dtype, tag=None):
             return keep.tile(shape, dtype, name=name, tag=tag or name, align_bytes=64)
+
+        def placed(name, shape, dtype, offset):
+            return lent.tile(shape, dtype, name=name, tag=name, align_bytes=64, offset=offset)
 
         offsets = keep.tile([P, B * COLS], U16, name="offsets")
         nc.sync.dma_start(offsets[:], offs)
@@ -45,10 +49,9 @@ def tile_attend_sink_seg_kernel(tc, qT, k_words, k_scales, vT, vs, sink, offs, o
         ks_pool = sb("ks_pool", [P, T // 4], I32, tag="early")
         vs_pool = sb("vs_pool", [P, T], F32, tag="scales")
         kw_pool = sb("kw_pool", [P, T], I32)
-        v_raw = {(0, 0): sb("v_raw00", [P, SEG], F32, tag="stage"), (1, 0): sb("v_raw10", [P, SEG], F32)}
-        v_raw.setdefault((1, 1), v_raw[0, 0])
-        v_bf = sb("v_bf", [P, 3 * SEG], BF16, tag="cast")
-        q_raw = [sb("q_raw%d" % b, [P, PASSES, 4 * NQ], F32) for b in range(B)]
+        v_raw = {(0, 0): placed("v_raw00", [P, SEG], F32, 0)}
+        v_bf = sb("v_bf", [P, T], BF16)
+        q_raw = [sb("q_raw%d" % b, [P, PASSES, 4 * NQ], F32, tag="query%d" % b) for b in range(B)]
         sinks = sb("sinks", [P, B], F32)
         ident = sb("ident", [P, P], F32)
         neg_all = sb("neg_all", [P, B, N + 8], F32)
@@ -79,11 +82,11 @@ def tile_attend_sink_seg_kernel(tc, qT, k_words, k_scales, vT, vs, sink, offs, o
             nc.sync.dma_start(ks_pool[96:P, :], ks_hbm.rearrange("o f t -> f o t"))
 
         ks_got = sb("ks_got", [P, B * N], U8)
-        kw_got = [sb("kw_got%d" % b, [P, N], U32) for b in range(B)]
+        kw_got = {0: sb("kw_got0", [P, N], U32, tag="words0"), 1: placed("kw_got1", [P, N], U32, 2048)}
         k_codes = [sb("k_codes%d" % b, [P, PASSES, 2 * N], U8, tag="mid%d" % b) for b in range(B)]
         vs_got = {}
         vs_col = [sb("vs_col%d" % b, [P, 8], F32, tag="dealt%d" % b) for b in range(B)]
-        q_bf = [sb("q_bf%d" % b, [P, PASSES * NQ * 4], BF16) for b in range(B)]
+        q_bf = {0: placed("q_bf0", [P, PASSES * NQ * 4], BF16, 0)}
         q_codes = [sb("q_codes%d" % b, [P, PASSES * NQ], U32, tag="late%d" % b) for b in range(B)]
         q_scales = [sb("q_scales%d" % b, [P, PASSES * NQ], U8) for b in range(B)]
         v_got = [{}, {}]
@@ -96,12 +99,11 @@ def tile_attend_sink_seg_kernel(tc, qT, k_words, k_scales, vT, vs, sink, offs, o
         w_bf = [sb("w_bf%d" % b, [P, 4 * NQ], BF16, tag="weights%d" % b) for b in range(B)]
         w_codes = [sb("w_codes%d" % b, [P, NQ], U32) for b in range(B)]
         w_scales = [sb("w_scales%d" % b, [P, NQ], U8) for b in range(B)]
-        result = [sb("result%d" % b, [P, DV], F32) for b in range(B)]
 
         scores = [psum.tile([P, N], F32, name="scores%d" % b, tag="scores%d" % b) for b in range(B)]
-        turned_v = {0: psum.tile([P, HALVES, 2, P], F32, name="turned_v0")}
+        turned_v = {}
         pairs = {}
-        turned_p = [psum.tile([P, 4, NQ], F32, name="turned_p%d" % b) for b in range(B)]
+        turned_p = [psum.tile([P, 4, NQ], F32, name="turned_p%d" % b, tag="turned_p%d" % b) for b in range(B)]
 
         def gather_ks():
             nc.vector.tensor_copy(ks_got[:], ks_pool[:].bitcast(U8).indirect(offsets[:]))
@@ -132,37 +134,39 @@ def tile_attend_sink_seg_kernel(tc, qT, k_words, k_scales, vT, vs, sink, offs, o
             nc.vector.quantize_mx(q_codes[b][:].bitcast(FP8X4), q_scales[b][:], q_bf[b][:])
 
 
-        def turn_v(b, h):
+        def turn_v(b, h, bank=None):
+            name = "turned_v%d%d" % (b, h)
+            turned_v.setdefault((b, h), psum.tile([P, 2, P], F32, name=name, tag=bank or name))
             for u in range(2):
-                nc.tensor.transpose(turned_v[b][:, h, u, :], pairs[b, h][u], ident[:])
+                nc.tensor.transpose(turned_v[b, h][:, u, :], pairs[b, h][u], ident[:])
 
-        def weave_v(b, first, count, copy, tag=None):
-            v_in.setdefault((b, first), sb("v_in%d%d" % (b, first), [P, count * 4 * P], BF16, tag=tag))
-            copy(
-                v_in[b, first][:].bitcast(F32).rearrange("p (h e u) -> p h e u", h=count, u=2),
-                turned_v[b][:, first : first + count].rearrange("p h u e -> p h e u"),
+        def weave_v(b, h):
+            v_in.setdefault((b, h), sb("v_in%d%d" % (b, h), [P, 4 * P], BF16))
+            nc.scalar.copy(
+                v_in[b, h][:].bitcast(F32).rearrange("p (e u) -> p e u", u=2),
+                turned_v[b, h][:].rearrange("p u e -> p e u"),
             )
 
         def cast_v(b, h):
-            nc.scalar.activation(v_bf[:, seg(b + h)], v_raw[b, h][:], ACT.Copy)
+            nc.scalar.activation(v_bf[:, seg(b)], v_raw[b, h][:], ACT.Copy)
 
         def gather_v_scalar(b, h, tag=None):
             v_got[b][h] = sb("v_got%d%d" % (b, h), [P, N], BF16, tag=tag)
             dealt = v_got[b][h][:].rearrange("p (u s j) -> p s u j", u=2, j=2)
-            nc.scalar.activation(dealt, listed(v_bf[:, h * SEG :], b), ACT.Copy)
+            nc.scalar.activation(dealt, listed(v_bf[:], b), ACT.Copy)
             words = v_got[b][h][:].bitcast(F32)
             pairs.setdefault((b, h), [words[:, u * P : (u + 1) * P] for u in range(2)])
 
-        def gather_v_vector(b, h, tag):
+        def gather_v_vector(b, h, tag=None):
             v_got[b][h] = sb("v_got%d%d" % (b, h), [P, N], BF16, tag=tag)
             nc.vector.tensor_copy(v_got[b][h][:], listed(v_raw[b, h][:], b))
             words = v_got[b][h][:].bitcast(F32)
             pairs.setdefault((b, h), [words[:, u : 2 * P : 2] for u in range(2)])
 
-        def quant_v(b, first, count, tag=None):
+        def quant_v(b, h, tag=None):
             v_codes.setdefault(b, sb("v_codes%d" % b, [P, DV], U32, tag=tag))
-            cols = slice(first * P, (first + count) * P)
-            nc.vector.quantize_mx(v_codes[b][:, cols].bitcast(FP8X4), v_scales[b][:, cols], v_in[b, first][:])
+            cols = slice(h * P, (h + 1) * P)
+            nc.vector.quantize_mx(v_codes[b][:, cols].bitcast(FP8X4), v_scales[b][:, cols], v_in[b, h][:])
 
         def score(b):
             for o in range(PASSES):
@@ -216,23 +220,24 @@ def tile_attend_sink_seg_kernel(tc, qT, k_words, k_scales, vT, vs, sink, offs, o
         def quant_w(b):
             nc.vector.quantize_mx(w_codes[b][:].bitcast(FP8X4), w_scales[b][:], w_bf[b][:])
 
-        def finish(b, r_total):
-            sums = psum.tile([P, 4, P], F32, name="sums%d" % b, tag="spare%d" % b)
-            y = sums[:].rearrange("p a c -> p (a c)")[:, 0:DV]
+        def finish(b, first, count, r_total, bank):
+            cols = slice(first * P, (first + count) * P)
+            sums = psum.tile([P, count * P], F32, name="sums%d%d" % (b, first), tag=bank)
+            result = sb("result%d%d" % (b, first), [P, count * P], F32)
             nc.tensor.matmul_mx(
-                y,
+                sums[:],
                 lhsT=w_codes[b][:].bitcast(FP8X4),
                 lhsT_scale=w_scales[b][:],
-                rhs=v_codes[b][:].bitcast(FP8X4),
-                rhs_scale=v_scales[b][:],
+                rhs=v_codes[b][:, cols].bitcast(FP8X4),
+                rhs_scale=v_scales[b][:, cols],
                 start=True,
                 stop=True,
             )
-            nc.scalar.activation(result[b][:], y, ACT.Copy, scale=r_total[:, b : b + 1])
-            nc.sync.dma_start(out[b], result[b][:])
+            nc.scalar.activation(result[:], sums[:], ACT.Copy, scale=r_total[:, b : b + 1])
+            nc.sync.dma_start(out[b][:, cols], result[:])
 
         def invert():
-            r_total = sb("r_total", [P, B], F32, tag="weights0")
+            r_total = sb("r_total", [P, B], F32)
             nc.vector.reciprocal(r_total[:], total[:])
             return r_total
 
@@ -242,52 +247,57 @@ def tile_attend_sink_seg_kernel(tc, qT, k_words, k_scales, vT, vs, sink, offs, o
         load_kw(0)
         load_q(0)
         load_kw(1)
-        load_v(1, 0)
         load_q(1)
         nc.sync.dma_start(vs_pool[0:1, :], vs[0:1, :])
         gather_ks()
+        v_raw.setdefault((1, 0), sb("v_raw10", [P, SEG], F32, tag="early"))
+        load_v(1, 0)
         cast_v(0, 0)
-        load_v(1, 1)
-        v_raw.setdefault((0, 1), sb("v_raw01", [P, SEG], F32, tag="early"))
-        load_v(0, 1)
         gather_v_scalar(0, 0)
         turn_v(0, 0)
-        weave_v(0, 0, 1, nc.scalar.copy)
         negate_sinks()
         gather_kw(0)
-        group_q(0, nc.scalar.copy)
         part_kw(0)
+        v_raw.setdefault((1, 1), sb("v_raw11", [P, SEG], F32, tag="words0"))
+        load_v(1, 1)
+        group_q(0, nc.scalar.copy)
+        weave_v(0, 0)
+        gather_kw(1)
         quant_q(0)
         score(0)
-        cast_v(1, 0)
-        gather_v_scalar(1, 0)
-        gather_kw(1)
-        group_q(1, nc.vector.tensor_copy)
         part_kw(1)
+        v_raw.setdefault((0, 1), placed("v_raw01", [P, SEG], F32, 0))
+        load_v(0, 1)
+        q_bf.setdefault(1, sb("q_bf1", [P, PASSES * NQ * 4], BF16, tag="query0"))
+        group_q(1, nc.scalar.copy)
+        quant_v(0, 0)
         quant_q(1)
         score(1)
-        gather_vs(0)
-        row_max(0, "column0")
+        cast_v(1, 0)
+        gather_vs(0, "query1")
+        row_max(0)
+        gather_v_scalar(1, 0)
+        exponentials(0, "early")
         cast_v(1, 1)
-        exponentials(0, "stage")
-        gather_vs(1, "late0")
-        row_max(1, "scales")
-        gather_v_scalar(1, 1, "column0")
-        exponentials(1, "cast")
-        turned_v.setdefault(1, psum.tile([P, HALVES, 2, P], F32, name="turned_v1", tag="scores0"))
+        gather_vs(1, "late1")
+        row_max(1)
         turn_v(1, 0)
-        turn_v(1, 1)
-        gather_v_vector(0, 1, "stage")
-        turn_v(0, 1)
-        quant_v(0, 0, 1)
-        weave_v(1, 0, 2, nc.scalar.copy)
+        exponentials(1, "words0")
+        gather_v_scalar(1, 1)
+        gather_v_vector(0, 1, "mid1")
         weigh(0)
+        turn_v(0, 1, "turned_p0")
+        turn_v(1, 1)
+        weave_v(1, 0)
+        weave_v(0, 1)
+        weave_v(1, 1)
         quant_w(0)
-        weigh(1)
         r_total = invert()
-        quant_v(1, 0, 2, "dealt0")
+        weigh(1)
         quant_w(1)
-        finish(1, r_total)
-        weave_v(0, 1, 1, nc.scalar.copy, "dealt1")
-        quant_v(0, 1, 1)
-        finish(0, r_total)
+        quant_v(1, 0)
+        quant_v(0, 1)
+        quant_v(1, 1)
+        finish(1, 0, 1, r_total, "scores1")
+        finish(0, 0, 2, r_total, "scores0")
+        finish(1, 1, 1, r_total, "turned_v00")

@@ -107,6 +107,8 @@ def tile_attend_sink_seg_kernel(tc, qT, k_words, k_scales, vT, vs, sink, offs, o
 
         def gather_ks():
             nc.vector.tensor_copy(ks_got[:], ks_pool[:].bitcast(U8).indirect(offsets[:]))
+
+        def move_ks():
             for quad in range(4):
                 rows = ks_got[:].bitcast(I32)[96 + 8 * quad : 104 + 8 * quad, :]
                 nc.sync.dma_start(k_planes[32 * quad : 32 * quad + 4, :], rows)
@@ -140,8 +142,8 @@ def tile_attend_sink_seg_kernel(tc, qT, k_words, k_scales, vT, vs, sink, offs, o
             for u in range(2):
                 nc.tensor.transpose(turned_v[b, h][:, u, :], pairs[b, h][u], ident[:])
 
-        def weave_v(b, h):
-            v_in.setdefault((b, h), sb("v_in%d%d" % (b, h), [P, 4 * P], BF16))
+        def weave_v(b, h, tag=None):
+            v_in.setdefault((b, h), sb("v_in%d%d" % (b, h), [P, 4 * P], BF16, tag=tag))
             nc.scalar.copy(
                 v_in[b, h][:].bitcast(F32).rearrange("p (e u) -> p e u", u=2),
                 turned_v[b, h][:].rearrange("p u e -> p e u"),
@@ -252,6 +254,7 @@ def tile_attend_sink_seg_kernel(tc, qT, k_words, k_scales, vT, vs, sink, offs, o
         gather_ks()
         v_raw.setdefault((1, 0), sb("v_raw10", [P, SEG], F32, tag="early"))
         load_v(1, 0)
+        move_ks()
         cast_v(0, 0)
         gather_v_scalar(0, 0)
         turn_v(0, 0)
@@ -275,29 +278,29 @@ def tile_attend_sink_seg_kernel(tc, qT, k_words, k_scales, vT, vs, sink, offs, o
         score(1)
         cast_v(1, 0)
         gather_vs(0, "query1")
-        row_max(0)
+        row_max(0, "column0")
         gather_v_scalar(1, 0)
         exponentials(0, "early")
         cast_v(1, 1)
         gather_vs(1, "late1")
-        row_max(1)
-        turn_v(1, 0)
+        row_max(1, "column1")
+        turn_v(1, 0, "scores1")
         exponentials(1, "words0")
         gather_v_scalar(1, 1)
-        gather_v_vector(0, 1, "mid1")
+        gather_v_vector(0, 1, "column0")
         weigh(0)
-        turn_v(0, 1, "turned_p0")
-        turn_v(1, 1)
         weave_v(1, 0)
-        weave_v(0, 1)
+        turn_v(0, 1)
+        turn_v(1, 1)
+        weave_v(0, 1, "column1")
         weave_v(1, 1)
         quant_w(0)
         r_total = invert()
         weigh(1)
         quant_w(1)
-        quant_v(1, 0)
+        quant_v(1, 0, "dealt1")
         quant_v(0, 1)
         quant_v(1, 1)
-        finish(1, 0, 1, r_total, "scores1")
+        finish(1, 0, 1, r_total, "turned_p0")
         finish(0, 0, 2, r_total, "scores0")
         finish(1, 1, 1, r_total, "turned_v00")

@@ -244,12 +244,12 @@ def tile_attend_sink_seg_kernel(tc, qT, k_words, k_scales, vT, vs, sink, offs, o
             return r_total
 
         load_key_scales()
-        load_sinks(slice(0, P), nc.gpsimd)
         load_v(0, 0)
         load_kw(0)
         load_q(0)
         load_kw(1)
         load_q(1)
+        load_sinks(slice(0, P), nc.sync)
         nc.sync.dma_start(vs_pool[0:1, :], vs[0:1, :])
         gather_ks()
         v_raw.setdefault((1, 0), sb("v_raw10", [P, SEG], F32, tag="early"))
@@ -273,7 +273,6 @@ def tile_attend_sink_seg_kernel(tc, qT, k_words, k_scales, vT, vs, sink, offs, o
         load_v(0, 1)
         q_bf.setdefault(1, sb("q_bf1", [P, PASSES * NQ * 4], BF16, tag="query0"))
         group_q(1, nc.scalar.copy)
-        quant_v(0, 0)
         quant_q(1)
         score(1)
         cast_v(1, 0)
@@ -289,18 +288,19 @@ def tile_attend_sink_seg_kernel(tc, qT, k_words, k_scales, vT, vs, sink, offs, o
         gather_v_scalar(1, 1)
         gather_v_vector(0, 1, "column0")
         weigh(0)
-        weave_v(1, 0)
+        quant_v(0, 0, "early")
         turn_v(0, 1)
         turn_v(1, 1)
         weave_v(0, 1, "column1")
+        weave_v(1, 0)
         weave_v(1, 1)
         quant_w(0)
         r_total = invert()
         weigh(1)
+        quant_v(0, 1)
         quant_w(1)
         quant_v(1, 0, "dealt1")
-        quant_v(0, 1)
         quant_v(1, 1)
-        finish(1, 0, 1, r_total, "turned_p0")
         finish(0, 0, 2, r_total, "scores0")
+        finish(1, 0, 1, r_total, "turned_p0")
         finish(1, 1, 1, r_total, "turned_v00")

@@ -38,7 +38,6 @@ def tile_attend_sink_seg_kernel(tc, qT, k_words, k_scales, vT, vs, sink, offs, o
             return lent.tile(shape, dtype, name=name, tag=name, align_bytes=64, offset=offset)
 
         offsets = keep.tile([P, B * COLS], U16, name="offsets")
-        nc.sync.dma_start(offsets[:], offs)
 
         def seg(b):
             return slice(b * SEG, (b + 1) * SEG)
@@ -50,8 +49,8 @@ def tile_attend_sink_seg_kernel(tc, qT, k_words, k_scales, vT, vs, sink, offs, o
         vs_pool = sb("vs_pool", [P, T], F32, tag="scales")
         kw_pool = sb("kw_pool", [P, T], I32)
         v_raw = {(0, 0): placed("v_raw00", [P, SEG], F32, 0)}
-        v_bf = sb("v_bf", [P, T], BF16)
-        q_raw = [sb("q_raw%d" % b, [P, PASSES, 4 * NQ], F32, tag="query%d" % b) for b in range(B)]
+        v_bf = sb("v_bf", [P, 3 * SEG], BF16)
+        q_raw = [sb("q_raw0", [P, PASSES, 4 * NQ], F32, tag="query0"), placed("q_raw1", [P, PASSES, 4 * NQ], F32, 4096)]
         sinks = sb("sinks", [P, B], F32)
         ident = sb("ident", [P, P], F32)
         neg_all = sb("neg_all", [P, B, N + 8], F32)
@@ -121,8 +120,8 @@ def tile_attend_sink_seg_kernel(tc, qT, k_words, k_scales, vT, vs, sink, offs, o
                 k_codes[b][:].bitcast(U16), kw_got[b][:].bitcast(U16).rearrange("p (s o) -> p o s", o=PASSES)
             )
 
-        def gather_vs(b, tag=None):
-            vs_got[b] = sb("vs_got%d" % b, [P, N], F32, tag=tag)
+        def gather_vs(b):
+            vs_got.setdefault(b, placed("vs_got%d" % b, [P, N], F32, 4096 + b * 2048))
             nc.vector.tensor_copy(vs_got[b][:], listed(vs_pool[:], b))
             nc.sync.dma_start(vs_col[b][:, 0:4], vs_got[b][0:1, :])
 
@@ -150,12 +149,12 @@ def tile_attend_sink_seg_kernel(tc, qT, k_words, k_scales, vT, vs, sink, offs, o
             )
 
         def cast_v(b, h):
-            nc.scalar.activation(v_bf[:, seg(b)], v_raw[b, h][:], ACT.Copy)
+            nc.scalar.activation(v_bf[:, seg(b + h)], v_raw[b, h][:], ACT.Copy)
 
         def gather_v_scalar(b, h, tag=None):
             v_got[b][h] = sb("v_got%d%d" % (b, h), [P, N], BF16, tag=tag)
             dealt = v_got[b][h][:].rearrange("p (u s j) -> p s u j", u=2, j=2)
-            nc.scalar.activation(dealt, listed(v_bf[:], b), ACT.Copy)
+            nc.scalar.activation(dealt, listed(v_bf[:, h * SEG :], b), ACT.Copy)
             words = v_got[b][h][:].bitcast(F32)
             pairs.setdefault((b, h), [words[:, u * P : (u + 1) * P] for u in range(2)])
 
@@ -184,7 +183,7 @@ def tile_attend_sink_seg_kernel(tc, qT, k_words, k_scales, vT, vs, sink, offs, o
                 )
 
         def negate_sinks():
-            nc.gpsimd.tensor_scalar(neg_all[:, :, N], sinks[:], -1.0, 0.0, ALU.mult, ALU.add)
+            nc.scalar.activation(neg_all[:, :, N], sinks[:], ACT.Copy, scale=-1.0)
 
         def row_max(b, tag=None):
             neg_m.setdefault(b, sb("neg_m%d" % b, [P, 1], F32, tag=tag))
@@ -244,6 +243,7 @@ def tile_attend_sink_seg_kernel(tc, qT, k_words, k_scales, vT, vs, sink, offs, o
             return r_total
 
         load_key_scales()
+        nc.sync.dma_start(offsets[:], offs)
         load_v(0, 0)
         load_kw(0)
         load_q(0)
@@ -258,7 +258,6 @@ def tile_attend_sink_seg_kernel(tc, qT, k_words, k_scales, vT, vs, sink, offs, o
         cast_v(0, 0)
         gather_v_scalar(0, 0)
         turn_v(0, 0)
-        negate_sinks()
         gather_kw(0)
         part_kw(0)
         v_raw.setdefault((1, 1), sb("v_raw11", [P, SEG], F32, tag="words0"))
@@ -273,15 +272,16 @@ def tile_attend_sink_seg_kernel(tc, qT, k_words, k_scales, vT, vs, sink, offs, o
         load_v(0, 1)
         q_bf.setdefault(1, sb("q_bf1", [P, PASSES * NQ * 4], BF16, tag="query0"))
         group_q(1, nc.scalar.copy)
+        negate_sinks()
         quant_q(1)
         score(1)
         cast_v(1, 0)
-        gather_vs(0, "query1")
-        row_max(0, "column0")
-        gather_v_scalar(1, 0)
-        exponentials(0, "early")
         cast_v(1, 1)
-        gather_vs(1, "late1")
+        gather_v_scalar(1, 0)
+        gather_vs(0)
+        gather_vs(1)
+        row_max(0, "column0")
+        exponentials(0, "early")
         row_max(1, "column1")
         turn_v(1, 0, "scores1")
         exponentials(1, "words0")

@@ -18,10 +18,14 @@ ALU = mybir.AluOpType
 ACT = mybir.ActivationFunctionType
 
 P = 128
+PACK = 4
+QUAD = 32
 SEG = T // B
-PASSES = D // 512
-HALVES = DV // P
+PASSES = D // (P * PACK)
 COLS = N // 16
+SCALE_ROWS = P - QUAD
+PADDED = N + 8
+STAGE = 4 * SEG
 
 
 def tile_attend_sink_seg_kernel(tc, qT, k_words, k_scales, vT, vs, sink, offs, out):
@@ -37,26 +41,32 @@ def tile_attend_sink_seg_kernel(tc, qT, k_words, k_scales, vT, vs, sink, offs, o
         def placed(name, shape, dtype, offset):
             return lent.tile(shape, dtype, name=name, tag=name, align_bytes=64, offset=offset)
 
+        def bank(name, shape, tag=None):
+            return psum.tile(shape, F32, name=name, tag=tag or name)
+
         offsets = keep.tile([P, B * COLS], U16, name="offsets")
 
-        def seg(b):
-            return slice(b * SEG, (b + 1) * SEG)
+        def seg(i):
+            return slice(i * SEG, (i + 1) * SEG)
 
         def listed(window, b):
             return window[:, 0 : (b + 1) * SEG].indirect(offsets[:, b * COLS : (b + 1) * COLS])
 
-        ks_pool = sb("ks_pool", [P, T // 4], I32, tag="early")
-        vs_pool = sb("vs_pool", [P, T], F32, tag="scales")
+        ks_pool = sb("ks_pool", [P, T // 4], I32, tag="after_ks_pool")
+        vs_pool = sb("vs_pool", [P, T], F32)
         kw_pool = sb("kw_pool", [P, T], I32)
         v_raw = {(0, 0): placed("v_raw00", [P, SEG], F32, 0)}
         v_bf = sb("v_bf", [P, 3 * SEG], BF16)
-        q_raw = [sb("q_raw0", [P, PASSES, 4 * NQ], F32, tag="query0"), placed("q_raw1", [P, PASSES, 4 * NQ], F32, 4096)]
+        q_raw = [
+            sb("q_raw0", [P, PASSES, PACK * NQ], F32, tag="after_q_raw0"),
+            placed("q_raw1", [P, PASSES, PACK * NQ], F32, STAGE),
+        ]
         sinks = sb("sinks", [P, B], F32)
         ident = sb("ident", [P, P], F32)
-        neg_all = sb("neg_all", [P, B, N + 8], F32)
+        neg_all = sb("neg_all", [P, B, PADDED], F32)
         k_planes = sb("k_planes", [P, PASSES * B * N // 4], I32)
 
-        nc.gpsimd.memset(ks_pool[0:96, :], 0)
+        nc.gpsimd.memset(ks_pool[0:SCALE_ROWS, :], 0)
         nc.vector.memset(vs_pool[:], 0.0)
         make_identity(nc, ident[:])
         nc.gpsimd.memset(k_planes[:], 0)
@@ -64,53 +74,45 @@ def tile_attend_sink_seg_kernel(tc, qT, k_words, k_scales, vT, vs, sink, offs, o
         kw_hbm = k_words[0].rearrange("p t c -> p (t c)").bitcast(I32)
         ks_hbm = k_scales.bitcast(I32)
 
+        ks_got = sb("ks_got", [P, B * N], U8)
+        kw_got = [sb("kw_got0", [P, N], U32, tag="after_kw_got0"), placed("kw_got1", [P, N], U32, STAGE // 2)]
+        k_codes = [sb("k_codes%d" % b, [P, PASSES, 2 * N], U8) for b in range(B)]
+        vs_col = [sb("vs_col%d" % b, [P, 8], F32, tag="after_vs_col%d" % b) for b in range(B)]
+        q_bf = {0: placed("q_bf0", [P, PASSES * NQ * PACK], BF16, 0)}
+        q_codes = [sb("q_codes%d" % b, [P, PASSES * NQ], U32) for b in range(B)]
+        q_scales = [sb("q_scales%d" % b, [P, PASSES * NQ], U8) for b in range(B)]
+        v_scales = [sb("v_scales%d" % b, [P, DV], U8) for b in range(B)]
+        total = sb("total", [P, B], F32)
+        w_bf = [sb("w_bf%d" % b, [P, PACK * NQ], BF16) for b in range(B)]
+        w_codes = [sb("w_codes%d" % b, [P, NQ], U32) for b in range(B)]
+        w_scales = [sb("w_scales%d" % b, [P, NQ], U8) for b in range(B)]
+        scores = [bank("scores%d" % b, [P, N]) for b in range(B)]
+        turned_p = [bank("turned_p%d" % b, [P, PACK, NQ]) for b in range(B)]
+        v_words, turned_v, v_in, v_codes, neg_m = {}, {}, {}, {}, {}
+
+        def load_key_scales():
+            nc.sync.dma_start(ks_pool[SCALE_ROWS:P, :], ks_hbm.rearrange("o f t -> f o t"))
+
         def load_kw(b):
             nc.sync.dma_start(kw_pool[:, seg(b)], kw_hbm[:, seg(b)])
 
         def load_q(b):
-            nc.sync.dma_start(q_raw[b][:], qT[b].rearrange("(o p j) q -> p o (j q)", o=PASSES, j=4))
+            nc.sync.dma_start(q_raw[b][:], qT[b].rearrange("(o p j) q -> p o (j q)", o=PASSES, j=PACK))
 
         def load_v(b, h):
             nc.sync.dma_start(v_raw[b, h][:], vT[h * P : (h + 1) * P, seg(b)])
 
-        def load_sinks(rows, queue):
-            with nc.allow_non_contiguous_dma(reason="one sink a partition"):
-                queue.dma_start(sinks[rows, :], sink[:, rows, 0].rearrange("b q -> q b"))
-
-        def load_key_scales():
-            nc.sync.dma_start(ks_pool[96:P, :], ks_hbm.rearrange("o f t -> f o t"))
-
-        ks_got = sb("ks_got", [P, B * N], U8)
-        kw_got = {0: sb("kw_got0", [P, N], U32, tag="words0"), 1: placed("kw_got1", [P, N], U32, 2048)}
-        k_codes = [sb("k_codes%d" % b, [P, PASSES, 2 * N], U8, tag="mid%d" % b) for b in range(B)]
-        vs_got = {}
-        vs_col = [sb("vs_col%d" % b, [P, 8], F32, tag="dealt%d" % b) for b in range(B)]
-        q_bf = {0: placed("q_bf0", [P, PASSES * NQ * 4], BF16, 0)}
-        q_codes = [sb("q_codes%d" % b, [P, PASSES * NQ], U32, tag="late%d" % b) for b in range(B)]
-        q_scales = [sb("q_scales%d" % b, [P, PASSES * NQ], U8) for b in range(B)]
-        v_got = [{}, {}]
-        v_in = {}
-        v_codes = {}
-        v_scales = [sb("v_scales%d" % b, [P, DV], U8) for b in range(B)]
-        neg_m = {}
-        probs = {}
-        total = sb("total", [P, B], F32)
-        w_bf = [sb("w_bf%d" % b, [P, 4 * NQ], BF16, tag="weights%d" % b) for b in range(B)]
-        w_codes = [sb("w_codes%d" % b, [P, NQ], U32) for b in range(B)]
-        w_scales = [sb("w_scales%d" % b, [P, NQ], U8) for b in range(B)]
-
-        scores = [psum.tile([P, N], F32, name="scores%d" % b, tag="scores%d" % b) for b in range(B)]
-        turned_v = {}
-        pairs = {}
-        turned_p = [psum.tile([P, 4, NQ], F32, name="turned_p%d" % b, tag="turned_p%d" % b) for b in range(B)]
+        def load_sinks():
+            with nc.allow_non_contiguous_dma(reason="one sink a partition and sequence"):
+                nc.sync.dma_start(sinks[0:P, :], sink[:, 0:P, 0].rearrange("b q -> q b"))
 
         def gather_ks():
             nc.vector.tensor_copy(ks_got[:], ks_pool[:].bitcast(U8).indirect(offsets[:]))
 
         def move_ks():
-            for quad in range(4):
-                rows = ks_got[:].bitcast(I32)[96 + 8 * quad : 104 + 8 * quad, :]
-                nc.sync.dma_start(k_planes[32 * quad : 32 * quad + 4, :], rows)
+            for quad in range(P // QUAD):
+                rows = ks_got[:].bitcast(I32)[SCALE_ROWS + 8 * quad : SCALE_ROWS + 8 * (quad + 1), :]
+                nc.sync.dma_start(k_planes[QUAD * quad : QUAD * quad + 4, :], rows)
 
         def gather_kw(b):
             nc.vector.tensor_copy(kw_got[b][:], listed(kw_pool[:].bitcast(U32), b))
@@ -121,53 +123,18 @@ def tile_attend_sink_seg_kernel(tc, qT, k_words, k_scales, vT, vs, sink, offs, o
             )
 
         def gather_vs(b):
-            vs_got.setdefault(b, placed("vs_got%d" % b, [P, N], F32, 4096 + b * 2048))
-            nc.vector.tensor_copy(vs_got[b][:], listed(vs_pool[:], b))
-            nc.sync.dma_start(vs_col[b][:, 0:4], vs_got[b][0:1, :])
+            got = placed("vs_got%d" % b, [P, N], F32, STAGE + b * STAGE // 2)
+            nc.vector.tensor_copy(got[:], listed(vs_pool[:], b))
+            nc.sync.dma_start(vs_col[b][:, 0:PACK], got[0:1, :])
 
-        def group_q(b, copy):
-            copy(
-                q_bf[b][:].rearrange("p (o c i j) -> p o c j i", o=PASSES, i=4, j=4),
-                q_raw[b][:].rearrange("p o (j c i) -> p o c j i", j=4, i=4),
+        def group_q(b):
+            nc.scalar.copy(
+                q_bf[b][:].rearrange("p (o c i j) -> p o c j i", o=PASSES, i=4, j=PACK),
+                q_raw[b][:].rearrange("p o (j c i) -> p o c j i", j=PACK, i=4),
             )
 
         def quant_q(b):
             nc.vector.quantize_mx(q_codes[b][:].bitcast(FP8X4), q_scales[b][:], q_bf[b][:])
-
-
-        def turn_v(b, h, bank=None):
-            name = "turned_v%d%d" % (b, h)
-            turned_v.setdefault((b, h), psum.tile([P, 2, P], F32, name=name, tag=bank or name))
-            for u in range(2):
-                nc.tensor.transpose(turned_v[b, h][:, u, :], pairs[b, h][u], ident[:])
-
-        def weave_v(b, h, tag=None):
-            v_in.setdefault((b, h), sb("v_in%d%d" % (b, h), [P, 4 * P], BF16, tag=tag))
-            nc.scalar.copy(
-                v_in[b, h][:].bitcast(F32).rearrange("p (e u) -> p e u", u=2),
-                turned_v[b, h][:].rearrange("p u e -> p e u"),
-            )
-
-        def cast_v(b, h):
-            nc.scalar.activation(v_bf[:, seg(b + h)], v_raw[b, h][:], ACT.Copy)
-
-        def gather_v_scalar(b, h, tag=None):
-            v_got[b][h] = sb("v_got%d%d" % (b, h), [P, N], BF16, tag=tag)
-            dealt = v_got[b][h][:].rearrange("p (u s j) -> p s u j", u=2, j=2)
-            nc.scalar.activation(dealt, listed(v_bf[:, h * SEG :], b), ACT.Copy)
-            words = v_got[b][h][:].bitcast(F32)
-            pairs.setdefault((b, h), [words[:, u * P : (u + 1) * P] for u in range(2)])
-
-        def gather_v_vector(b, h, tag=None):
-            v_got[b][h] = sb("v_got%d%d" % (b, h), [P, N], BF16, tag=tag)
-            nc.vector.tensor_copy(v_got[b][h][:], listed(v_raw[b, h][:], b))
-            words = v_got[b][h][:].bitcast(F32)
-            pairs.setdefault((b, h), [words[:, u : 2 * P : 2] for u in range(2)])
-
-        def quant_v(b, h, tag=None):
-            v_codes.setdefault(b, sb("v_codes%d" % b, [P, DV], U32, tag=tag))
-            cols = slice(h * P, (h + 1) * P)
-            nc.vector.quantize_mx(v_codes[b][:, cols].bitcast(FP8X4), v_scales[b][:, cols], v_in[b, h][:])
 
         def score(b):
             for o in range(PASSES):
@@ -182,14 +149,46 @@ def tile_attend_sink_seg_kernel(tc, qT, k_words, k_scales, vT, vs, sink, offs, o
                     stop=(o == PASSES - 1),
                 )
 
+        def cast_v(b, h):
+            nc.scalar.activation(v_bf[:, seg(b + h)], v_raw[b, h][:], ACT.Copy)
+
+        def gather_v_scalar(b, h):
+            got = sb("v_got%d%d" % (b, h), [P, N], BF16)
+            dealt = got[:].rearrange("p (u s j) -> p s u j", u=2, j=2)
+            nc.scalar.activation(dealt, listed(v_bf[:, h * SEG :], b), ACT.Copy)
+            words = got[:].bitcast(F32)
+            v_words.setdefault((b, h), [words[:, u * P : (u + 1) * P] for u in range(2)])
+
+        def gather_v_vector(b, h, tag):
+            got = sb("v_got%d%d" % (b, h), [P, N], BF16, tag=tag)
+            nc.vector.tensor_copy(got[:], listed(v_raw[b, h][:], b))
+            words = got[:].bitcast(F32)
+            v_words.setdefault((b, h), [words[:, u : 2 * P : 2] for u in range(2)])
+
+        def turn_v(b, h, tag=None):
+            turned_v.setdefault((b, h), bank("turned_v%d%d" % (b, h), [P, 2, P], tag))
+            for u in range(2):
+                nc.tensor.transpose(turned_v[b, h][:, u, :], v_words[b, h][u], ident[:])
+
+        def weave_v(b, h, tag=None):
+            v_in.setdefault((b, h), sb("v_in%d%d" % (b, h), [P, PACK * P], BF16, tag=tag))
+            nc.scalar.copy(
+                v_in[b, h][:].bitcast(F32).rearrange("p (e u) -> p e u", u=2),
+                turned_v[b, h][:].rearrange("p u e -> p e u"),
+            )
+
+        def quant_v(b, h):
+            cols = slice(h * P, (h + 1) * P)
+            nc.vector.quantize_mx(v_codes[b][:, cols].bitcast(FP8X4), v_scales[b][:, cols], v_in[b, h][:])
+
         def negate_sinks():
             nc.scalar.activation(neg_all[:, :, N], sinks[:], ACT.Copy, scale=-1.0)
 
-        def row_max(b, tag=None):
-            neg_m.setdefault(b, sb("neg_m%d" % b, [P, 1], F32, tag=tag))
+        def row_max(b):
+            neg_m.setdefault(b, sb("neg_m%d" % b, [P, 1], F32, tag="after_neg_m%d" % b))
             nc.vector.tensor_scalar(
-                neg_all[:, b, 0:N].rearrange("p (t s) -> p t s", t=4),
-                scores[b][:].rearrange("p (s t) -> p t s", t=4),
+                neg_all[:, b, 0:N].rearrange("p (t s) -> p t s", t=PACK),
+                scores[b][:].rearrange("p (s t) -> p t s", t=PACK),
                 -1.0,
                 neg_all[:, b, N : N + 1],
                 ALU.mult,
@@ -197,34 +196,34 @@ def tile_attend_sink_seg_kernel(tc, qT, k_words, k_scales, vT, vs, sink, offs, o
                 accum_out=neg_m[b][:],
             )
 
-        def exponentials(b, tag=None):
-            probs.setdefault(b, sb("probs%d" % b, [P, N + 8], F32, tag=tag))
+        def exponentials(b, tag):
+            probs = sb("probs%d" % b, [P, PADDED], F32, tag=tag)
             nc.scalar.activation(
-                probs[b][:, 0 : N + 1],
+                probs[:, 0 : N + 1],
                 neg_all[:, b, 0 : N + 1],
                 ACT.Exp,
                 bias=neg_m[b][:],
                 scale=-1.0,
                 accum_out=total[:, b : b + 1],
             )
-            for t in range(4):
-                nc.tensor.transpose(turned_p[b][:, t, :], probs[b][:, t * P : (t + 1) * P], ident[:])
+            for t in range(PACK):
+                nc.tensor.transpose(turned_p[b][:, t, :], probs[:, t * P : (t + 1) * P], ident[:])
 
         def weigh(b):
             nc.vector.tensor_tensor(
-                w_bf[b][:].rearrange("p (q t) -> p q t", t=4),
+                w_bf[b][:].rearrange("p (q t) -> p q t", t=PACK),
                 turned_p[b][:].rearrange("p t q -> p q t"),
-                vs_col[b][:, 0:4].unsqueeze(1).to_broadcast([P, NQ, 4]),
+                vs_col[b][:, 0:PACK].unsqueeze(1).to_broadcast([P, NQ, PACK]),
                 ALU.mult,
             )
 
         def quant_w(b):
             nc.vector.quantize_mx(w_codes[b][:].bitcast(FP8X4), w_scales[b][:], w_bf[b][:])
 
-        def finish(b, first, count, r_total, bank):
-            cols = slice(first * P, (first + count) * P)
-            sums = psum.tile([P, count * P], F32, name="sums%d%d" % (b, first), tag=bank)
-            result = sb("result%d%d" % (b, first), [P, count * P], F32)
+        def finish(b, cols, r_total, tag):
+            width = cols.stop - cols.start
+            sums = bank("sums%d_%d" % (b, cols.start), [P, width], tag)
+            result = sb("result%d_%d" % (b, cols.start), [P, width], F32)
             nc.tensor.matmul_mx(
                 sums[:],
                 lhsT=w_codes[b][:].bitcast(FP8X4),
@@ -237,11 +236,6 @@ def tile_attend_sink_seg_kernel(tc, qT, k_words, k_scales, vT, vs, sink, offs, o
             nc.scalar.activation(result[:], sums[:], ACT.Copy, scale=r_total[:, b : b + 1])
             nc.sync.dma_start(out[b][:, cols], result[:])
 
-        def invert():
-            r_total = sb("r_total", [P, B], F32)
-            nc.vector.reciprocal(r_total[:], total[:])
-            return r_total
-
         load_key_scales()
         nc.sync.dma_start(offsets[:], offs)
         load_v(0, 0)
@@ -249,20 +243,22 @@ def tile_attend_sink_seg_kernel(tc, qT, k_words, k_scales, vT, vs, sink, offs, o
         load_q(0)
         load_kw(1)
         load_q(1)
-        load_sinks(slice(0, P), nc.sync)
+        load_sinks()
         nc.sync.dma_start(vs_pool[0:1, :], vs[0:1, :])
+
         gather_ks()
-        v_raw.setdefault((1, 0), sb("v_raw10", [P, SEG], F32, tag="early"))
+        v_raw.setdefault((1, 0), sb("v_raw10", [P, SEG], F32, tag="after_ks_pool"))
         load_v(1, 0)
         move_ks()
+
         cast_v(0, 0)
         gather_v_scalar(0, 0)
         turn_v(0, 0)
         gather_kw(0)
         part_kw(0)
-        v_raw.setdefault((1, 1), sb("v_raw11", [P, SEG], F32, tag="words0"))
+        v_raw.setdefault((1, 1), sb("v_raw11", [P, SEG], F32, tag="after_kw_got0"))
         load_v(1, 1)
-        group_q(0, nc.scalar.copy)
+        group_q(0)
         weave_v(0, 0)
         gather_kw(1)
         quant_q(0)
@@ -270,37 +266,43 @@ def tile_attend_sink_seg_kernel(tc, qT, k_words, k_scales, vT, vs, sink, offs, o
         part_kw(1)
         v_raw.setdefault((0, 1), placed("v_raw01", [P, SEG], F32, 0))
         load_v(0, 1)
-        q_bf.setdefault(1, sb("q_bf1", [P, PASSES * NQ * 4], BF16, tag="query0"))
-        group_q(1, nc.scalar.copy)
+        q_bf.setdefault(1, sb("q_bf1", [P, PASSES * NQ * PACK], BF16, tag="after_q_raw0"))
+        group_q(1)
         negate_sinks()
         quant_q(1)
         score(1)
+
         cast_v(1, 0)
         cast_v(1, 1)
         gather_v_scalar(1, 0)
         gather_vs(0)
         gather_vs(1)
-        row_max(0, "column0")
-        exponentials(0, "early")
-        row_max(1, "column1")
+        row_max(0)
+        exponentials(0, "after_ks_pool")
+        row_max(1)
         turn_v(1, 0, "scores1")
-        exponentials(1, "words0")
+        exponentials(1, "after_kw_got0")
         gather_v_scalar(1, 1)
-        gather_v_vector(0, 1, "column0")
+
+        gather_v_vector(0, 1, "after_neg_m0")
         weigh(0)
-        quant_v(0, 0, "early")
+        v_codes.setdefault(0, sb("v_codes0", [P, DV], U32, tag="after_ks_pool"))
+        quant_v(0, 0)
         turn_v(0, 1)
         turn_v(1, 1)
-        weave_v(0, 1, "column1")
+        weave_v(0, 1, "after_neg_m1")
         weave_v(1, 0)
         weave_v(1, 1)
         quant_w(0)
-        r_total = invert()
+        r_total = sb("r_total", [P, B], F32)
+        nc.vector.reciprocal(r_total[:], total[:])
         weigh(1)
         quant_v(0, 1)
         quant_w(1)
-        quant_v(1, 0, "dealt1")
+        v_codes.setdefault(1, sb("v_codes1", [P, DV], U32, tag="after_vs_col1"))
+        quant_v(1, 0)
         quant_v(1, 1)
-        finish(0, 0, 2, r_total, "scores0")
-        finish(1, 0, 1, r_total, "turned_p0")
-        finish(1, 1, 1, r_total, "turned_v00")
+
+        finish(0, slice(0, DV), r_total, "scores0")
+        finish(1, slice(0, P), r_total, "turned_p0")
+        finish(1, slice(P, DV), r_total, "turned_v00")

@@ -52,22 +52,23 @@ def tile_attend_sink_seg_kernel(tc, qT, k_words, k_scales, vT, vs, sink, offs, o
         def listed(window, b):
             return window[:, 0 : (b + 1) * SEG].indirect(offsets[:, b * COLS : (b + 1) * COLS])
 
-        ks_pool = sb("ks_pool", [P, T // 4], I32, tag="after_ks_pool")
+        ks_pool = placed("ks_pool", [P, T // 4], I32, STAGE)
         vs_pool = sb("vs_pool", [P, T], F32)
         kw_pool = sb("kw_pool", [P, T], I32)
-        v_raw = {(0, 0): placed("v_raw00", [P, SEG], F32, 0)}
+        v_pair = placed("v_pair", [P, T], F32, 5 * STAGE)
+        v_late = placed("v_late", [P, SEG], F32, STAGE + 576)
         v_bf = sb("v_bf", [P, 3 * SEG], BF16)
         q_raw = [
-            sb("q_raw0", [P, PASSES, PACK * NQ], F32, tag="after_q_raw0"),
-            placed("q_raw1", [P, PASSES, PACK * NQ], F32, STAGE),
+            placed("q_raw0", [P, PASSES, PACK * NQ], F32, 3 * STAGE),
+            placed("q_raw1", [P, PASSES, PACK * NQ], F32, 512),
         ]
-        sinks = sb("sinks", [P, B], F32)
+        sinks = placed("sinks", [P, B], F32, STAGE + 512)
         ident = sb("ident", [P, P], F32)
         neg_all = sb("neg_all", [P, B, PADDED], F32)
         k_planes = sb("k_planes", [P, PASSES * B * N // 4], I32)
 
         nc.gpsimd.memset(ks_pool[0:SCALE_ROWS, :], 0)
-        nc.vector.memset(vs_pool[:], 0.0)
+        nc.vector.memset(vs_pool[0 : P - 1, :], 0.0)
         make_identity(nc, ident[:])
         nc.gpsimd.memset(k_planes[:], 0)
 
@@ -75,20 +76,25 @@ def tile_attend_sink_seg_kernel(tc, qT, k_words, k_scales, vT, vs, sink, offs, o
         ks_hbm = k_scales.bitcast(I32)
 
         ks_got = sb("ks_got", [P, B * N], U8)
-        kw_got = [sb("kw_got0", [P, N], U32, tag="after_kw_got0"), placed("kw_got1", [P, N], U32, STAGE // 2)]
-        k_codes = [sb("k_codes%d" % b, [P, PASSES, 2 * N], U8) for b in range(B)]
-        vs_col = [sb("vs_col%d" % b, [P, 8], F32, tag="after_vs_col%d" % b) for b in range(B)]
-        q_bf = {0: placed("q_bf0", [P, PASSES * NQ * PACK], BF16, 0)}
+        kw_got = [sb("kw_got0", [P, N], U32), sb("kw_got1", [P, N], U32)]
+        k_codes = [placed("k_codes0", [P, PASSES, 2 * N], U8, 3 * STAGE + 3072), sb("k_codes1", [P, PASSES, 2 * N], U8)]
+        vs_col = [placed("vs_col%d" % b, [P, 8], F32, 4 * STAGE + 1024 + 64 * b) for b in range(B)]
+        q_bf = [placed("q_bf0", [P, PASSES * NQ * PACK], BF16, 4 * STAGE + 1024), sb("q_bf1", [P, PASSES * NQ * PACK], BF16, tag="after_q_bf1")]
         q_codes = [sb("q_codes%d" % b, [P, PASSES * NQ], U32) for b in range(B)]
         q_scales = [sb("q_scales%d" % b, [P, PASSES * NQ], U8) for b in range(B)]
-        v_scales = [sb("v_scales%d" % b, [P, DV], U8) for b in range(B)]
+        v_scales = {(b, h): sb("v_scales%d%d" % (b, h), [P, P], U8) for b, h in ((0, 0), (1, 0), (1, 1))}
+        v_scales.setdefault((0, 1), placed("v_scales01", [P, P], U8, 5 * STAGE))
+        v_codes = {(b, h): sb("v_codes%d%d" % (b, h), [P, P], U32) for b in range(B) for h in range(2)}
         total = sb("total", [P, B], F32)
-        w_bf = [sb("w_bf%d" % b, [P, PACK * NQ], BF16) for b in range(B)]
+        w_bf = [placed("w_bf0", [P, PACK * NQ], BF16, 5 * STAGE + 1024), sb("w_bf1", [P, PACK * NQ], BF16)]
         w_codes = [sb("w_codes%d" % b, [P, NQ], U32) for b in range(B)]
         w_scales = [sb("w_scales%d" % b, [P, NQ], U8) for b in range(B)]
         scores = [bank("scores%d" % b, [P, N]) for b in range(B)]
         turned_p = [bank("turned_p%d" % b, [P, PACK, NQ]) for b in range(B)]
-        v_words, turned_v, v_in, v_codes, neg_m = {}, {}, {}, {}, {}
+        turned_v = {}
+        v_raw = {(0, 0): v_pair[:, SEG:T], (0, 1): v_pair[:, 0:SEG], (1, 0): v_late[:], (1, 1): v_pair[:, SEG:T]}
+        cast_at = {(0, 0): 0, (1, 0): 1, (0, 1): 2}
+        v_words, v_in, neg_m, vs_got = {}, {}, {}, {}
 
         def load_key_scales():
             nc.sync.dma_start(ks_pool[SCALE_ROWS:P, :], ks_hbm.rearrange("o f t -> f o t"))
@@ -100,7 +106,7 @@ def tile_attend_sink_seg_kernel(tc, qT, k_words, k_scales, vT, vs, sink, offs, o
             nc.sync.dma_start(q_raw[b][:], qT[b].rearrange("(o p j) q -> p o (j q)", o=PASSES, j=PACK))
 
         def load_v(b, h):
-            nc.sync.dma_start(v_raw[b, h][:], vT[h * P : (h + 1) * P, seg(b)])
+            nc.sync.dma_start(v_raw[b, h], vT[h * P : (h + 1) * P, seg(b)])
 
         def load_sinks():
             with nc.allow_non_contiguous_dma(reason="one sink a partition and sequence"):
@@ -123,9 +129,11 @@ def tile_attend_sink_seg_kernel(tc, qT, k_words, k_scales, vT, vs, sink, offs, o
             )
 
         def gather_vs(b):
-            got = placed("vs_got%d" % b, [P, N], F32, STAGE + b * STAGE // 2)
+            got = vs_got.setdefault(b, sb("vs_got%d" % b, [P, N], F32))
             nc.vector.tensor_copy(got[:], listed(vs_pool[:], b))
-            nc.sync.dma_start(vs_col[b][:, 0:PACK], got[0:1, :])
+
+        def deal_vs(b):
+            nc.sync.dma_start(vs_col[b][:, 0:PACK], vs_got[b][P - 1 : P, :])
 
         def group_q(b):
             nc.scalar.copy(
@@ -150,42 +158,42 @@ def tile_attend_sink_seg_kernel(tc, qT, k_words, k_scales, vT, vs, sink, offs, o
                 )
 
         def cast_v(b, h):
-            nc.scalar.activation(v_bf[:, seg(b + h)], v_raw[b, h][:], ACT.Copy)
+            nc.scalar.activation(v_bf[:, seg(cast_at[b, h])], v_raw[b, h], ACT.Copy)
 
-        def gather_v_scalar(b, h):
-            got = sb("v_got%d%d" % (b, h), [P, N], BF16)
-            dealt = got[:].rearrange("p (u s j) -> p s u j", u=2, j=2)
-            nc.scalar.activation(dealt, listed(v_bf[:, h * SEG :], b), ACT.Copy)
-            words = got[:].bitcast(F32)
+        def gather_v_scalar(b, h, got, part=0, parts=1):
+            dealt = got.rearrange("p (u s j) -> p s u j", u=2, j=2)[:, part * P // parts : (part + 1) * P // parts]
+            window = v_bf[:, (cast_at[b, h] - b) * SEG : (cast_at[b, h] + 1) * SEG]
+            first = b * COLS + part * COLS // parts
+            nc.scalar.activation(dealt, window.indirect(offsets[:, first : first + COLS // parts]), ACT.Copy)
+            words = got.bitcast(F32)
             v_words.setdefault((b, h), [words[:, u * P : (u + 1) * P] for u in range(2)])
 
-        def gather_v_vector(b, h, tag):
-            got = sb("v_got%d%d" % (b, h), [P, N], BF16, tag=tag)
-            nc.vector.tensor_copy(got[:], listed(v_raw[b, h][:], b))
+        def gather_v_vector(b, h):
+            got = sb("v_got%d%d" % (b, h), [P, N], BF16, tag="after_q_bf1")
+            nc.vector.tensor_copy(got[:], listed(v_pair[:], b))
             words = got[:].bitcast(F32)
             v_words.setdefault((b, h), [words[:, u : 2 * P : 2] for u in range(2)])
 
         def turn_v(b, h, tag=None):
-            turned_v.setdefault((b, h), bank("turned_v%d%d" % (b, h), [P, 2, P], tag))
+            turned_v.setdefault((b, h), bank("turned_v%d%d" % (b, h), [P, 2, P], tag)[:])
             for u in range(2):
                 nc.tensor.transpose(turned_v[b, h][:, u, :], v_words[b, h][u], ident[:])
 
-        def weave_v(b, h, tag=None):
-            v_in.setdefault((b, h), sb("v_in%d%d" % (b, h), [P, PACK * P], BF16, tag=tag))
+        def weave_v(b, h, tile):
+            v_in.setdefault((b, h), tile)
             nc.scalar.copy(
                 v_in[b, h][:].bitcast(F32).rearrange("p (e u) -> p e u", u=2),
-                turned_v[b, h][:].rearrange("p u e -> p e u"),
+                turned_v[b, h].rearrange("p u e -> p e u"),
             )
 
         def quant_v(b, h):
-            cols = slice(h * P, (h + 1) * P)
-            nc.vector.quantize_mx(v_codes[b][:, cols].bitcast(FP8X4), v_scales[b][:, cols], v_in[b, h][:])
+            nc.vector.quantize_mx(v_codes[b, h][:].bitcast(FP8X4), v_scales[b, h][:], v_in[b, h][:])
 
         def negate_sinks():
             nc.scalar.activation(neg_all[:, :, N], sinks[:], ACT.Copy, scale=-1.0)
 
-        def row_max(b):
-            neg_m.setdefault(b, sb("neg_m%d" % b, [P, 1], F32, tag="after_neg_m%d" % b))
+        def row_max(b, tile):
+            neg_m.setdefault(b, tile)
             nc.vector.tensor_scalar(
                 neg_all[:, b, 0:N].rearrange("p (t s) -> p t s", t=PACK),
                 scores[b][:].rearrange("p (s t) -> p t s", t=PACK),
@@ -193,16 +201,15 @@ def tile_attend_sink_seg_kernel(tc, qT, k_words, k_scales, vT, vs, sink, offs, o
                 neg_all[:, b, N : N + 1],
                 ALU.mult,
                 ALU.min,
-                accum_out=neg_m[b][:],
+                accum_out=neg_m[b],
             )
 
-        def exponentials(b, tag):
-            probs = sb("probs%d" % b, [P, PADDED], F32, tag=tag)
+        def exponentials(b, probs):
             nc.scalar.activation(
                 probs[:, 0 : N + 1],
                 neg_all[:, b, 0 : N + 1],
                 ACT.Exp,
-                bias=neg_m[b][:],
+                bias=neg_m[b],
                 scale=-1.0,
                 accum_out=total[:, b : b + 1],
             )
@@ -224,85 +231,81 @@ def tile_attend_sink_seg_kernel(tc, qT, k_words, k_scales, vT, vs, sink, offs, o
             width = cols.stop - cols.start
             sums = bank("sums%d_%d" % (b, cols.start), [P, width], tag)
             result = sb("result%d_%d" % (b, cols.start), [P, width], F32)
-            nc.tensor.matmul_mx(
-                sums[:],
-                lhsT=w_codes[b][:].bitcast(FP8X4),
-                lhsT_scale=w_scales[b][:],
-                rhs=v_codes[b][:, cols].bitcast(FP8X4),
-                rhs_scale=v_scales[b][:, cols],
-                start=True,
-                stop=True,
-            )
+            for h in range(cols.start // P, cols.stop // P):
+                nc.tensor.matmul_mx(
+                    sums[:, h * P - cols.start : (h + 1) * P - cols.start],
+                    lhsT=w_codes[b][:].bitcast(FP8X4),
+                    lhsT_scale=w_scales[b][:],
+                    rhs=v_codes[b, h][:].bitcast(FP8X4),
+                    rhs_scale=v_scales[b, h][:],
+                    start=True,
+                    stop=True,
+                )
             nc.scalar.activation(result[:], sums[:], ACT.Copy, scale=r_total[:, b : b + 1])
             nc.sync.dma_start(out[b][:, cols], result[:])
 
         load_key_scales()
         nc.sync.dma_start(offsets[:], offs)
         load_v(0, 0)
+        nc.sync.dma_start(vs_pool[P - 1 : P, :], vs[0:1, :])
         load_kw(0)
         load_q(0)
+        load_v(0, 1)
         load_kw(1)
-        load_q(1)
-        load_sinks()
-        nc.sync.dma_start(vs_pool[0:1, :], vs[0:1, :])
 
         gather_ks()
-        v_raw.setdefault((1, 0), sb("v_raw10", [P, SEG], F32, tag="after_ks_pool"))
-        load_v(1, 0)
         move_ks()
-
+        load_q(1)
+        load_sinks()
+        load_v(1, 0)
         cast_v(0, 0)
-        gather_v_scalar(0, 0)
-        turn_v(0, 0)
-        gather_kw(0)
-        part_kw(0)
-        v_raw.setdefault((1, 1), sb("v_raw11", [P, SEG], F32, tag="after_kw_got0"))
         load_v(1, 1)
-        group_q(0)
-        weave_v(0, 0)
-        gather_kw(1)
-        quant_q(0)
-        score(0)
-        part_kw(1)
-        v_raw.setdefault((0, 1), placed("v_raw01", [P, SEG], F32, 0))
-        load_v(0, 1)
-        q_bf.setdefault(1, sb("q_bf1", [P, PASSES * NQ * PACK], BF16, tag="after_q_raw0"))
-        group_q(1)
-        negate_sinks()
-        quant_q(1)
-        score(1)
-
-        cast_v(1, 0)
-        cast_v(1, 1)
-        gather_v_scalar(1, 0)
+        gather_v_scalar(0, 0, sb("v_got00", [P, N], BF16)[:])
+        turn_v(0, 0)
         gather_vs(0)
         gather_vs(1)
-        row_max(0)
-        exponentials(0, "after_ks_pool")
-        row_max(1)
-        turn_v(1, 0, "scores1")
-        exponentials(1, "after_kw_got0")
-        gather_v_scalar(1, 1)
-
-        gather_v_vector(0, 1, "after_neg_m0")
-        weigh(0)
-        v_codes.setdefault(0, sb("v_codes0", [P, DV], U32, tag="after_ks_pool"))
+        gather_kw(0)
+        group_q(0)
+        cast_v(0, 1)
+        weave_v(0, 0, placed("v_in00", [P, PACK * P], BF16, 3 * STAGE))
+        gather_v_scalar(0, 1, sb("v_got01", [P, N], BF16)[:])
+        quant_q(0)
+        part_kw(0)
+        deal_vs(0)
+        deal_vs(1)
+        score(0)
+        gather_kw(1)
         quant_v(0, 0)
-        turn_v(0, 1)
+        part_kw(1)
+        group_q(1)
+        negate_sinks()
+        cast_v(1, 0)
+        quant_q(1)
+        score(1)
+        row_max(0, placed("neg_m0", [P, 1], F32, 512)[:])
+        turn_v(0, 1, "scores0")
+        exponentials(0, placed("probs0", [P, PADDED], F32, STAGE + 2048))
+        weave_v(0, 1, placed("v_in01", [P, PACK * P], BF16, STAGE + 640))
+        gather_v_vector(1, 1)
+        got10 = placed("v_got10", [P, N // 2], F32, 5 * STAGE + 2048)
+        row_max(1, got10[:, N // 2 - 1 : N // 2])
+        gather_v_scalar(1, 0, got10[:].bitcast(BF16), 0, 2)
+        exponentials(1, sb("probs1", [P, PADDED], F32, tag="after_probs1"))
+        gather_v_scalar(1, 0, got10[:].bitcast(BF16), 1, 2)
         turn_v(1, 1)
-        weave_v(0, 1, "after_neg_m1")
-        weave_v(1, 0)
-        weave_v(1, 1)
+        turn_v(1, 0)
+        weigh(0)
+        quant_v(0, 1)
         quant_w(0)
-        r_total = sb("r_total", [P, B], F32)
+        r_total = placed("r_total", [P, B], F32, 4 * STAGE + 1024)
         nc.vector.reciprocal(r_total[:], total[:])
         weigh(1)
-        quant_v(0, 1)
-        quant_w(1)
-        v_codes.setdefault(1, sb("v_codes1", [P, DV], U32, tag="after_vs_col1"))
-        quant_v(1, 0)
+        weave_v(1, 1, sb("v_in11", [P, PACK * P], BF16, tag="after_probs1"))
+        weave_v(1, 0, sb("v_in10", [P, PACK * P], BF16))
         quant_v(1, 1)
+        quant_w(1)
+        quant_v(1, 0)
 
         finish(0, slice(0, DV), r_total, "scores0")
-        finish(1, slice(0, P), r_total, "turned_p0")
-        finish(1, slice(P, DV), r_total, "turned_v00")
+        finish(1, slice(P, DV), r_total, "turned_p0")
+        finish(1, slice(0, P), r_total, "turned_v00")

@@ -26,6 +26,15 @@ COLS = N // 16
 SCALE_ROWS = P - QUAD
 PADDED = N + 8
 STAGE = 4 * SEG
+LINE = 64
+
+KS_AT = STAGE
+Q0_AT = 3 * STAGE
+V_PAIR_AT = 5 * STAGE
+VS_AT = 7 * STAGE
+KW_AT = 9 * STAGE
+PROBS1_AT = 12 * STAGE
+Q1_AT = (KS_AT + LINE - STAGE // 2, KS_AT + 2 * LINE)
 
 
 def tile_attend_sink_seg_kernel(tc, qT, k_words, k_scales, vT, vs, sink, offs, out):
@@ -35,11 +44,11 @@ def tile_attend_sink_seg_kernel(tc, qT, k_words, k_scales, vT, vs, sink, offs, o
         lent = ctx.enter_context(tc.tile_pool(name="lent", bufs=1))
         psum = ctx.enter_context(tc.psum_pool(name="psum", bufs=1))
 
-        def sb(name, shape, dtype, tag=None):
-            return keep.tile(shape, dtype, name=name, tag=tag or name, align_bytes=64)
+        def sb(name, shape, dtype):
+            return keep.tile(shape, dtype, name=name, tag=name, align_bytes=LINE)
 
         def placed(name, shape, dtype, offset):
-            return lent.tile(shape, dtype, name=name, tag=name, align_bytes=64, offset=offset)
+            return lent.tile(shape, dtype, name=name, tag=name, align_bytes=LINE, offset=offset)
 
         def bank(name, shape, tag=None):
             return psum.tile(shape, F32, name=name, tag=tag or name)
@@ -52,17 +61,15 @@ def tile_attend_sink_seg_kernel(tc, qT, k_words, k_scales, vT, vs, sink, offs, o
         def listed(window, b):
             return window[:, 0 : (b + 1) * SEG].indirect(offsets[:, b * COLS : (b + 1) * COLS])
 
-        ks_pool = placed("ks_pool", [P, T // 4], I32, STAGE)
-        vs_pool = sb("vs_pool", [P, T], F32)
-        kw_pool = sb("kw_pool", [P, T], I32)
-        v_pair = placed("v_pair", [P, T], F32, 5 * STAGE)
-        v_late = placed("v_late", [P, SEG], F32, STAGE + 576)
+        ks_pool = placed("ks_pool", [P, T // 4], I32, KS_AT)
+        vs_pool = placed("vs_pool", [P, T], F32, VS_AT)
+        kw_pool = placed("kw_pool", [P, T], I32, KW_AT)
+        v_pair = placed("v_pair", [P, T], F32, V_PAIR_AT)
+        v_late = placed("v_late", [P, SEG], F32, VS_AT)
         v_bf = sb("v_bf", [P, 3 * SEG], BF16)
-        q_raw = [
-            placed("q_raw0", [P, PASSES, PACK * NQ], F32, 3 * STAGE),
-            placed("q_raw1", [P, PASSES, PACK * NQ], F32, 512),
-        ]
-        sinks = placed("sinks", [P, B], F32, STAGE + 512)
+        q_raw0 = placed("q_raw0", [P, PASSES, PACK * NQ], F32, Q0_AT)
+        q_raw1 = [placed("q_raw1%d" % o, [P, PACK * NQ], F32, Q1_AT[o]) for o in range(PASSES)]
+        sinks = placed("sinks", [P, B], F32, KS_AT + LINE)
         ident = sb("ident", [P, P], F32)
         neg_all = sb("neg_all", [P, B, PADDED], F32)
         k_planes = sb("k_planes", [P, PASSES * B * N // 4], I32)
@@ -76,25 +83,27 @@ def tile_attend_sink_seg_kernel(tc, qT, k_words, k_scales, vT, vs, sink, offs, o
         ks_hbm = k_scales.bitcast(I32)
 
         ks_got = sb("ks_got", [P, B * N], U8)
-        kw_got = [sb("kw_got0", [P, N], U32), sb("kw_got1", [P, N], U32)]
-        k_codes = [placed("k_codes0", [P, PASSES, 2 * N], U8, 3 * STAGE + 3072), sb("k_codes1", [P, PASSES, 2 * N], U8)]
-        vs_col = [placed("vs_col%d" % b, [P, 8], F32, 4 * STAGE + 1024 + 64 * b) for b in range(B)]
-        q_bf = [placed("q_bf0", [P, PASSES * NQ * PACK], BF16, 4 * STAGE + 1024), sb("q_bf1", [P, PASSES * NQ * PACK], BF16, tag="after_q_bf1")]
+        kw_got = [sb("kw_got%d" % b, [P, N], U32) for b in range(B)]
+        k_codes = [
+            placed("k_codes0", [P, PASSES, 2 * N], U8, Q0_AT + 3 * STAGE // 4),
+            sb("k_codes1", [P, PASSES, 2 * N], U8),
+        ]
+        vs_col = [placed("vs_col%d" % b, [P, 8], F32, KW_AT + LINE * b) for b in range(B)]
+        q_bf = [sb("q_bf%d" % b, [P, PASSES * NQ * PACK], BF16) for b in range(B)]
         q_codes = [sb("q_codes%d" % b, [P, PASSES * NQ], U32) for b in range(B)]
         q_scales = [sb("q_scales%d" % b, [P, PASSES * NQ], U8) for b in range(B)]
-        v_scales = {(b, h): sb("v_scales%d%d" % (b, h), [P, P], U8) for b, h in ((0, 0), (1, 0), (1, 1))}
-        v_scales.setdefault((0, 1), placed("v_scales01", [P, P], U8, 5 * STAGE))
-        v_codes = {(b, h): sb("v_codes%d%d" % (b, h), [P, P], U32) for b in range(B) for h in range(2)}
+        v_scales = {(b, h): sb("v_scales%d%d" % (b, h), [P, P], U8) for b in range(B) for h in range(DV // P)}
+        v_codes = {(b, h): sb("v_codes%d%d" % (b, h), [P, P], U32) for b in range(B) for h in range(DV // P)}
         total = sb("total", [P, B], F32)
-        w_bf = [placed("w_bf0", [P, PACK * NQ], BF16, 5 * STAGE + 1024), sb("w_bf1", [P, PACK * NQ], BF16)]
-        w_codes = [sb("w_codes%d" % b, [P, NQ], U32) for b in range(B)]
+        w_bf = [placed("w_bf0", [P, PACK * NQ], BF16, VS_AT + STAGE // 4), sb("w_bf1", [P, PACK * NQ], BF16)]
+        w_codes = [placed("w_codes0", [P, NQ], U32, PROBS1_AT), sb("w_codes1", [P, NQ], U32)]
         w_scales = [sb("w_scales%d" % b, [P, NQ], U8) for b in range(B)]
         scores = [bank("scores%d" % b, [P, N]) for b in range(B)]
         turned_p = [bank("turned_p%d" % b, [P, PACK, NQ]) for b in range(B)]
-        turned_v = {}
-        v_raw = {(0, 0): v_pair[:, SEG:T], (0, 1): v_pair[:, 0:SEG], (1, 0): v_late[:], (1, 1): v_pair[:, SEG:T]}
+        v_raw = {(0, 0): v_pair[:, 0:SEG], (0, 1): v_pair[:, SEG:T], (1, 0): v_late[:], (1, 1): v_pair[:, SEG:T]}
         cast_at = {(0, 0): 0, (1, 0): 1, (0, 1): 2}
-        v_words, v_in, neg_m, vs_got = {}, {}, {}, {}
+        vs_got = sb("vs_got", [P, B * N], F32)
+        v_words, turned_v, v_in, neg_m = {}, {}, {}, {}
 
         def load_key_scales():
             nc.sync.dma_start(ks_pool[SCALE_ROWS:P, :], ks_hbm.rearrange("o f t -> f o t"))
@@ -102,8 +111,14 @@ def tile_attend_sink_seg_kernel(tc, qT, k_words, k_scales, vT, vs, sink, offs, o
         def load_kw(b):
             nc.sync.dma_start(kw_pool[:, seg(b)], kw_hbm[:, seg(b)])
 
-        def load_q(b):
-            nc.sync.dma_start(q_raw[b][:], qT[b].rearrange("(o p j) q -> p o (j q)", o=PASSES, j=PACK))
+        def q_hbm(b):
+            return qT[b].rearrange("(o p j) q -> p o (j q)", o=PASSES, j=PACK)
+
+        def load_q0():
+            nc.sync.dma_start(q_raw0[:], q_hbm(0))
+
+        def load_q1(o):
+            nc.sync.dma_start(q_raw1[o][:], q_hbm(1)[:, o, :])
 
         def load_v(b, h):
             nc.sync.dma_start(v_raw[b, h], vT[h * P : (h + 1) * P, seg(b)])
@@ -128,24 +143,34 @@ def tile_attend_sink_seg_kernel(tc, qT, k_words, k_scales, vT, vs, sink, offs, o
                 k_codes[b][:].bitcast(U16), kw_got[b][:].bitcast(U16).rearrange("p (s o) -> p o s", o=PASSES)
             )
 
-        def gather_vs(b):
-            got = vs_got.setdefault(b, sb("vs_got%d" % b, [P, N], F32))
-            nc.vector.tensor_copy(got[:], listed(vs_pool[:], b))
+        def gather_vs():
+            nc.vector.tensor_copy(vs_got[:], vs_pool[:].indirect(offsets[:]))
 
         def deal_vs(b):
-            nc.sync.dma_start(vs_col[b][:, 0:PACK], vs_got[b][P - 1 : P, :])
+            nc.sync.dma_start(vs_col[b][:, 0:PACK], vs_got[P - 1 : P, b * N : (b + 1) * N])
 
-        def group_q(b):
+        def group_q0():
             nc.scalar.copy(
-                q_bf[b][:].rearrange("p (o c i j) -> p o c j i", o=PASSES, i=4, j=PACK),
-                q_raw[b][:].rearrange("p o (j c i) -> p o c j i", j=PACK, i=4),
+                q_bf[0][:].rearrange("p (o c i j) -> p o c j i", o=PASSES, i=4, j=PACK),
+                q_raw0[:].rearrange("p o (j c i) -> p o c j i", j=PACK, i=4),
             )
 
-        def quant_q(b):
-            nc.vector.quantize_mx(q_codes[b][:].bitcast(FP8X4), q_scales[b][:], q_bf[b][:])
+        def group_q1(o):
+            nc.scalar.copy(
+                q_bf[1][:, o * PACK * NQ : (o + 1) * PACK * NQ].rearrange("p (c i j) -> p c j i", i=4, j=PACK),
+                q_raw1[o][:].rearrange("p (j c i) -> p c j i", j=PACK, i=4),
+            )
 
-        def score(b):
-            for o in range(PASSES):
+        def quant_q(b, first, last):
+            cols = slice(first * NQ, last * NQ)
+            nc.vector.quantize_mx(
+                q_codes[b][:, cols].bitcast(FP8X4),
+                q_scales[b][:, cols],
+                q_bf[b][:, PACK * cols.start : PACK * cols.stop],
+            )
+
+        def score(b, first, last):
+            for o in range(first, last):
                 cols = slice(o * NQ, (o + 1) * NQ)
                 nc.tensor.matmul_mx(
                     scores[b][:],
@@ -157,8 +182,11 @@ def tile_attend_sink_seg_kernel(tc, qT, k_words, k_scales, vT, vs, sink, offs, o
                     stop=(o == PASSES - 1),
                 )
 
-        def cast_v(b, h):
+        def cast_v_scalar(b, h):
             nc.scalar.activation(v_bf[:, seg(cast_at[b, h])], v_raw[b, h], ACT.Copy)
+
+        def cast_v_vector(b, h):
+            nc.vector.tensor_copy(v_bf[:, seg(cast_at[b, h])], v_raw[b, h])
 
         def gather_v_scalar(b, h, got, part=0, parts=1):
             dealt = got.rearrange("p (u s j) -> p s u j", u=2, j=2)[:, part * P // parts : (part + 1) * P // parts]
@@ -168,10 +196,9 @@ def tile_attend_sink_seg_kernel(tc, qT, k_words, k_scales, vT, vs, sink, offs, o
             words = got.bitcast(F32)
             v_words.setdefault((b, h), [words[:, u * P : (u + 1) * P] for u in range(2)])
 
-        def gather_v_vector(b, h):
-            got = sb("v_got%d%d" % (b, h), [P, N], BF16, tag="after_q_bf1")
-            nc.vector.tensor_copy(got[:], listed(v_pair[:], b))
-            words = got[:].bitcast(F32)
+        def gather_v_vector(b, h, got):
+            nc.vector.tensor_copy(got, listed(v_pair[:], b))
+            words = got.bitcast(F32)
             v_words.setdefault((b, h), [words[:, u : 2 * P : 2] for u in range(2)])
 
         def turn_v(b, h, tag=None):
@@ -192,8 +219,8 @@ def tile_attend_sink_seg_kernel(tc, qT, k_words, k_scales, vT, vs, sink, offs, o
         def negate_sinks():
             nc.scalar.activation(neg_all[:, :, N], sinks[:], ACT.Copy, scale=-1.0)
 
-        def row_max(b, tile):
-            neg_m.setdefault(b, tile)
+        def row_max(b, column):
+            neg_m.setdefault(b, column)
             nc.vector.tensor_scalar(
                 neg_all[:, b, 0:N].rearrange("p (t s) -> p t s", t=PACK),
                 scores[b][:].rearrange("p (s t) -> p t s", t=PACK),
@@ -249,63 +276,70 @@ def tile_attend_sink_seg_kernel(tc, qT, k_words, k_scales, vT, vs, sink, offs, o
         load_v(0, 0)
         nc.sync.dma_start(vs_pool[P - 1 : P, :], vs[0:1, :])
         load_kw(0)
-        load_q(0)
+        load_q0()
         load_v(0, 1)
         load_kw(1)
 
         gather_ks()
         move_ks()
-        load_q(1)
+        load_q1(0)
+        load_q1(1)
         load_sinks()
-        load_v(1, 0)
-        cast_v(0, 0)
-        load_v(1, 1)
+        cast_v_scalar(0, 0)
         gather_v_scalar(0, 0, sb("v_got00", [P, N], BF16)[:])
         turn_v(0, 0)
-        gather_vs(0)
-        gather_vs(1)
+        gather_vs()
+        load_v(1, 0)
+
         gather_kw(0)
-        group_q(0)
-        cast_v(0, 1)
-        weave_v(0, 0, placed("v_in00", [P, PACK * P], BF16, 3 * STAGE))
+        group_q0()
+        cast_v_scalar(0, 1)
+        load_v(1, 1)
+        weave_v(0, 0, placed("v_in00", [P, PACK * P], BF16, Q0_AT))
         gather_v_scalar(0, 1, sb("v_got01", [P, N], BF16)[:])
-        quant_q(0)
+        quant_q(0, 0, PASSES)
         part_kw(0)
+        score(0, 0, PASSES)
+        gather_kw(1)
         deal_vs(0)
         deal_vs(1)
-        score(0)
-        gather_kw(1)
         quant_v(0, 0)
         part_kw(1)
-        group_q(1)
         negate_sinks()
-        cast_v(1, 0)
-        quant_q(1)
-        score(1)
-        row_max(0, placed("neg_m0", [P, 1], F32, 512)[:])
-        turn_v(0, 1, "scores0")
-        exponentials(0, placed("probs0", [P, PADDED], F32, STAGE + 2048))
-        weave_v(0, 1, placed("v_in01", [P, PACK * P], BF16, STAGE + 640))
-        gather_v_vector(1, 1)
-        got10 = placed("v_got10", [P, N // 2], F32, 5 * STAGE + 2048)
-        row_max(1, got10[:, N // 2 - 1 : N // 2])
-        gather_v_scalar(1, 0, got10[:].bitcast(BF16), 0, 2)
-        exponentials(1, sb("probs1", [P, PADDED], F32, tag="after_probs1"))
-        gather_v_scalar(1, 0, got10[:].bitcast(BF16), 1, 2)
-        turn_v(1, 1)
-        turn_v(1, 0)
+
+        group_q1(0)
+        group_q1(1)
+        quant_q(1, 0, 1)
+        score(1, 0, 1)
+        row_max(0, placed("neg_m0", [P, 1], F32, Q1_AT[0])[:])
+        quant_q(1, 1, 2)
+        score(1, 1, 2)
+        exponentials(0, sb("probs0", [P, PADDED], F32))
+
+        cast_v_vector(1, 0)
+        v_got10 = placed("v_got10", [P, N // 2], F32, VS_AT)
+        row_max(1, v_got10[:, N // 2 - 1 : N // 2])
+        gather_v_scalar(1, 0, v_got10[:].bitcast(BF16), 0, 2)
+
+        turn_v(0, 1, "scores1")
+        exponentials(1, placed("probs1", [P, PADDED], F32, PROBS1_AT))
+        gather_v_scalar(1, 0, v_got10[:].bitcast(BF16), 1, 2)
         weigh(0)
-        quant_v(0, 1)
-        quant_w(0)
-        r_total = placed("r_total", [P, B], F32, 4 * STAGE + 1024)
-        nc.vector.reciprocal(r_total[:], total[:])
+        gather_v_vector(1, 1, placed("v_got11", [P, N], BF16, VS_AT + STAGE // 2)[:])
+        turn_v(1, 1, "turned_p0")
         weigh(1)
-        weave_v(1, 1, sb("v_in11", [P, PACK * P], BF16, tag="after_probs1"))
+        weave_v(0, 1, placed("v_in01", [P, PACK * P], BF16, PROBS1_AT + STAGE // 4))
+        turn_v(1, 0, "scores1")
+        weave_v(1, 1, sb("v_in11", [P, PACK * P], BF16))
         weave_v(1, 0, sb("v_in10", [P, PACK * P], BF16))
-        quant_v(1, 1)
+        quant_w(0)
+        r_total = placed("r_total", [P, B], F32, PROBS1_AT + STAGE // 8)
+        nc.vector.reciprocal(r_total[:], total[:])
+        quant_v(0, 1)
         quant_w(1)
+        quant_v(1, 1)
         quant_v(1, 0)
 
         finish(0, slice(0, DV), r_total, "scores0")
-        finish(1, slice(P, DV), r_total, "turned_p0")
+        finish(1, slice(P, DV), r_total, "sums")
         finish(1, slice(0, P), r_total, "turned_v00")

@@ -34,7 +34,7 @@ V_PAIR_AT = 5 * STAGE
 VS_AT = 7 * STAGE
 KW_AT = 9 * STAGE
 PROBS1_AT = 12 * STAGE
-Q1_AT = (KS_AT + LINE - STAGE // 2, KS_AT + 2 * LINE)
+Q1_AT = (KS_AT - STAGE // 4, KS_AT + STAGE // 4)
 
 
 def tile_attend_sink_seg_kernel(tc, qT, k_words, k_scales, vT, vs, sink, offs, out):
@@ -69,7 +69,7 @@ def tile_attend_sink_seg_kernel(tc, qT, k_words, k_scales, vT, vs, sink, offs, o
         v_bf = sb("v_bf", [P, 3 * SEG], BF16)
         q_raw0 = placed("q_raw0", [P, PASSES, PACK * NQ], F32, Q0_AT)
         q_raw1 = [placed("q_raw1%d" % o, [P, PACK * NQ], F32, Q1_AT[o]) for o in range(PASSES)]
-        sinks = placed("sinks", [P, B], F32, KS_AT + LINE)
+        sink_rows = sb("sink_rows", [P, NQ], F32)
         ident = sb("ident", [P, P], F32)
         neg_all = sb("neg_all", [P, B, PADDED], F32)
         k_planes = sb("k_planes", [P, PASSES * B * N // 4], I32)
@@ -77,6 +77,7 @@ def tile_attend_sink_seg_kernel(tc, qT, k_words, k_scales, vT, vs, sink, offs, o
         nc.gpsimd.memset(ks_pool[0:SCALE_ROWS, :], 0)
         nc.vector.memset(vs_pool[0 : P - 1, :], 0.0)
         make_identity(nc, ident[:])
+        nc.gpsimd.memset(sink_rows[0 : P - B, :], 0.0)
         nc.gpsimd.memset(k_planes[:], 0)
 
         kw_hbm = k_words[0].rearrange("p t c -> p (t c)").bitcast(I32)
@@ -88,7 +89,7 @@ def tile_attend_sink_seg_kernel(tc, qT, k_words, k_scales, vT, vs, sink, offs, o
             placed("k_codes0", [P, PASSES, 2 * N], U8, Q0_AT + 3 * STAGE // 4),
             sb("k_codes1", [P, PASSES, 2 * N], U8),
         ]
-        vs_col = [placed("vs_col%d" % b, [P, 8], F32, KW_AT + LINE * b) for b in range(B)]
+        vs_col = [sb("vs_col0", [P, 8], F32), placed("vs_col1", [P, 8], F32, KW_AT)]
         q_bf = [sb("q_bf%d" % b, [P, PASSES * NQ * PACK], BF16) for b in range(B)]
         q_codes = [sb("q_codes%d" % b, [P, PASSES * NQ], U32) for b in range(B)]
         q_scales = [sb("q_scales%d" % b, [P, PASSES * NQ], U8) for b in range(B)]
@@ -124,8 +125,7 @@ def tile_attend_sink_seg_kernel(tc, qT, k_words, k_scales, vT, vs, sink, offs, o
             nc.sync.dma_start(v_raw[b, h], vT[h * P : (h + 1) * P, seg(b)])
 
         def load_sinks():
-            with nc.allow_non_contiguous_dma(reason="one sink a partition and sequence"):
-                nc.sync.dma_start(sinks[0:P, :], sink[:, 0:P, 0].rearrange("b q -> q b"))
+            nc.sync.dma_start(sink_rows[P - B : P, :], sink.rearrange("b q o -> b (q o)"))
 
         def gather_ks():
             nc.vector.tensor_copy(ks_got[:], ks_pool[:].bitcast(U8).indirect(offsets[:]))
@@ -217,7 +217,9 @@ def tile_attend_sink_seg_kernel(tc, qT, k_words, k_scales, vT, vs, sink, offs, o
             nc.vector.quantize_mx(v_codes[b, h][:].bitcast(FP8X4), v_scales[b, h][:], v_in[b, h][:])
 
         def negate_sinks():
-            nc.scalar.activation(neg_all[:, :, N], sinks[:], ACT.Copy, scale=-1.0)
+            turned = bank("turned_sinks", [P, P])
+            nc.tensor.transpose(turned[:], sink_rows[:], ident[:])
+            nc.scalar.activation(neg_all[:, :, N], turned[:, P - B : P], ACT.Copy, scale=-1.0)
 
         def row_max(b, column):
             neg_m.setdefault(b, column)
@@ -279,17 +281,18 @@ def tile_attend_sink_seg_kernel(tc, qT, k_words, k_scales, vT, vs, sink, offs, o
         load_q0()
         load_v(0, 1)
         load_kw(1)
+        load_sinks()
 
         gather_ks()
         move_ks()
         load_q1(0)
         load_q1(1)
-        load_sinks()
         cast_v_scalar(0, 0)
         gather_v_scalar(0, 0, sb("v_got00", [P, N], BF16)[:])
         turn_v(0, 0)
         gather_vs()
         load_v(1, 0)
+        deal_vs(0)
 
         gather_kw(0)
         group_q0()
@@ -301,7 +304,6 @@ def tile_attend_sink_seg_kernel(tc, qT, k_words, k_scales, vT, vs, sink, offs, o
         part_kw(0)
         score(0, 0, PASSES)
         gather_kw(1)
-        deal_vs(0)
         deal_vs(1)
         quant_v(0, 0)
         part_kw(1)
@@ -314,7 +316,7 @@ def tile_attend_sink_seg_kernel(tc, qT, k_words, k_scales, vT, vs, sink, offs, o
         row_max(0, placed("neg_m0", [P, 1], F32, Q1_AT[0])[:])
         quant_q(1, 1, 2)
         score(1, 1, 2)
-        exponentials(0, sb("probs0", [P, PADDED], F32))
+        exponentials(0, placed("probs0", [P, PADDED], F32, VS_AT + STAGE))
 
         cast_v_vector(1, 0)
         v_got10 = placed("v_got10", [P, N // 2], F32, VS_AT)
@@ -325,7 +327,7 @@ def tile_attend_sink_seg_kernel(tc, qT, k_words, k_scales, vT, vs, sink, offs, o
         exponentials(1, placed("probs1", [P, PADDED], F32, PROBS1_AT))
         gather_v_scalar(1, 0, v_got10[:].bitcast(BF16), 1, 2)
         weigh(0)
-        gather_v_vector(1, 1, placed("v_got11", [P, N], BF16, VS_AT + STAGE // 2)[:])
+        gather_v_vector(1, 1, placed("v_got11", [P, N], BF16, VS_AT + 7 * STAGE // 8)[:])
         turn_v(1, 1, "turned_p0")
         weigh(1)
         weave_v(0, 1, placed("v_in01", [P, PACK * P], BF16, PROBS1_AT + STAGE // 4))
@@ -341,5 +343,5 @@ def tile_attend_sink_seg_kernel(tc, qT, k_words, k_scales, vT, vs, sink, offs, o
         quant_v(1, 0)
 
         finish(0, slice(0, DV), r_total, "scores0")
-        finish(1, slice(P, DV), r_total, "sums")
+        finish(1, slice(P, DV), r_total, "turned_sinks")
         finish(1, slice(0, P), r_total, "turned_v00")

@@ -25,16 +25,17 @@ PASSES = D // (P * PACK)
 COLS = N // 16
 SCALE_ROWS = P - QUAD
 PADDED = N + 8
-STAGE = 4 * SEG
 LINE = 64
+KIB = 1024
 
-KS_AT = STAGE
-Q0_AT = 3 * STAGE
-V_PAIR_AT = 5 * STAGE
-VS_AT = 7 * STAGE
-KW_AT = 9 * STAGE
-PROBS1_AT = 12 * STAGE
-Q1_AT = (KS_AT - STAGE // 4, KS_AT + STAGE // 4)
+KS_AT = 3 * KIB // 2
+Q1_AT = 12 * KIB
+V10_AT = 3 * KIB
+VS_AT = 18 * KIB
+V1_AT = 25 * KIB
+VS_COL0_AT = 34 * KIB
+VS_COL1_AT = 38 * KIB
+VS_GOT_AT = (40 * KIB, 44 * KIB)
 
 
 def tile_attend_sink_seg_kernel(tc, qT, k_words, k_scales, vT, vs, sink, offs, out):
@@ -58,17 +59,20 @@ def tile_attend_sink_seg_kernel(tc, qT, k_words, k_scales, vT, vs, sink, offs, o
         def seg(i):
             return slice(i * SEG, (i + 1) * SEG)
 
-        def listed(window, b):
-            return window[:, 0 : (b + 1) * SEG].indirect(offsets[:, b * COLS : (b + 1) * COLS])
+        def entries(b):
+            return offsets[:, b * COLS : (b + 1) * COLS]
 
         ks_pool = placed("ks_pool", [P, T // 4], I32, KS_AT)
         vs_pool = placed("vs_pool", [P, T], F32, VS_AT)
-        kw_pool = placed("kw_pool", [P, T], I32, KW_AT)
-        v_pair = placed("v_pair", [P, T], F32, V_PAIR_AT)
-        v_late = placed("v_late", [P, SEG], F32, VS_AT)
-        v_bf = sb("v_bf", [P, 3 * SEG], BF16)
-        q_raw0 = placed("q_raw0", [P, PASSES, PACK * NQ], F32, Q0_AT)
-        q_raw1 = [placed("q_raw1%d" % o, [P, PACK * NQ], F32, Q1_AT[o]) for o in range(PASSES)]
+        kw_pool = sb("kw_pool", [P, T], I32)
+        v_first = sb("v_first", [P, SEG], F32)
+        v_mid = placed("v_mid", [P, T], F32, V10_AT)
+        v_last = placed("v_last", [P, T], F32, V1_AT)
+        v_pool = {(0, 0): v_first, (1, 0): v_mid, (0, 1): v_last, (1, 1): v_last}
+        q_raw = [
+            sb("q_raw0", [P, PASSES, PACK * NQ], F32),
+            placed("q_raw1", [P, PASSES, PACK * NQ], F32, Q1_AT),
+        ]
         sink_rows = sb("sink_rows", [P, NQ], F32)
         ident = sb("ident", [P, P], F32)
         neg_all = sb("neg_all", [P, B, PADDED], F32)
@@ -85,47 +89,42 @@ def tile_attend_sink_seg_kernel(tc, qT, k_words, k_scales, vT, vs, sink, offs, o
 
         ks_got = sb("ks_got", [P, B * N], U8)
         kw_got = [sb("kw_got%d" % b, [P, N], U32) for b in range(B)]
-        k_codes = [
-            placed("k_codes0", [P, PASSES, 2 * N], U8, Q0_AT + 3 * STAGE // 4),
-            sb("k_codes1", [P, PASSES, 2 * N], U8),
-        ]
-        vs_col = [sb("vs_col0", [P, 8], F32), placed("vs_col1", [P, 8], F32, KW_AT)]
+        k_codes = [sb("k_codes%d" % b, [P, PASSES, 2 * N], U8) for b in range(B)]
+        vs_got = [placed("vs_got%d" % b, [P, N], F32, VS_GOT_AT[b]) for b in range(B)]
+        vs_col = [placed("vs_col0", [P, 8], F32, VS_COL0_AT), placed("vs_col1", [P, 2 * LINE // 4], F32, VS_COL1_AT)]
         q_bf = [sb("q_bf%d" % b, [P, PASSES * NQ * PACK], BF16) for b in range(B)]
         q_codes = [sb("q_codes%d" % b, [P, PASSES * NQ], U32) for b in range(B)]
         q_scales = [sb("q_scales%d" % b, [P, PASSES * NQ], U8) for b in range(B)]
-        v_scales = {(b, h): sb("v_scales%d%d" % (b, h), [P, P], U8) for b in range(B) for h in range(DV // P)}
-        v_codes = {(b, h): sb("v_codes%d%d" % (b, h), [P, P], U32) for b in range(B) for h in range(DV // P)}
+        tiles = [(b, h) for b in range(B) for h in range(DV // P)]
+        v_got = {(b, h): sb("v_got%d%d" % (b, h), [P, N], BF16) for b, h in tiles}
+        v_in = {(b, h): sb("v_in%d%d" % (b, h), [P, PACK * P], BF16) for b, h in tiles[1:]}
+        v_in.setdefault((0, 0), placed("v_in00", [P, PACK * P], BF16, Q1_AT))
+        v_scales = {(b, h): sb("v_scales%d%d" % (b, h), [P, P], U8) for b, h in tiles}
+        v_codes = {
+            (0, 1): placed("v_codes01", [P, P], U32, VS_COL1_AT + LINE),
+            (1, 1): placed("v_codes11", [P, P], U32, VS_COL1_AT + LINE - 4 * P),
+        }
+        v_codes.setdefault((0, 0), placed("v_codes00", [P, P], U32, Q1_AT + KIB))
+        v_codes.setdefault((1, 0), placed("v_codes10", [P, P], U32, VS_GOT_AT[0] + KIB // 2))
         total = sb("total", [P, B], F32)
-        w_bf = [placed("w_bf0", [P, PACK * NQ], BF16, VS_AT + STAGE // 4), sb("w_bf1", [P, PACK * NQ], BF16)]
-        w_codes = [placed("w_codes0", [P, NQ], U32, PROBS1_AT), sb("w_codes1", [P, NQ], U32)]
+        r_total = placed("r_total", [P, B], F32, VS_COL0_AT)
+        neg_m = [sb("neg_m0", [P, 1], F32)[:], v_got[0, 1][:].bitcast(F32)[:, N // 2 - 1 : N // 2]]
+        probs = [placed("probs0", [P, PADDED], F32, VS_GOT_AT[1]), sb("probs1", [P, PADDED], F32)]
+        w_bf = [sb("w_bf0", [P, PACK * NQ], BF16), placed("w_bf1", [P, PACK * NQ], BF16, VS_GOT_AT[0] + KIB)]
+        w_codes = [placed("w_codes0", [P, NQ], U32, VS_GOT_AT[0]), sb("w_codes1", [P, NQ], U32)]
         w_scales = [sb("w_scales%d" % b, [P, NQ], U8) for b in range(B)]
         scores = [bank("scores%d" % b, [P, N]) for b in range(B)]
         turned_p = [bank("turned_p%d" % b, [P, PACK, NQ]) for b in range(B)]
-        v_raw = {(0, 0): v_pair[:, 0:SEG], (0, 1): v_pair[:, SEG:T], (1, 0): v_late[:], (1, 1): v_pair[:, SEG:T]}
-        cast_at = {(0, 0): 0, (1, 0): 1, (0, 1): 2}
-        vs_got = sb("vs_got", [P, B * N], F32)
-        v_words, turned_v, v_in, neg_m = {}, {}, {}, {}
-
-        def load_key_scales():
-            nc.sync.dma_start(ks_pool[SCALE_ROWS:P, :], ks_hbm.rearrange("o f t -> f o t"))
-
-        def load_kw(b):
-            nc.sync.dma_start(kw_pool[:, seg(b)], kw_hbm[:, seg(b)])
+        turned_v = {}
 
         def q_hbm(b):
             return qT[b].rearrange("(o p j) q -> p o (j q)", o=PASSES, j=PACK)
 
-        def load_q0():
-            nc.sync.dma_start(q_raw0[:], q_hbm(0))
-
-        def load_q1(o):
-            nc.sync.dma_start(q_raw1[o][:], q_hbm(1)[:, o, :])
+        def load_kw(b):
+            nc.sync.dma_start(kw_pool[:, seg(b)], kw_hbm[:, seg(b)])
 
         def load_v(b, h):
-            nc.sync.dma_start(v_raw[b, h], vT[h * P : (h + 1) * P, seg(b)])
-
-        def load_sinks():
-            nc.sync.dma_start(sink_rows[P - B : P, :], sink.rearrange("b q o -> b (q o)"))
+            nc.sync.dma_start(v_pool[b, h][:, seg(b)], vT[h * P : (h + 1) * P, seg(b)])
 
         def gather_ks():
             nc.vector.tensor_copy(ks_got[:], ks_pool[:].bitcast(U8).indirect(offsets[:]))
@@ -136,29 +135,28 @@ def tile_attend_sink_seg_kernel(tc, qT, k_words, k_scales, vT, vs, sink, offs, o
                 nc.sync.dma_start(k_planes[QUAD * quad : QUAD * quad + 4, :], rows)
 
         def gather_kw(b):
-            nc.vector.tensor_copy(kw_got[b][:], listed(kw_pool[:].bitcast(U32), b))
+            window = kw_pool[:].bitcast(U32)[:, 0 : (b + 1) * SEG]
+            nc.vector.tensor_copy(kw_got[b][:], window.indirect(entries(b)))
 
         def part_kw(b):
             nc.vector.tensor_copy(
                 k_codes[b][:].bitcast(U16), kw_got[b][:].bitcast(U16).rearrange("p (s o) -> p o s", o=PASSES)
             )
 
-        def gather_vs():
-            nc.vector.tensor_copy(vs_got[:], vs_pool[:].indirect(offsets[:]))
+        def gather_vs(b):
+            nc.scalar.activation(vs_got[b][:], vs_pool[:].indirect(entries(b)), ACT.Copy)
 
         def deal_vs(b):
-            nc.sync.dma_start(vs_col[b][:, 0:PACK], vs_got[P - 1 : P, b * N : (b + 1) * N])
+            nc.sync.dma_start(vs_col[b][:, 0:PACK], vs_got[b][P - 1 : P, :])
 
-        def group_q0():
-            nc.scalar.copy(
-                q_bf[0][:].rearrange("p (o c i j) -> p o c j i", o=PASSES, i=4, j=PACK),
-                q_raw0[:].rearrange("p o (j c i) -> p o c j i", j=PACK, i=4),
-            )
+        def load_q(b, o):
+            nc.sync.dma_start(q_raw[b][:, o, :], q_hbm(b)[:, o, :])
 
-        def group_q1(o):
-            nc.scalar.copy(
-                q_bf[1][:, o * PACK * NQ : (o + 1) * PACK * NQ].rearrange("p (c i j) -> p c j i", i=4, j=PACK),
-                q_raw1[o][:].rearrange("p (j c i) -> p c j i", j=PACK, i=4),
+        def group_q(b, o):
+            nc.scalar.activation(
+                q_bf[b][:, o * PACK * NQ : (o + 1) * PACK * NQ].rearrange("p (c i j) -> p c j i", i=4, j=PACK),
+                q_raw[b][:, o, :].rearrange("p (j c i) -> p c j i", j=PACK, i=4),
+                ACT.Copy,
             )
 
         def quant_q(b, first, last):
@@ -182,33 +180,25 @@ def tile_attend_sink_seg_kernel(tc, qT, k_words, k_scales, vT, vs, sink, offs, o
                     stop=(o == PASSES - 1),
                 )
 
-        def cast_v_scalar(b, h):
-            nc.scalar.activation(v_bf[:, seg(cast_at[b, h])], v_raw[b, h], ACT.Copy)
-
-        def cast_v_vector(b, h):
-            nc.vector.tensor_copy(v_bf[:, seg(cast_at[b, h])], v_raw[b, h])
-
-        def gather_v_scalar(b, h, got, part=0, parts=1):
-            dealt = got.rearrange("p (u s j) -> p s u j", u=2, j=2)[:, part * P // parts : (part + 1) * P // parts]
-            window = v_bf[:, (cast_at[b, h] - b) * SEG : (cast_at[b, h] + 1) * SEG]
+        def gather_v_scalar(b, h, part=0, parts=1):
             first = b * COLS + part * COLS // parts
-            nc.scalar.activation(dealt, window.indirect(offsets[:, first : first + COLS // parts]), ACT.Copy)
-            words = got.bitcast(F32)
-            v_words.setdefault((b, h), [words[:, u * P : (u + 1) * P] for u in range(2)])
+            nc.scalar.activation(
+                v_got[b, h][:, part * N // parts : (part + 1) * N // parts],
+                v_pool[b, h][:].indirect(offsets[:, first : first + COLS // parts]),
+                ACT.Copy,
+            )
 
-        def gather_v_vector(b, h, got):
-            nc.vector.tensor_copy(got, listed(v_pair[:], b))
-            words = got.bitcast(F32)
-            v_words.setdefault((b, h), [words[:, u : 2 * P : 2] for u in range(2)])
+        def gather_v_vector(b, h):
+            nc.vector.tensor_copy(v_got[b, h][:], v_pool[b, h][:].indirect(entries(b)))
 
         def turn_v(b, h, tag=None):
             turned_v.setdefault((b, h), bank("turned_v%d%d" % (b, h), [P, 2, P], tag)[:])
+            words = v_got[b, h][:].bitcast(F32)
             for u in range(2):
-                nc.tensor.transpose(turned_v[b, h][:, u, :], v_words[b, h][u], ident[:])
+                nc.tensor.transpose(turned_v[b, h][:, u, :], words[:, u : 2 * P : 2], ident[:])
 
-        def weave_v(b, h, tile):
-            v_in.setdefault((b, h), tile)
-            nc.scalar.copy(
+        def weave_v(b, h, copy):
+            copy(
                 v_in[b, h][:].bitcast(F32).rearrange("p (e u) -> p e u", u=2),
                 turned_v[b, h].rearrange("p u e -> p e u"),
             )
@@ -221,8 +211,7 @@ def tile_attend_sink_seg_kernel(tc, qT, k_words, k_scales, vT, vs, sink, offs, o
             nc.tensor.transpose(turned[:], sink_rows[:], ident[:])
             nc.scalar.activation(neg_all[:, :, N], turned[:, P - B : P], ACT.Copy, scale=-1.0)
 
-        def row_max(b, column):
-            neg_m.setdefault(b, column)
+        def row_max(b):
             nc.vector.tensor_scalar(
                 neg_all[:, b, 0:N].rearrange("p (t s) -> p t s", t=PACK),
                 scores[b][:].rearrange("p (s t) -> p t s", t=PACK),
@@ -233,9 +222,9 @@ def tile_attend_sink_seg_kernel(tc, qT, k_words, k_scales, vT, vs, sink, offs, o
                 accum_out=neg_m[b],
             )
 
-        def exponentials(b, probs):
+        def exponentials(b):
             nc.scalar.activation(
-                probs[:, 0 : N + 1],
+                probs[b][:, 0 : N + 1],
                 neg_all[:, b, 0 : N + 1],
                 ACT.Exp,
                 bias=neg_m[b],
@@ -243,7 +232,7 @@ def tile_attend_sink_seg_kernel(tc, qT, k_words, k_scales, vT, vs, sink, offs, o
                 accum_out=total[:, b : b + 1],
             )
             for t in range(PACK):
-                nc.tensor.transpose(turned_p[b][:, t, :], probs[:, t * P : (t + 1) * P], ident[:])
+                nc.tensor.transpose(turned_p[b][:, t, :], probs[b][:, t * P : (t + 1) * P], ident[:])
 
         def weigh(b):
             nc.vector.tensor_tensor(
@@ -256,92 +245,87 @@ def tile_attend_sink_seg_kernel(tc, qT, k_words, k_scales, vT, vs, sink, offs, o
         def quant_w(b):
             nc.vector.quantize_mx(w_codes[b][:].bitcast(FP8X4), w_scales[b][:], w_bf[b][:])
 
-        def finish(b, cols, r_total, tag):
-            width = cols.stop - cols.start
-            sums = bank("sums%d_%d" % (b, cols.start), [P, width], tag)
-            result = sb("result%d_%d" % (b, cols.start), [P, width], F32)
-            for h in range(cols.start // P, cols.stop // P):
-                nc.tensor.matmul_mx(
-                    sums[:, h * P - cols.start : (h + 1) * P - cols.start],
-                    lhsT=w_codes[b][:].bitcast(FP8X4),
-                    lhsT_scale=w_scales[b][:],
-                    rhs=v_codes[b, h][:].bitcast(FP8X4),
-                    rhs_scale=v_scales[b, h][:],
-                    start=True,
-                    stop=True,
-                )
-            nc.scalar.activation(result[:], sums[:], ACT.Copy, scale=r_total[:, b : b + 1])
-            nc.sync.dma_start(out[b][:, cols], result[:])
+        def finish(b, h, tag, on_vector=False):
+            sums = bank("sums%d%d" % (b, h), [P, P], tag)
+            result = sb("result%d%d" % (b, h), [P, P], F32)
+            nc.tensor.matmul_mx(
+                sums[:],
+                lhsT=w_codes[b][:].bitcast(FP8X4),
+                lhsT_scale=w_scales[b][:],
+                rhs=v_codes[b, h][:].bitcast(FP8X4),
+                rhs_scale=v_scales[b, h][:],
+                start=True,
+                stop=True,
+            )
+            if on_vector:
+                nc.vector.tensor_scalar(result[:], sums[:], r_total[:, b : b + 1], None, ALU.mult)
+            else:
+                nc.scalar.activation(result[:], sums[:], ACT.Copy, scale=r_total[:, b : b + 1])
+            nc.sync.dma_start(out[b][:, h * P : (h + 1) * P], result[:])
 
-        load_key_scales()
+        nc.sync.dma_start(ks_pool[SCALE_ROWS:P, :], ks_hbm.rearrange("o f t -> f o t"))
         nc.sync.dma_start(offsets[:], offs)
-        load_v(0, 0)
+        load_q(0, 0)
+        load_q(0, 1)
         nc.sync.dma_start(vs_pool[P - 1 : P, :], vs[0:1, :])
         load_kw(0)
-        load_q0()
-        load_v(0, 1)
+        nc.sync.dma_start(sink_rows[P - B : P, :], sink.rearrange("b q o -> b (q o)"))
         load_kw(1)
-        load_sinks()
+        load_v(0, 0)
+        nc.sync.dma_start(q_raw[1][:], q_hbm(1))
 
+        group_q(0, 0)
+        group_q(0, 1)
         gather_ks()
         move_ks()
-        load_q1(0)
-        load_q1(1)
-        cast_v_scalar(0, 0)
-        gather_v_scalar(0, 0, sb("v_got00", [P, N], BF16)[:])
-        turn_v(0, 0)
-        gather_vs()
         load_v(1, 0)
+        nc.gpsimd.memset(v_mid[:, seg(0)], 0.0)
+        gather_vs(1)
+        gather_vs(0)
+        deal_vs(1)
+        load_v(0, 1)
+        load_v(1, 1)
         deal_vs(0)
 
         gather_kw(0)
-        group_q0()
-        cast_v_scalar(0, 1)
-        load_v(1, 1)
-        weave_v(0, 0, placed("v_in00", [P, PACK * P], BF16, Q0_AT))
-        gather_v_scalar(0, 1, sb("v_got01", [P, N], BF16)[:])
         quant_q(0, 0, PASSES)
         part_kw(0)
+        negate_sinks()
+        gather_v_scalar(0, 0)
+        turn_v(0, 0, "turned_sinks")
         score(0, 0, PASSES)
         gather_kw(1)
-        deal_vs(1)
-        quant_v(0, 0)
+        group_q(1, 0)
+        group_q(1, 1)
+        weave_v(0, 0, nc.scalar.copy)
         part_kw(1)
-        negate_sinks()
-
-        group_q1(0)
-        group_q1(1)
         quant_q(1, 0, 1)
         score(1, 0, 1)
-        row_max(0, placed("neg_m0", [P, 1], F32, Q1_AT[0])[:])
         quant_q(1, 1, 2)
         score(1, 1, 2)
-        exponentials(0, placed("probs0", [P, PADDED], F32, VS_AT + STAGE))
-
-        cast_v_vector(1, 0)
-        v_got10 = placed("v_got10", [P, N // 2], F32, VS_AT)
-        row_max(1, v_got10[:, N // 2 - 1 : N // 2])
-        gather_v_scalar(1, 0, v_got10[:].bitcast(BF16), 0, 2)
-
-        turn_v(0, 1, "scores1")
-        exponentials(1, placed("probs1", [P, PADDED], F32, PROBS1_AT))
-        gather_v_scalar(1, 0, v_got10[:].bitcast(BF16), 1, 2)
+        row_max(0)
+        quant_v(0, 0)
+        gather_v_scalar(1, 0)
+        turn_v(1, 0)
+        exponentials(0)
+        row_max(1)
+        weave_v(1, 0, nc.scalar.copy)
+        exponentials(1)
+        gather_v_vector(1, 1)
+        gather_v_scalar(0, 1)
+        turn_v(1, 1)
+        turn_v(0, 1)
         weigh(0)
-        gather_v_vector(1, 1, placed("v_got11", [P, N], BF16, VS_AT + 7 * STAGE // 8)[:])
-        turn_v(1, 1, "turned_p0")
         weigh(1)
-        weave_v(0, 1, placed("v_in01", [P, PACK * P], BF16, PROBS1_AT + STAGE // 4))
-        turn_v(1, 0, "scores1")
-        weave_v(1, 1, sb("v_in11", [P, PACK * P], BF16))
-        weave_v(1, 0, sb("v_in10", [P, PACK * P], BF16))
         quant_w(0)
-        r_total = placed("r_total", [P, B], F32, PROBS1_AT + STAGE // 8)
         nc.vector.reciprocal(r_total[:], total[:])
-        quant_v(0, 1)
+        weave_v(1, 1, nc.scalar.copy)
+        weave_v(0, 1, nc.scalar.copy)
+        quant_v(1, 0)
         quant_w(1)
         quant_v(1, 1)
-        quant_v(1, 0)
-
-        finish(0, slice(0, DV), r_total, "scores0")
-        finish(1, slice(P, DV), r_total, "turned_sinks")
-        finish(1, slice(0, P), r_total, "turned_v00")
+        quant_v(0, 1)
+        finish(0, 0, "scores0")
+        finish(1, 0, "scores1")
+        finish(1, 1, "turned_p0")
+        finish(0, 1, "turned_p1", True)

@@ -28,14 +28,15 @@ PADDED = N + 8
 LINE = 64
 KIB = 1024
 
-KS_AT = 3 * KIB // 2
-Q1_AT = 12 * KIB
-V10_AT = 3 * KIB
-VS_AT = 18 * KIB
-V1_AT = 25 * KIB
-VS_COL0_AT = 34 * KIB
-VS_COL1_AT = 38 * KIB
-VS_GOT_AT = (40 * KIB, 44 * KIB)
+Q1_AT = 3 * KIB // 2
+KS_AT = 3 * KIB
+V10_AT = 4 * KIB
+VS_AT = 12 * KIB
+V1_AT = 19 * KIB
+VS_COL0_AT = 28 * KIB
+Q10_AT = 44 * KIB
+VS_COL1_AT = 30 * KIB
+NEG_M1_AT = 36 * KIB
 
 
 def tile_attend_sink_seg_kernel(tc, qT, k_words, k_scales, vT, vs, sink, offs, out):
@@ -69,19 +70,20 @@ def tile_attend_sink_seg_kernel(tc, qT, k_words, k_scales, vT, vs, sink, offs, o
         v_mid = placed("v_mid", [P, T], F32, V10_AT)
         v_last = placed("v_last", [P, T], F32, V1_AT)
         v_pool = {(0, 0): v_first, (1, 0): v_mid, (0, 1): v_last, (1, 1): v_last}
-        q_raw = [
-            sb("q_raw0", [P, PASSES, PACK * NQ], F32),
-            placed("q_raw1", [P, PASSES, PACK * NQ], F32, Q1_AT),
-        ]
+        q_first = sb("q_first", [P, PASSES, PACK * NQ], F32)
+        q_raw = {(0, o): q_first[:, o, :] for o in range(PASSES)}
+        q_raw.setdefault((1, 0), placed("q_raw10", [P, PACK * NQ], F32, Q10_AT)[:])
+        q_raw.setdefault((1, 1), placed("q_raw11", [P, PACK * NQ], F32, Q1_AT)[:])
         sink_rows = sb("sink_rows", [P, NQ], F32)
         ident = sb("ident", [P, P], F32)
         neg_all = sb("neg_all", [P, B, PADDED], F32)
         k_planes = sb("k_planes", [P, PASSES * B * N // 4], I32)
 
+        nc.gpsimd.memset(ident[:], 0.0)
+        nc.scalar.activation(sink_rows[0 : P - B, :], ident[0 : P - B, :], ACT.Copy)
+        make_identity(nc, ident[:], nomemset=True)
         nc.gpsimd.memset(ks_pool[0:SCALE_ROWS, :], 0)
         nc.vector.memset(vs_pool[0 : P - 1, :], 0.0)
-        make_identity(nc, ident[:])
-        nc.gpsimd.memset(sink_rows[0 : P - B, :], 0.0)
         nc.gpsimd.memset(k_planes[:], 0)
 
         kw_hbm = k_words[0].rearrange("p t c -> p (t c)").bitcast(I32)
@@ -89,29 +91,29 @@ def tile_attend_sink_seg_kernel(tc, qT, k_words, k_scales, vT, vs, sink, offs, o
 
         ks_got = sb("ks_got", [P, B * N], U8)
         kw_got = [sb("kw_got%d" % b, [P, N], U32) for b in range(B)]
-        k_codes = [sb("k_codes%d" % b, [P, PASSES, 2 * N], U8) for b in range(B)]
-        vs_got = [placed("vs_got%d" % b, [P, N], F32, VS_GOT_AT[b]) for b in range(B)]
-        vs_col = [placed("vs_col0", [P, 8], F32, VS_COL0_AT), placed("vs_col1", [P, 2 * LINE // 4], F32, VS_COL1_AT)]
+        k_codes = [sb("k_codes0", [P, PASSES, 2 * N], U8), placed("k_codes1", [P, PASSES, 2 * N], U8, Q10_AT)]
+        vs_got = sb("vs_got", [P, B * N], F32)
+        vs_col = [placed("vs_col0", [P, 2 * LINE // 4], F32, VS_COL0_AT), placed("vs_col1", [P, 2 * LINE // 4], F32, VS_COL1_AT)]
         q_bf = [sb("q_bf%d" % b, [P, PASSES * NQ * PACK], BF16) for b in range(B)]
         q_codes = [sb("q_codes%d" % b, [P, PASSES * NQ], U32) for b in range(B)]
         q_scales = [sb("q_scales%d" % b, [P, PASSES * NQ], U8) for b in range(B)]
         tiles = [(b, h) for b in range(B) for h in range(DV // P)]
-        v_got = {(b, h): sb("v_got%d%d" % (b, h), [P, N], BF16) for b, h in tiles}
-        v_in = {(b, h): sb("v_in%d%d" % (b, h), [P, PACK * P], BF16) for b, h in tiles[1:]}
+        v_got = {(b, h): sb("v_got%d%d" % (b, h), [P, N], BF16) for b, h in tiles[:-1]}
+        v_got.setdefault((1, 1), placed("v_got11", [P, N], BF16, NEG_M1_AT))
+        v_in = {(b, h): sb("v_in%d%d" % (b, h), [P, PACK * P], BF16) for b, h in tiles[3:]}
+        v_in.setdefault((1, 0), placed("v_in10", [P, PACK * P], BF16, V1_AT + 3 * KIB))
         v_in.setdefault((0, 0), placed("v_in00", [P, PACK * P], BF16, Q1_AT))
+        v_in.setdefault((0, 1), placed("v_in01", [P, PACK * P], BF16, V1_AT + 2 * KIB))
         v_scales = {(b, h): sb("v_scales%d%d" % (b, h), [P, P], U8) for b, h in tiles}
-        v_codes = {
-            (0, 1): placed("v_codes01", [P, P], U32, VS_COL1_AT + LINE),
-            (1, 1): placed("v_codes11", [P, P], U32, VS_COL1_AT + LINE - 4 * P),
-        }
-        v_codes.setdefault((0, 0), placed("v_codes00", [P, P], U32, Q1_AT + KIB))
-        v_codes.setdefault((1, 0), placed("v_codes10", [P, P], U32, VS_GOT_AT[0] + KIB // 2))
+        v_codes = {(0, 0): sb("v_codes00", [P, P], U32), (1, 0): placed("v_codes10", [P, P], U32, VS_COL0_AT + LINE)}
+        v_codes.setdefault((0, 1), placed("v_codes01", [P, P], U32, VS_COL1_AT + LINE))
+        v_codes.setdefault((1, 1), placed("v_codes11", [P, P], U32, VS_COL1_AT + LINE - 4 * P))
         total = sb("total", [P, B], F32)
         r_total = placed("r_total", [P, B], F32, VS_COL0_AT)
-        neg_m = [sb("neg_m0", [P, 1], F32)[:], v_got[0, 1][:].bitcast(F32)[:, N // 2 - 1 : N // 2]]
-        probs = [placed("probs0", [P, PADDED], F32, VS_GOT_AT[1]), sb("probs1", [P, PADDED], F32)]
-        w_bf = [sb("w_bf0", [P, PACK * NQ], BF16), placed("w_bf1", [P, PACK * NQ], BF16, VS_GOT_AT[0] + KIB)]
-        w_codes = [placed("w_codes0", [P, NQ], U32, VS_GOT_AT[0]), sb("w_codes1", [P, NQ], U32)]
+        neg_m = [placed("neg_m0", [P, 1], F32, Q1_AT + KIB), sb("neg_m1", [P, 1], F32)]
+        probs = [sb("probs0", [P, PADDED], F32), sb("probs1", [P, PADDED], F32)]
+        w_bf = [sb("w_bf%d" % b, [P, PACK * NQ], BF16) for b in range(B)]
+        w_codes = [sb("w_codes%d" % b, [P, NQ], U32) for b in range(B)]
         w_scales = [sb("w_scales%d" % b, [P, NQ], U8) for b in range(B)]
         scores = [bank("scores%d" % b, [P, N]) for b in range(B)]
         turned_p = [bank("turned_p%d" % b, [P, PACK, NQ]) for b in range(B)]
@@ -130,7 +132,7 @@ def tile_attend_sink_seg_kernel(tc, qT, k_words, k_scales, vT, vs, sink, offs, o
             nc.vector.tensor_copy(ks_got[:], ks_pool[:].bitcast(U8).indirect(offsets[:]))
 
         def move_ks():
-            for quad in range(P // QUAD):
+            for quad in (0, 2, 1, 3):
                 rows = ks_got[:].bitcast(I32)[SCALE_ROWS + 8 * quad : SCALE_ROWS + 8 * (quad + 1), :]
                 nc.sync.dma_start(k_planes[QUAD * quad : QUAD * quad + 4, :], rows)
 
@@ -138,24 +140,23 @@ def tile_attend_sink_seg_kernel(tc, qT, k_words, k_scales, vT, vs, sink, offs, o
             window = kw_pool[:].bitcast(U32)[:, 0 : (b + 1) * SEG]
             nc.vector.tensor_copy(kw_got[b][:], window.indirect(entries(b)))
 
-        def part_kw(b):
-            nc.vector.tensor_copy(
-                k_codes[b][:].bitcast(U16), kw_got[b][:].bitcast(U16).rearrange("p (s o) -> p o s", o=PASSES)
-            )
+        def part_kw(b, first, last):
+            halves = kw_got[b][:].bitcast(U16).rearrange("p (s o) -> p o s", o=PASSES)
+            nc.vector.tensor_copy(k_codes[b][:].bitcast(U16)[:, first:last, :], halves[:, first:last, :])
 
-        def gather_vs(b):
-            nc.scalar.activation(vs_got[b][:], vs_pool[:].indirect(entries(b)), ACT.Copy)
+        def gather_vs():
+            nc.scalar.activation(vs_got[:], vs_pool[:].indirect(offsets[:]), ACT.Copy)
 
         def deal_vs(b):
-            nc.sync.dma_start(vs_col[b][:, 0:PACK], vs_got[b][P - 1 : P, :])
+            nc.sync.dma_start(vs_col[b][:, 0:PACK], vs_got[P - 1 : P, b * N : (b + 1) * N])
 
         def load_q(b, o):
-            nc.sync.dma_start(q_raw[b][:, o, :], q_hbm(b)[:, o, :])
+            nc.sync.dma_start(q_raw[b, o], q_hbm(b)[:, o, :])
 
         def group_q(b, o):
             nc.scalar.activation(
                 q_bf[b][:, o * PACK * NQ : (o + 1) * PACK * NQ].rearrange("p (c i j) -> p c j i", i=4, j=PACK),
-                q_raw[b][:, o, :].rearrange("p (j c i) -> p c j i", j=PACK, i=4),
+                q_raw[b, o].rearrange("p (j c i) -> p c j i", j=PACK, i=4),
                 ACT.Copy,
             )
 
@@ -180,13 +181,8 @@ def tile_attend_sink_seg_kernel(tc, qT, k_words, k_scales, vT, vs, sink, offs, o
                     stop=(o == PASSES - 1),
                 )
 
-        def gather_v_scalar(b, h, part=0, parts=1):
-            first = b * COLS + part * COLS // parts
-            nc.scalar.activation(
-                v_got[b, h][:, part * N // parts : (part + 1) * N // parts],
-                v_pool[b, h][:].indirect(offsets[:, first : first + COLS // parts]),
-                ACT.Copy,
-            )
+        def gather_v_scalar(b, h):
+            nc.scalar.activation(v_got[b, h][:], v_pool[b, h][:].indirect(entries(b)), ACT.Copy)
 
         def gather_v_vector(b, h):
             nc.vector.tensor_copy(v_got[b, h][:], v_pool[b, h][:].indirect(entries(b)))
@@ -207,7 +203,7 @@ def tile_attend_sink_seg_kernel(tc, qT, k_words, k_scales, vT, vs, sink, offs, o
             nc.vector.quantize_mx(v_codes[b, h][:].bitcast(FP8X4), v_scales[b, h][:], v_in[b, h][:])
 
         def negate_sinks():
-            turned = bank("turned_sinks", [P, P])
+            turned = bank("turned_sinks", [P, P], "turned_v00")
             nc.tensor.transpose(turned[:], sink_rows[:], ident[:])
             nc.scalar.activation(neg_all[:, :, N], turned[:, P - B : P], ACT.Copy, scale=-1.0)
 
@@ -219,7 +215,7 @@ def tile_attend_sink_seg_kernel(tc, qT, k_words, k_scales, vT, vs, sink, offs, o
                 neg_all[:, b, N : N + 1],
                 ALU.mult,
                 ALU.min,
-                accum_out=neg_m[b],
+                accum_out=neg_m[b][:],
             )
 
         def exponentials(b):
@@ -227,7 +223,7 @@ def tile_attend_sink_seg_kernel(tc, qT, k_words, k_scales, vT, vs, sink, offs, o
                 probs[b][:, 0 : N + 1],
                 neg_all[:, b, 0 : N + 1],
                 ACT.Exp,
-                bias=neg_m[b],
+                bias=neg_m[b][:],
                 scale=-1.0,
                 accum_out=total[:, b : b + 1],
             )
@@ -247,7 +243,7 @@ def tile_attend_sink_seg_kernel(tc, qT, k_words, k_scales, vT, vs, sink, offs, o
 
         def finish(b, h, tag, on_vector=False):
             sums = bank("sums%d%d" % (b, h), [P, P], tag)
-            result = sb("result%d%d" % (b, h), [P, P], F32)
+            result = placed("result%d%d" % (b, h), [P, P], F32, NEG_M1_AT + (2 * h + b) * KIB // 2)
             nc.tensor.matmul_mx(
                 sums[:],
                 lhsT=w_codes[b][:].bitcast(FP8X4),
@@ -265,42 +261,42 @@ def tile_attend_sink_seg_kernel(tc, qT, k_words, k_scales, vT, vs, sink, offs, o
 
         nc.sync.dma_start(ks_pool[SCALE_ROWS:P, :], ks_hbm.rearrange("o f t -> f o t"))
         nc.sync.dma_start(offsets[:], offs)
-        load_q(0, 0)
-        load_q(0, 1)
         nc.sync.dma_start(vs_pool[P - 1 : P, :], vs[0:1, :])
         load_kw(0)
         nc.sync.dma_start(sink_rows[P - B : P, :], sink.rearrange("b q o -> b (q o)"))
-        load_kw(1)
+        nc.sync.dma_start(q_first[:], q_hbm(0))
         load_v(0, 0)
-        nc.sync.dma_start(q_raw[1][:], q_hbm(1))
+        load_kw(1)
+        load_q(1, 0)
 
-        group_q(0, 0)
-        group_q(0, 1)
+        gather_vs()
+        negate_sinks()
         gather_ks()
         move_ks()
+        load_q(1, 1)
         load_v(1, 0)
         nc.gpsimd.memset(v_mid[:, seg(0)], 0.0)
-        gather_vs(1)
-        gather_vs(0)
-        deal_vs(1)
         load_v(0, 1)
         load_v(1, 1)
         deal_vs(0)
+        deal_vs(1)
 
         gather_kw(0)
+        part_kw(0, 0, PASSES)
+        group_q(0, 0)
+        group_q(0, 1)
         quant_q(0, 0, PASSES)
-        part_kw(0)
-        negate_sinks()
         gather_v_scalar(0, 0)
-        turn_v(0, 0, "turned_sinks")
+        turn_v(0, 0)
         score(0, 0, PASSES)
         gather_kw(1)
         group_q(1, 0)
         group_q(1, 1)
         weave_v(0, 0, nc.scalar.copy)
-        part_kw(1)
         quant_q(1, 0, 1)
+        part_kw(1, 0, 1)
         score(1, 0, 1)
+        part_kw(1, 1, 2)
         quant_q(1, 1, 2)
         score(1, 1, 2)
         row_max(0)
@@ -309,23 +305,23 @@ def tile_attend_sink_seg_kernel(tc, qT, k_words, k_scales, vT, vs, sink, offs, o
         turn_v(1, 0)
         exponentials(0)
         row_max(1)
-        weave_v(1, 0, nc.scalar.copy)
         exponentials(1)
-        gather_v_vector(1, 1)
-        gather_v_scalar(0, 1)
-        turn_v(1, 1)
+        gather_v_vector(0, 1)
         turn_v(0, 1)
         weigh(0)
+        gather_v_scalar(1, 1)
+        turn_v(1, 1)
+        weave_v(1, 0, nc.scalar.copy)
         weigh(1)
         quant_w(0)
-        nc.vector.reciprocal(r_total[:], total[:])
-        weave_v(1, 1, nc.scalar.copy)
-        weave_v(0, 1, nc.scalar.copy)
         quant_v(1, 0)
+        nc.vector.reciprocal(r_total[:], total[:])
+        weave_v(0, 1, nc.scalar.copy)
+        weave_v(1, 1, nc.scalar.copy)
         quant_w(1)
-        quant_v(1, 1)
         quant_v(0, 1)
+        quant_v(1, 1)
         finish(0, 0, "scores0")
-        finish(1, 0, "scores1")
-        finish(1, 1, "turned_p0")
-        finish(0, 1, "turned_p1", True)
+        finish(1, 0, "turned_v01")
+        finish(0, 1, "turned_v00")
+        finish(1, 1, "turned_p0", True)

@@ -209,8 +209,8 @@ def tile_attend_sink_seg_kernel(tc, qT, k_words, k_scales, vT, vs, sink, offs, o
 
         def row_max(b):
             nc.vector.tensor_scalar(
-                neg_all[:, b, 0:N].rearrange("p (t s) -> p t s", t=PACK),
-                scores[b][:].rearrange("p (s t) -> p t s", t=PACK),
+                neg_all[:, b, 0:N].rearrange("p (t s) -> p s t", t=PACK),
+                scores[b][:].rearrange("p (s t) -> p s t", t=PACK),
                 -1.0,
                 neg_all[:, b, N : N + 1],
                 ALU.mult,

@@ -276,8 +276,7 @@ def tile_attend_sink_seg_kernel(tc, qT, k_words, k_scales, vT, vs, sink, offs, o
         load_q(1, 1)
         load_v(1, 0)
         nc.gpsimd.memset(v_mid[:, seg(0)], 0.0)
-        load_v(0, 1)
-        load_v(1, 1)
+        nc.sync.dma_start(v_last[:], vT[P : 2 * P, :])
         deal_vs(0)
         deal_vs(1)
 

from contextlib import ExitStack

import concourse.mybir as mybir
from concourse.masks import make_identity

B, N, T, D, DV, NQ = 2, 512, 2048, 1024, 256, 128
FLOPS = 2 * B * NQ * N * (D + DV)

F32 = mybir.dt.float32
BF16 = mybir.dt.bfloat16
I32 = mybir.dt.int32
U32 = mybir.dt.uint32
U16 = mybir.dt.uint16
U8 = mybir.dt.uint8
FP8X4 = mybir.dt.float8_e4m3fn_x4
FP4X4 = mybir.dt.float4_e2m1fn_x4
ALU = mybir.AluOpType
ACT = mybir.ActivationFunctionType

P = 128
PACK = 4
QUAD = 32
SEG = T // B
PASSES = D // (P * PACK)
COLS = N // 16
SCALE_ROWS = P - QUAD
PADDED = N + 8
LINE = 64
KIB = 1024

Q1_AT = 3 * KIB // 2
KS_AT = 3 * KIB
V10_AT = 4 * KIB
VS_AT = 12 * KIB
V1_AT = 19 * KIB
VS_COL0_AT = 28 * KIB
Q10_AT = 44 * KIB
VS_COL1_AT = 30 * KIB
NEG_M1_AT = 36 * KIB


def tile_attend_sink_seg_kernel(tc, qT, k_words, k_scales, vT, vs, sink, offs, out):
    nc = tc.nc
    with ExitStack() as ctx:
        keep = ctx.enter_context(tc.tile_pool(name="keep", bufs=1))
        lent = ctx.enter_context(tc.tile_pool(name="lent", bufs=1))
        psum = ctx.enter_context(tc.psum_pool(name="psum", bufs=1))

        def sb(name, shape, dtype):
            return keep.tile(shape, dtype, name=name, tag=name, align_bytes=LINE)

        def placed(name, shape, dtype, offset):
            return lent.tile(shape, dtype, name=name, tag=name, align_bytes=LINE, offset=offset)

        def bank(name, shape, tag=None):
            return psum.tile(shape, F32, name=name, tag=tag or name)

        offsets = keep.tile([P, B * COLS], U16, name="offsets")

        def seg(i):
            return slice(i * SEG, (i + 1) * SEG)

        def entries(b):
            return offsets[:, b * COLS : (b + 1) * COLS]

        ks_pool = placed("ks_pool", [P, T // 4], I32, KS_AT)
        vs_pool = placed("vs_pool", [P, T], F32, VS_AT)
        kw_pool = sb("kw_pool", [P, T], I32)
        v_first = sb("v_first", [P, SEG], F32)
        v_mid = placed("v_mid", [P, T], F32, V10_AT)
        v_last = placed("v_last", [P, T], F32, V1_AT)
        v_pool = {(0, 0): v_first, (1, 0): v_mid, (0, 1): v_last, (1, 1): v_last}
        q_first = sb("q_first", [P, PASSES, PACK * NQ], F32)
        q_raw = {(0, o): q_first[:, o, :] for o in range(PASSES)}
        q_raw.setdefault((1, 0), placed("q_raw10", [P, PACK * NQ], F32, Q10_AT)[:])
        q_raw.setdefault((1, 1), placed("q_raw11", [P, PACK * NQ], F32, Q1_AT)[:])
        sink_rows = sb("sink_rows", [P, NQ], F32)
        ident = sb("ident", [P, P], F32)
        neg_all = sb("neg_all", [P, B, PADDED], F32)
        k_planes = sb("k_planes", [P, PASSES * B * N // 4], I32)

        nc.gpsimd.memset(ident[:], 0.0)
        nc.scalar.activation(sink_rows[0 : P - B, :], ident[0 : P - B, :], ACT.Copy)
        make_identity(nc, ident[:], nomemset=True)
        nc.gpsimd.memset(ks_pool[0:SCALE_ROWS, :], 0)
        nc.vector.memset(vs_pool[0 : P - 1, :], 0.0)
        nc.gpsimd.memset(k_planes[:], 0)

        kw_hbm = k_words[0].rearrange("p t c -> p (t c)").bitcast(I32)
        ks_hbm = k_scales.bitcast(I32)

        ks_got = sb("ks_got", [P, B * N], U8)
        kw_got = [sb("kw_got%d" % b, [P, N], U32) for b in range(B)]
        k_codes = [sb("k_codes0", [P, PASSES, 2 * N], U8), placed("k_codes1", [P, PASSES, 2 * N], U8, Q10_AT)]
        vs_got = sb("vs_got", [P, B * N], F32)
        vs_col = [placed("vs_col0", [P, 2 * LINE // 4], F32, VS_COL0_AT), placed("vs_col1", [P, 2 * LINE // 4], F32, VS_COL1_AT)]
        q_bf = [sb("q_bf%d" % b, [P, PASSES * NQ * PACK], BF16) for b in range(B)]
        q_codes = [sb("q_codes%d" % b, [P, PASSES * NQ], U32) for b in range(B)]
        q_scales = [sb("q_scales%d" % b, [P, PASSES * NQ], U8) for b in range(B)]
        tiles = [(b, h) for b in range(B) for h in range(DV // P)]
        v_got = {(b, h): sb("v_got%d%d" % (b, h), [P, N], BF16) for b, h in tiles[:-1]}
        v_got.setdefault((1, 1), placed("v_got11", [P, N], BF16, NEG_M1_AT))
        v_in = {(b, h): sb("v_in%d%d" % (b, h), [P, PACK * P], BF16) for b, h in tiles[3:]}
        v_in.setdefault((1, 0), placed("v_in10", [P, PACK * P], BF16, V1_AT + 3 * KIB))
        v_in.setdefault((0, 0), placed("v_in00", [P, PACK * P], BF16, Q1_AT))
        v_in.setdefault((0, 1), placed("v_in01", [P, PACK * P], BF16, V1_AT + 2 * KIB))
        v_scales = {(b, h): sb("v_scales%d%d" % (b, h), [P, P], U8) for b, h in tiles}
        v_codes = {(0, 0): sb("v_codes00", [P, P], U32), (1, 0): placed("v_codes10", [P, P], U32, VS_COL0_AT + LINE)}
        v_codes.setdefault((0, 1), placed("v_codes01", [P, P], U32, VS_COL1_AT + LINE))
        v_codes.setdefault((1, 1), placed("v_codes11", [P, P], U32, VS_COL1_AT + LINE - 4 * P))
        total = sb("total", [P, B], F32)
        r_total = placed("r_total", [P, B], F32, VS_COL0_AT)
        neg_m = [placed("neg_m0", [P, 1], F32, Q1_AT + KIB), sb("neg_m1", [P, 1], F32)]
        probs = [sb("probs0", [P, PADDED], F32), sb("probs1", [P, PADDED], F32)]
        w_bf = [sb("w_bf%d" % b, [P, PACK * NQ], BF16) for b in range(B)]
        w_codes = [sb("w_codes%d" % b, [P, NQ], U32) for b in range(B)]
        w_scales = [sb("w_scales%d" % b, [P, NQ], U8) for b in range(B)]
        scores = [bank("scores%d" % b, [P, N]) for b in range(B)]
        turned_p = [bank("turned_p%d" % b, [P, PACK, NQ]) for b in range(B)]
        turned_v = {}

        def q_hbm(b):
            return qT[b].rearrange("(o p j) q -> p o (j q)", o=PASSES, j=PACK)

        def load_kw(b):
            nc.sync.dma_start(kw_pool[:, seg(b)], kw_hbm[:, seg(b)])

        def load_v(b, h):
            nc.sync.dma_start(v_pool[b, h][:, seg(b)], vT[h * P : (h + 1) * P, seg(b)])

        def gather_ks():
            nc.vector.tensor_copy(ks_got[:], ks_pool[:].bitcast(U8).indirect(offsets[:]))

        def move_ks():
            for quad in (0, 2, 1, 3):
                rows = ks_got[:].bitcast(I32)[SCALE_ROWS + 8 * quad : SCALE_ROWS + 8 * (quad + 1), :]
                nc.sync.dma_start(k_planes[QUAD * quad : QUAD * quad + 4, :], rows)

        def gather_kw(b):
            window = kw_pool[:].bitcast(U32)[:, 0 : (b + 1) * SEG]
            nc.vector.tensor_copy(kw_got[b][:], window.indirect(entries(b)))

        def part_kw(b, first, last):
            halves = kw_got[b][:].bitcast(U16).rearrange("p (s o) -> p o s", o=PASSES)
            nc.vector.tensor_copy(k_codes[b][:].bitcast(U16)[:, first:last, :], halves[:, first:last, :])

        def gather_vs():
            nc.scalar.activation(vs_got[:], vs_pool[:].indirect(offsets[:]), ACT.Copy)

        def deal_vs(b):
            nc.sync.dma_start(vs_col[b][:, 0:PACK], vs_got[P - 1 : P, b * N : (b + 1) * N])

        def load_q(b, o):
            nc.sync.dma_start(q_raw[b, o], q_hbm(b)[:, o, :])

        def group_q(b, o):
            nc.scalar.activation(
                q_bf[b][:, o * PACK * NQ : (o + 1) * PACK * NQ].rearrange("p (c i j) -> p c j i", i=4, j=PACK),
                q_raw[b, o].rearrange("p (j c i) -> p c j i", j=PACK, i=4),
                ACT.Copy,
            )

        def quant_q(b, first, last):
            cols = slice(first * NQ, last * NQ)
            nc.vector.quantize_mx(
                q_codes[b][:, cols].bitcast(FP8X4),
                q_scales[b][:, cols],
                q_bf[b][:, PACK * cols.start : PACK * cols.stop],
            )

        def score(b, first, last):
            for o in range(first, last):
                cols = slice(o * NQ, (o + 1) * NQ)
                nc.tensor.matmul_mx(
                    scores[b][:],
                    lhsT=q_codes[b][:, cols].bitcast(FP8X4),
                    lhsT_scale=q_scales[b][:, cols],
                    rhs=k_codes[b][:, o, :].bitcast(FP4X4),
                    rhs_scale=k_planes[:].bitcast(U8)[:, (o * B + b) * N : (o * B + b + 1) * N],
                    start=(o == 0),
                    stop=(o == PASSES - 1),
                )

        def gather_v_scalar(b, h):
            nc.scalar.activation(v_got[b, h][:], v_pool[b, h][:].indirect(entries(b)), ACT.Copy)

        def gather_v_vector(b, h):
            nc.vector.tensor_copy(v_got[b, h][:], v_pool[b, h][:].indirect(entries(b)))

        def turn_v(b, h, tag=None):
            turned_v.setdefault((b, h), bank("turned_v%d%d" % (b, h), [P, 2, P], tag)[:])
            words = v_got[b, h][:].bitcast(F32)
            for u in range(2):
                nc.tensor.transpose(turned_v[b, h][:, u, :], words[:, u : 2 * P : 2], ident[:])

        def weave_v(b, h, copy):
            copy(
                v_in[b, h][:].bitcast(F32).rearrange("p (e u) -> p e u", u=2),
                turned_v[b, h].rearrange("p u e -> p e u"),
            )

        def quant_v(b, h):
            nc.vector.quantize_mx(v_codes[b, h][:].bitcast(FP8X4), v_scales[b, h][:], v_in[b, h][:])

        def negate_sinks():
            turned = bank("turned_sinks", [P, P], "turned_v00")
            nc.tensor.transpose(turned[:], sink_rows[:], ident[:])
            nc.scalar.activation(neg_all[:, :, N], turned[:, P - B : P], ACT.Copy, scale=-1.0)

        def row_max(b):
            nc.vector.tensor_scalar(
                neg_all[:, b, 0:N].rearrange("p (t s) -> p s t", t=PACK),
                scores[b][:].rearrange("p (s t) -> p s t", t=PACK),
                -1.0,
                neg_all[:, b, N : N + 1],
                ALU.mult,
                ALU.min,
                accum_out=neg_m[b][:],
            )

        def exponentials(b):
            nc.scalar.activation(
                probs[b][:, 0 : N + 1],
                neg_all[:, b, 0 : N + 1],
                ACT.Exp,
                bias=neg_m[b][:],
                scale=-1.0,
                accum_out=total[:, b : b + 1],
            )
            for t in range(PACK):
                nc.tensor.transpose(turned_p[b][:, t, :], probs[b][:, t * P : (t + 1) * P], ident[:])

        def weigh(b):
            nc.vector.tensor_tensor(
                w_bf[b][:].rearrange("p (q t) -> p q t", t=PACK),
                turned_p[b][:].rearrange("p t q -> p q t"),
                vs_col[b][:, 0:PACK].unsqueeze(1).to_broadcast([P, NQ, PACK]),
                ALU.mult,
            )

        def quant_w(b):
            nc.vector.quantize_mx(w_codes[b][:].bitcast(FP8X4), w_scales[b][:], w_bf[b][:])

        def finish(b, h, tag, on_vector=False):
            sums = bank("sums%d%d" % (b, h), [P, P], tag)
            result = placed("result%d%d" % (b, h), [P, P], F32, NEG_M1_AT + (2 * h + b) * KIB // 2)
            nc.tensor.matmul_mx(
                sums[:],
                lhsT=w_codes[b][:].bitcast(FP8X4),
                lhsT_scale=w_scales[b][:],
                rhs=v_codes[b, h][:].bitcast(FP8X4),
                rhs_scale=v_scales[b, h][:],
                start=True,
                stop=True,
            )
            if on_vector:
                nc.vector.tensor_scalar(result[:], sums[:], r_total[:, b : b + 1], None, ALU.mult)
            else:
                nc.scalar.activation(result[:], sums[:], ACT.Copy, scale=r_total[:, b : b + 1])
            nc.sync.dma_start(out[b][:, h * P : (h + 1) * P], result[:])

        nc.sync.dma_start(ks_pool[SCALE_ROWS:P, :], ks_hbm.rearrange("o f t -> f o t"))
        nc.sync.dma_start(offsets[:], offs)
        nc.sync.dma_start(vs_pool[P - 1 : P, :], vs[0:1, :])
        load_kw(0)
        nc.sync.dma_start(sink_rows[P - B : P, :], sink.rearrange("b q o -> b (q o)"))
        nc.sync.dma_start(q_first[:], q_hbm(0))
        load_v(0, 0)
        load_kw(1)
        load_q(1, 0)

        gather_vs()
        negate_sinks()
        gather_ks()
        move_ks()
        load_q(1, 1)
        load_v(1, 0)
        nc.gpsimd.memset(v_mid[:, seg(0)], 0.0)
        nc.sync.dma_start(v_last[:], vT[P : 2 * P, :])
        deal_vs(0)
        deal_vs(1)

        gather_kw(0)
        part_kw(0, 0, PASSES)
        group_q(0, 0)
        group_q(0, 1)
        quant_q(0, 0, PASSES)
        gather_v_scalar(0, 0)
        turn_v(0, 0)
        score(0, 0, PASSES)
        gather_kw(1)
        group_q(1, 0)
        group_q(1, 1)
        weave_v(0, 0, nc.scalar.copy)
        quant_q(1, 0, 1)
        part_kw(1, 0, 1)
        score(1, 0, 1)
        part_kw(1, 1, 2)
        quant_q(1, 1, 2)
        score(1, 1, 2)
        row_max(0)
        quant_v(0, 0)
        gather_v_scalar(1, 0)
        turn_v(1, 0)
        exponentials(0)
        row_max(1)
        exponentials(1)
        gather_v_vector(0, 1)
        turn_v(0, 1)
        weigh(0)
        gather_v_scalar(1, 1)
        turn_v(1, 1)
        weave_v(1, 0, nc.scalar.copy)
        weigh(1)
        quant_w(0)
        quant_v(1, 0)
        nc.vector.reciprocal(r_total[:], total[:])
        weave_v(0, 1, nc.scalar.copy)
        weave_v(1, 1, nc.scalar.copy)
        quant_w(1)
        quant_v(0, 1)
        quant_v(1, 1)
        finish(0, 0, "scores0")
        finish(1, 0, "turned_v01")
        finish(0, 1, "turned_v00")
        finish(1, 1, "turned_p0", True)
